import numpy as np, ml_dtypes
CORES = [40,64,80,88,96,104,120,144]
N = 8
BF = ml_dtypes.bfloat16
def gentries(a):
    return np.ascontiguousarray(a.reshape(8, 16, -1).transpose(0, 2, 1)).reshape(8, -1)
def gtable(e):
    e = np.asarray(e); return np.ascontiguousarray(e.reshape(8, -1, 16).transpose(0, 2, 1)).reshape(128, -1).astype(np.int32)
V, U, S, C, RO = 384, 384, 6, 1, 4
X, M, NONE = V + U, N * V, N * V + U
def cut(p, c):
    return np.where(np.arange(S) < c[..., None], p, NONE)
def around(rng, o, j):
    j = np.minimum(j, o); m = np.maximum(S - 1 - j, 1)
    below = rng.integers(1, np.maximum(o // np.maximum(j, 1), 1) + 1); above = rng.integers(1, np.maximum((M - 1 - o) // m, 1) + 1)
    d = np.arange(S) - j[..., None]; x = o[..., None] + np.where(d < 0, below[..., None], above[..., None]) * d
    return np.where(x < M, x, NONE)
def hold(rng, o, lo, hi):
    n = hi - lo; d = np.sort(rng.integers(0, n - S + 1, o.shape + (S - 1,)), axis=-1) + np.arange(1, S)
    d = np.concatenate([np.zeros(o.shape + (1,), np.int64), d], axis=-1)
    return np.sort(lo + (o[..., None] - lo + d) % n, axis=-1)
def numbers_of():
    return np.arange(M).reshape(N, 1, V) + np.zeros((1, 8, 1), np.int64)
def parts(rng):
    size = rng.random((N, 8, X, 1)); low = rng.random((N, 8, X, 1)) * (1 - size)
    x = np.minimum((low + size * rng.random((N, 8, X, S))) * (M - S + 1), M - S).astype(np.int64)
    p = cut(np.sort(x, axis=-1) + np.arange(S), rng.integers(0, S + 1, (N, 8, X)))
    return p, rng.integers(0, NONE + 1, (N, 8, X)), rng.integers(0, NONE + 1, (N, 8, C, X)), rng.integers(0, NONE + 1, (N, 8, V)), rng.integers(0, NONE + 1, (N, 8, V))
def name(rng, p, xs):
    xs = np.array(xs)
    for r in range(N):
        for g in range(8):
            tab = np.concatenate([p[:, g, :V].reshape(M, S), p[r, g, V:]])
            place, slot = np.nonzero(tab // V == r); k = rng.permutation(len(place))
            new = np.array(xs[r, g]); new[tab[place[k], slot[k]] - r * V] = place[k]
            xs[r, g] = np.where(rng.random(V) < 0.65, new, xs[r, g])
    return xs
def pack(p, ld, cp, xs, ys):
    a = np.full((N, 8, 16, X), NONE, np.int32); a[:, :, :S] = p.transpose(0, 1, 3, 2)
    return {"pts": a.reshape(N, 128, X), "ld": np.stack([gtable(e) for e in ld]), "cp": np.stack([gtable(e.reshape(8, -1)) for e in cp]),
            "xs": np.stack([gtable(e) for e in xs]), "ys": np.stack([gtable(e) for e in ys])}
def setup_inputs(rng):
    p, ld, cp, xs, ys = parts(rng)
    return pack(p, ld, cp, name(rng, p, xs), ys)
def setup_inputs_alike(rng):
    p, ld, cp, xs, ys = parts(rng)
    own = np.stack([np.concatenate([r * V + np.arange(V), M + np.arange(U)]) for r in range(N)])
    p[:, 0, :V] = around(rng, numbers_of(), rng.integers(0, S, (N, 8, V)))[:, 0]
    ld[:, 0] = own; cp[:, 0] = own[:, None]; xs[:, 0] = own[:, :V]
    ld[:, 1] = rng.integers(0, M, (N, 1)); cp[:, 1] = rng.integers(0, M, (N, 1, 1)); xs[:, 1] = rng.integers(0, M, (N, 1)); ys[:, 1] = rng.integers(0, M, (N, 1))
    p[:, 2, :V] = around(rng, np.array([M // 3]), np.array([S // 2]))[0]
    ld[:, 3] = NONE; cp[:, 3] = NONE
    ld[:, 4] = rng.integers(M, M + U, (N, X))
    ld[:, 5] = rng.integers(0, V, (N, X)) + V * np.arange(N)[:, None]
    ld[:, 6] = rng.integers(0, V, (N, X)) + V * ((np.arange(N) + 1) % N)[:, None]
    cp[:, 7] = ld[:, 7][:, None]
    keep = name(rng, p, xs); xs[:, 2:] = keep[:, 2:]
    return pack(p, ld, cp, xs, ys)
def setup_inputs_chain(rng):
    p, ld, cp, xs, ys = parts(rng); p[:] = NONE; ld[:] = NONE; cp[:] = NONE; xs[:] = NONE
    h = M // 4; kind = rng.permutation(8)
    for g in kind[:4]:
        o = rng.permutation(M); hub, shelf, leaf, rest = o[:h], o[h:2 * h], np.sort(o[2 * h:3 * h]), o[3 * h:]
        p[leaf // V, g, leaf % V, 0] = np.sort(rng.permutation(M)[:h])
        pick = np.sort(rng.integers(0, h - S + 1, (h, S)), axis=1) + np.arange(S)
        p[shelf // V, g, shelf % V] = leaf[pick]
        p[hub // V, g, hub % V, 0] = leaf[pick[:, 0]]; cp[hub // V, g, C - 1, hub % V] = shelf
        ld[:, g, V:] = hub[rng.integers(0, h, (N, U))]; ld[rest // V, g, rest % V] = hub[rng.integers(0, h, len(rest))]
    for g in kind[4:6]:
        e = 2 * h; o = rng.permutation(e); hub, shelf = o[:h], o[h:]
        leaf = e + np.sort(rng.permutation(e - 1)[:h]); held = np.sort(rng.permutation(e)[:h])
        pick = np.sort(rng.integers(0, h - 2 * S + 2, (h, 2 * S - 1)), axis=1) + np.arange(2 * S - 1)
        i = rng.integers(0, h, (N, X)); ld[:, g] = hub[i]
        p[:, g, :, :S - 1] = held[pick[i][:, :, :S - 1]]
        p[leaf // V, g, leaf % V] = NONE; p[leaf // V, g, leaf % V, 0] = held; p[leaf // V, g, leaf % V, 1] = M - 1
        p[hub // V, g, hub % V] = leaf[pick[:, :S]]; cp[hub // V, g, C - 1, hub % V] = shelf
        p[shelf // V, g, shelf % V] = np.concatenate([leaf[pick[:, S:]], np.full((h, 1), M - 1)], axis=1)
    for g in kind[6:]:
        b = int(rng.integers(0, N)); b1 = (b + 1) % N; b2 = (b + 2) % N; half = U // 2
        p[b, g, V:] = np.sort(rng.integers(0, M - S + 1, (U, S)), axis=1) + np.arange(S)
        cp[b, g, C - 1, :V] = M + rng.integers(0, U, V)
        cp[b1, g, C - 1] = b * V + rng.integers(0, V, X)
        cp[b2, g, C - 1] = b1 * V + rng.integers(0, V, X)
        for d in range(3, N):
            q = (b + d) % N
            p[q, g, V:V + half, 0] = rng.integers(0, M, half)
            cp[q, g, C - 1, :V] = M + rng.integers(0, half, V)
            cp[q, g, C - 1, V + half:] = b1 * V + rng.integers(0, V, U - half)
    return pack(p, ld, cp, xs, ys)
def setup_inputs_ends(rng):
    p, ld, cp, xs, ys = parts(rng)
    e = np.full((8, S), NONE); e[1, 0] = 0; e[2, 0] = M - 1; e[3, :2] = (0, M - 1); e[4] = np.arange(S); e[5] = M - S + np.arange(S); e[6, :2] = (V - 1, V); e[7, 0] = 1
    p = np.where((rng.random((N, 8, X)) < 0.7)[..., None], e[rng.integers(0, 8, (N, 8, X))], p)
    ends = np.array([0, V - 1, V, M - 1, M, NONE - 1, NONE]); xs = name(rng, p, xs)
    ld, cp, ys = [np.where(rng.random(a.shape) < 0.4, ends[rng.integers(0, 7, a.shape)], a) for a in (ld, cp, ys)]
    xs = np.where(rng.random(xs.shape) < 0.3, ends[rng.integers(0, 7, xs.shape)], xs)
    return pack(p, ld, cp, xs, ys)
def full_stores(rng, g, p, ld, cp, xs, ys):
    b = N - 1; low = M - V; to = rng.permutation(V)
    hr = (np.arange(b)[:, None] + rng.integers(1, b)) % b
    ld[:, g, :2 * V] = NONE; cp[:, g, :, :2 * V] = NONE
    p[hr, g, to] = hold(rng, np.arange(low).reshape(b, V), 0, low); xs[:b, g] = hr * V + to
    p[b, g, :V] = hold(rng, low + np.arange(V), low, M); ys[:b, g] = low + rng.integers(0, V, (b, V))
    xs[b, g] = rng.integers(0, low, V); ys[b, g] = rng.integers(0, low, V)
    nx = np.append((np.arange(b) + 1) % b, 0)
    p[:, g, V:2 * V] = p[nx, g, :V]; cp[:, g, C - 1, V:2 * V] = nx[:, None] * V + np.arange(V)
def late_names(rng, g, p, ld, cp, xs, ys):
    H = V // 3; Q = (V - 2 * H) // 2; ra = np.arange(N)[:, None]; k = np.arange(H)
    pm = np.concatenate([1 + np.argsort(rng.random((N, V - 1)), axis=1), np.zeros((N, 1), np.int64)], axis=1)
    namer, quiet, source = pm[:, :H], pm[:, 2 * H:2 * H + Q], pm[:, 2 * H + Q:]
    ld[:, g, :V + H] = NONE; cp[:, g, :, :V + H] = NONE; ld[:, g, X - 1] = NONE; cp[:, g, :, X - 1] = NONE; xs[:, g] = NONE
    far = (ra + np.where(k // (RO - 1) % 2 == 1, rng.integers(1, N, H), 0)) % N
    feed = around(rng, ra * V + namer, k % (RO - 1)); hv = pm[far, H + k]; low = feed[..., 0]
    p[far, g, V + k] = feed; cp[far, g, C - 1, hv] = M + k + np.zeros((N, 1), np.int64)
    p[far, g, hv] = NONE; p[far, g, hv, 0] = np.where((low > 0) & (rng.random(low.shape) < 0.5), low - 1, NONE)
    xs[ra, g, namer] = far * V + hv
    p[ra, g, source] = hold(rng, ra * V + source, 0, M)
    p[0, g, 0] = np.sort(rng.permutation((ra * V + quiet).reshape(-1))[:S])
    p[:, g, X - 1] = np.sort(ra * V + quiet[:, :S], axis=1)
    ask = np.concatenate([namer, quiet], axis=1); away = (ra + rng.integers(1, N, ask.shape)) % N
    sv = source[away, rng.integers(0, source.shape[1], ask.shape)]
    ys[ra, g, ask] = away * V + sv
    p[ra, g, ask] = cut(p[away, g, sv], rng.integers(0, S, ask.shape))
def setup_inputs_stores(rng):
    p, ld, cp, xs, ys = parts(rng); o = numbers_of(); sh = (N, 8, V)
    case = rng.integers(0, 4, sh); mid = np.where(case == 2, np.where(o + 1 < M, o + 1, 0), o)
    x = around(rng, mid, np.where(case == 1, S - 1, 0))
    p[:, :, V:2 * V] = np.where((case == 3)[..., None], NONE, x)
    ld[:, :, V:2 * V] = np.where(case == 3, NONE, ld[:, :, V:2 * V]); cp[:, :, :, V:2 * V] = NONE
    cp[:, :, 0, V:2 * V] = np.where(case == 3, (o + V) % M, NONE)
    j = rng.integers(0, RO, sh); k = around(rng, o, j)
    k = cut(k, np.where(rng.random(sh) < 0.5, np.minimum(j, o) + 1, S)); p[:, :, :V] = np.roll(k, 1, axis=0)
    quiet = rng.random(sh) < 0.5
    ld[:, :, :V] = np.where(quiet, NONE, ld[:, :, :V]); cp[..., :V] = np.where(quiet[:, :, None], NONE, cp[..., :V])
    xs = M + np.arange(V) + np.zeros(sh, np.int64)
    kind = [int(g) for g in rng.permutation(8)]
    for g in kind[:2]: full_stores(rng, g, p, ld, cp, xs, ys)
    for g in kind[2:4]: late_names(rng, g, p, ld, cp, xs, ys)
    return pack(p, ld, cp, xs, ys)
def setup_inputs_spread(rng):
    p, ld, cp, xs, ys = parts(rng)
    x = np.minimum(np.exp2(np.log2(M - S + 1) * rng.random((N, 8, X, S))).astype(np.int64) - 1, M - S)
    x = np.sort(x, axis=-1) + np.arange(S); x = np.where(rng.random((N, 8, X, 1)) < 0.35, (M - 1 - x)[..., ::-1], x)
    p = cut(x, np.minimum((rng.random((N, 8, X)) ** 2 * (S + 1)).astype(np.int64), S))
    ld, cp, xs, ys = [np.minimum((rng.random(a.shape) ** 3 * (NONE + 1)).astype(np.int64), NONE) for a in (ld, cp, xs, ys)]
    return pack(p, ld, cp, name(rng, p, xs), ys)
def check_inputs(d):
    bad = []
    a = np.asarray(d["pts"]).reshape(N, 8, 16, X); h = a[:, :, :S]
    if not np.all(((h >= 0) & (h < M)) | (h == NONE)): bad.append("range of pts")
    if not np.all((h[:, :, 1:] > h[:, :, :-1]) | (h[:, :, 1:] == NONE)): bad.append("pts rises")
    if not np.all(a[:, :, S:] == NONE): bad.append("later slots of pts")
    for k in ("ld", "cp", "xs", "ys"):
        if np.min(d[k]) < 0 or np.max(d[k]) > NONE: bad.append("range of " + k)
    return bad
def reference(pts, ld, cp, xs, ys):
    p = pts.astype(np.int64).reshape(N, 8, 16, X)
    lds, cps, xss, yss = [np.stack([gentries(a) for a in b]).astype(np.int64) for b in (ld, cp, xs, ys)]
    cps = cps.reshape(N, 8, C, X)
    def take(w, ix):
        return np.take_along_axis(w, ix[:, None, :], 2)
    for t in range(RO):
        objects = np.concatenate([p[q, :, :, :V] for q in range(N)], axis=2); gain = []
        for a in range(N):
            w = np.concatenate([objects, p[a, :, :, V:], np.full((8, 16, 1), NONE)], axis=2)
            top = np.max(np.where(p[a] == NONE, -1, p[a]), axis=1)[:, None, :]
            best = np.full((8, X), NONE)
            edge = take(w, lds[a])
            for i in range(S + t):
                s = take(w, edge[:, i]); best = np.minimum(best, np.min(np.where(s > top, s, NONE), axis=1))
            for c in range(C):
                s = take(w, cps[a, :, c]); best = np.minimum(best, np.min(np.where(s > top, s, NONE), axis=1))
            named = np.any(take(w, xss[a]) == a * V + np.arange(V), axis=1)[:, None, :]
            s = take(w, yss[a]); s = np.min(np.where(named & (s > top[:, :, :V]), s, NONE), axis=1)
            best[:, :V] = np.minimum(best[:, :V], s); gain.append(best)
        p[:, :, S + t] = np.stack(gain)
    return {"yp": p.reshape(N, 128, X).astype(np.float32)}

@@ -1,0 +1,684 @@
+from concourse.bass import DstId, RemoteDMATransfer
+from concourse.mybir import AluOpType, ActivationFunctionType
+
+N, V, RO = 8, 384, 4
+K = 4096.0
+WW = 3457
+RING = 10
+MAGIC = 1.5 * 2.0 ** 35
+EDGE_ROWS = [0, 2, 4, 6, 12, 14]
+TAIL = [9, 11, 14]
+PAR = {"fused": [3, 1, 3, 0, 3, 0, 2, 0], "edge_act": [0] * 8, "ecopy": [0, 1, 3, 5], "s2v": 0, "gat": 1.56, "cyc": 0.00104,
+       "pe": 0.00052, "dma": 4.0, "slack": 0.12, "mod_act": 1}
+
+f32, f16, bf16, i32, u16 = "float32", "float16", "bfloat16", "int32", "uint16"
+SCRATCH = {
+    "stage": ("dram", [8, 128, 64], i32), "land": ("dram", [8, 128, 64], i32), "hand": ("dram", [2, 128, 64], i32),
+    "handg": ("sbuf", [128, 96], f16), "SG": ("sbuf", [128, 192], f16), "RG": ("sbuf", [128, 192], f16),
+    "OG": ("sbuf", [128, 256], f32),
+    "own": ("sbuf", [128, 768], i32), "ownf": ("sbuf", [128, 768], f32),
+    "nat": ("sbuf", [128, 384], i32), "natf": ("sbuf", [128, 384], f16), "natm": ("sbuf", [128, 384], f16),
+    "L": ("sbuf", [128, 144], i32), "La": ("sbuf", [128, 144], f32), "Lb": ("sbuf", [128, 144], f32),
+    "LI": ("sbuf", [128, 144], u16), "EL": ("sbuf", [128, 432], u16), "EG": ("sbuf", [128, 768], f16),
+    "EF": ("sbuf", [128, 768], f32),
+    "C": ("sbuf", [128, 384], f16), "U": ("sbuf", [128, 384], f16),
+    "W0": ("sbuf", [128, 3464], f32), "W1": ("sbuf", [128, 3464], f32),
+    "KI": ("sbuf", [128, 8], i32), "KJ": ("sbuf", [128, 9], i32), "KF": ("sbuf", [128, 9], f32), "KC": ("sbuf", [128, 32], f32),
+    "J": ("sbuf", [128, 160], f32), "CP": ("sbuf", [128, 128], f32), "CPW": ("sbuf", [128, 128], f32),
+    "CG": ("sbuf", [128, 128], f32), "C16": ("sbuf", [128, 16], f32), "CS": ("sbuf", [128, 128], f32),
+    "CQ": ("sbuf", [128, 128], f32), "CV": ("sbuf", [128, 384], f32), "CO": ("sbuf", [128, 24], f32),
+    "ID": ("sbuf", [128, 128], f16), "P1": ("sbuf", [128, 128], f16), "P2": ("sbuf", [128, 128], f16),
+    "H1": ("sbuf", [128, 128], bf16), "H2": ("sbuf", [128, 128], bf16), "HI": ("sbuf", [128, 128], bf16),
+    "LO": ("sbuf", [128, 128], bf16), "BD": ("sbuf", [128, 128], bf16),
+    "SWH": ("sbuf", [128, 1152], bf16), "SWL": ("sbuf", [128, 1152], bf16),
+    "M16": ("sbuf", [128, 16], f32), "MK": ("sbuf", [128, 16], f32), "MQ": ("sbuf", [128, 16], f32), "GM": ("sbuf", [128, 8], f32),
+    "WT": ("sbuf", [128, 8], f32), "SS": ("sbuf", [128, 32], f32), "TS": ("sbuf", [128, 24], f32), "NS": ("sbuf", [128, 8], bf16),
+    "WF": ("sbuf", [128, 160], f32), "WH": ("sbuf", [128, 160], bf16), "WD": ("sbuf", [128, 960], bf16),
+    "SB": ("sbuf", [128, 768], bf16), "SM": ("sbuf", [128, 2304], bf16), "SH3": ("sbuf", [128, 128], bf16), "M3": ("sbuf", [128, 4], f32),
+    "SO0": ("sbuf", [128, 128], f16), "SY0": ("sbuf", [128, 256], f16),
+    "OK": ("sbuf", [128, 384], f32), "OC": ("sbuf", [128, 24], f32), "R0": ("sbuf", [128, 384], bf16),
+    "RS": ("sbuf", [128, 8 * 264], bf16), "SC": ("sbuf", [128, 2 * 264], f32), "MA": ("sbuf", [128, 528], f32),
+    "MB": ("sbuf", [128, 528], f32), "MC": ("sbuf", [128, 528], f32),
+    "TN": ("sbuf", [128, 192], f32), "SA": ("sbuf", [128, 192], f32), "BS": ("sbuf", [128, 192], f32),
+    "GA": ("sbuf", [128, 144], f32), "GB": ("sbuf", [128, 144], f32), "TC": ("sbuf", [128, 576], f16),
+    "UT": ("sbuf", [128, 6 * 128], f16), "S1": ("sbuf", [128, 3 * 384], f32), "S2": ("sbuf", [128, 3 * 384], f32),
+    "YS": ("sbuf", [128, 768], f32), "G": ("sbuf", [128, RING * 384], f32), "XG": ("sbuf", [128, 384], f32),
+    "XB": ("sbuf", [128, 384], bf16), "NE": ("sbuf", [128, 24], f32),
+}
+for _b in range(8):
+    SCRATCH["B%d" % _b] = ("psum", [128, 512], f32)
+NDMA = 56
+SEMAPHORES = ["cv", "ca", "cp", "cg", "sent", "arr", "arrg", "h0", "h1"] + ["d%d" % _i for _i in range(NDMA)]
+
+A = AluOpType
+IDENT = ActivationFunctionType.Identity
+
+
+def routes(T, topo, core):
+    cores = list(T.cores)
+    direct = [q for q in range(N) if cores[q] != core and topo.may_write(core, cores[q])]
+    far = [q for q in range(N) if cores[q] != core and q not in direct]
+    able = [c for c in topo.cores_of(core) if c not in cores and all(topo.may_write(c, cores[q]) for q in far)]
+    able.sort(key=lambda c: topo.die(c) == topo.die(core))
+    return direct, [(able[j], far[2 * j:2 * j + 2]) for j in range((len(far) + 1) // 2)]
+
+
+def bits(es):
+    return sum(1 << e for e in es)
+
+
+def dst(topo, d, s):
+    rid, pid = topo.addr(d, s)
+    return DstId(rid=rid, pnc=pid)
+
+
+def span_start(qs):
+    return min(qs[0], N - 4)
+
+
+def helper_program(g, core, T, topo, rank, qs):
+    cores = list(T.cores)
+    es = topo.engines(core, cores[qs[0]])
+    n = len(es) // 2
+    g.wait_ge(T.sem.h0, 2 * len(qs))
+    g.remote_dma_fused([RemoteDMATransfer(dst_ids=[dst(topo, cores[q], core)], dma_engine_mask=bits(es[n * j:n * j + n]),
+                                          remote_sem=T.sem.arr, src=T.hand[j], dst=T.land[rank]) for j, q in enumerate(qs)],
+                       local_sem=T.sem.sent)
+    g.wait_ge(T.sem.h1, 4)
+    s = span_start(qs)
+    g.remote_dma_fused([RemoteDMATransfer(dst_ids=[dst(topo, cores[q], core)], dma_engine_mask=bits(es[n * j:n * j + n]),
+                                          remote_sem=T.sem.arrg, src=T.handg[:, 24 * (q - s):24 * (q - s) + 24],
+                                          dst=T.RG[:, 24 * rank:24 * rank + 24]) for j, q in enumerate(qs)],
+                       local_sem=T.sem.sent)
+    g.wait_ge(T.sem.sent, 2 * n * len(qs))
+
+
+def direct_masks(topo, core, cores, direct):
+    es = topo.engines(core, cores[direct[0]])
+    cut = [es[0:4], es[4:6], es[6:8]]
+    return [cut[j] for j in range(len(direct))]
+
+
+def arrivals(T, topo, rank):
+    cores = list(T.cores)
+    total = 0
+    for s in range(N):
+        if s == rank:
+            continue
+        direct, helpers = routes(T, topo, cores[s])
+        if rank in direct:
+            total += len(direct_masks(topo, cores[s], cores, direct)[direct.index(rank)])
+        else:
+            hc = [c for c, qs in helpers if rank in qs][0]
+            total += len(topo.engines(hc, cores[rank])) // 2
+    return total
+
+
+def rank_program(g, core, T, topo):
+    rank = T.rank_of(core)
+    if rank is None:
+        for r, c in enumerate(T.cores):
+            if c in topo.cores_of(core):
+                for hc, qs in routes(T, topo, c)[1]:
+                    if hc == core:
+                        helper_program(g, core, T, topo, r, qs)
+        return
+    cores = list(T.cores)
+    direct, helpers = routes(T, topo, core)
+    ops = []
+    cyc, gat = PAR["cyc"], PAR["gat"]
+
+    def op(q, fn, rd, wr, n=64, kind="c", cost=None):
+        ops.append({"q": q, "fn": fn, "rd": rd, "wr": wr, "kind": kind, "cost": 0.05 + max(n, 64) * cyc if cost is None else cost})
+
+    def raw(q, fn, rd, wr, cost):
+        op(q, fn, rd, wr, kind="raw", cost=cost)
+
+    def dma(q, out, in_, rd, wr, cost=None):
+        op(q, lambda e: e.dma_start(out, in_), rd, wr, kind="dma", cost=PAR["dma"] if cost is None else cost)
+
+    def ts(out, in0, s1, s2, o0, o1, rd, wr, n=64):
+        if o1 is None:
+            op("v", lambda e: e.tensor_scalar(out, in0, s1, None, o0), rd, wr, n)
+        else:
+            op("v", lambda e: e.tensor_scalar(out, in0, s1, s2, o0, o1), rd, wr, n)
+
+    def tt(out, a, b, o, rd, wr, n=64):
+        op("v", lambda e: e.tensor_tensor(out, a, b, o), rd, wr, n)
+
+    def ms(ap, c, wr, n=64):
+        op("v", lambda e: e.memset(ap, c), [], wr, n)
+
+    def mm(out, lhsT, rhs, start, stop, rd, wr, n):
+        op("p", lambda e: e.matmul(out, lhsT, rhs, start, stop), rd, wr, cost=0.01 + n * PAR["pe"])
+
+    def act(out, in_, rd, wr, n=64, bias=0.0, scale=1.0):
+        op("a", lambda e: e.activation(out, in_, IDENT, bias=bias, scale=scale), rd, wr, n)
+
+    def iota(out, pat, base, cm, wr, n, flt=True):
+        if flt:
+            op("g", lambda e: e.iota(out, pat, base, cm, allow_small_or_imprecise_dtypes=True), [], wr, cost=0.13 + 2 * n * cyc)
+        else:
+            op("g", lambda e: e.iota(out, pat, base, cm), [], wr, cost=0.13 + 2 * n * cyc)
+
+    B = [T["B%d" % b] for b in range(8)]
+    W = [T.W0, T.W1]
+    YB, DB, PU, PS1, PS2, PL = [0, 1], [2, 3], 4, 5, 6, 7
+
+    for i in range(6):
+        dma("sa"[i % 2], T.stage[:, 12 * i:12 * i + 12, :], T.pts[i::16, :], [], ["st%d" % i])
+    dma("s", T.stage[:, 72:84, :], T.ld[:, :], [], ["st6"])
+    dma("a", T.stage[:, 84:96, :], T.cp[:, :], [], ["st7"])
+    dma("s", T.stage[:, 96:102, :], T.xs[:, :], [], ["st8"])
+    dma("a", T.stage[:, 102:108, :], T.ys[:, :], [], ["st9"])
+    dma("s", T.stage[:, 108:120, :], T.pts[6::16, :], [], ["st10"])
+    dma("a", T.stage[:, 120:128, :], T.pts[7::16, 0:512], [], ["st11"])
+    st = ["st%d" % i for i in range(12)]
+    iota(T.KI[:, :], [[1, 8]], 0, 1, ["KI"], 8, False)
+    iota(T.C16[:, :], [[1, 16]], 0, 0, ["C16"], 16)
+    iota(T.CP[:, :], [[0, 8], [1, 8], [0, 2]], 0, 0, ["CP"], 128)
+    iota(T.CPW[:, :], [[0, 8], [1, 8], [100, 2]], -100, 0, ["CPW"], 128)
+    iota(T.J[:, :], [[1, 160]], 0, -1, ["J"], 160)
+    iota(T.CG[:, :], [[1, 8], [0, 16]], 0, 0, ["CG"], 128)
+    dm = direct_masks(topo, core, cores, direct)
+    inner = [e for e in topo.engines(core, helpers[0][0]) if e not in topo.engines(core, cores[direct[0]])]
+    tr = []
+    for j, (hc, qs) in enumerate(helpers):
+        for i, q in enumerate(qs):
+            tr.append(RemoteDMATransfer(dst_ids=[dst(topo, hc, core)], dma_engine_mask=bits(inner[4 * j + 2 * i:4 * j + 2 * i + 2]),
+                                        remote_sem=T.sem.h0, src=T.stage[q], dst=T.hand[i]))
+    for j, q in enumerate(direct):
+        tr.append(RemoteDMATransfer(dst_ids=[dst(topo, cores[q], core)], dma_engine_mask=bits(dm[j]),
+                                    remote_sem=T.sem.arr, src=T.stage[q], dst=T.land[rank]))
+    sent = [sum(2 * len(qs) for hc, qs in helpers) + sum(len(m) for m in dm)]
+    raw("g", lambda e: e.remote_dma_fused(tr, local_sem=T.sem.sent), st, ["away"], 1.0)
+    dma("s", T.land[rank], T.stage[rank], st, ["landown"])
+    dma("s", T.own[:, :], T.pts[:, :], [], ["own"])
+    iota(T.CS[:, :], [[1, 2], [12, 8], [2, 8]], 0, -1, ["CS"], 128)
+    iota(T.CQ[:, :], [[100, 2], [0, 8], [1, 8]], 0, 0, ["CQ"], 128)
+    iota(T.CO[:, :], [[128, 3], [384, 8]], -1536, 1, ["CO"], 24)
+    iota(T.CV[:, :], [[1, 384]], 0, 0, ["CV"], 384)
+    narr = arrivals(T, topo, rank)
+    raw("s", lambda e: e.wait_ge(T.sem.arr, narr), ["away"], [], 8.0)
+    dma("s", T.nat[0:96, :], T.land[:, 0:72, :], ["landown"], ["nat"])
+    dma("s", T.L[:, 0:48], T.land[:, 72:84, :], ["landown"], ["L0"])
+    dma("s", T.L[:, 48:96], T.land[:, 84:96, :], ["landown"], ["L1"])
+    dma("s", T.L[:, 96:120], T.land[:, 96:102, :], ["landown"], ["L2"])
+    dma("s", T.L[:, 120:144], T.land[:, 102:108, :], ["landown"], ["L3"])
+
+    for j, (c, s, o) in enumerate([(0, 15, A.bitwise_and), (0, 4, A.arith_shift_right), (0, 3, A.arith_shift_right),
+                                   (0, 7, A.bitwise_and), (0, 3, A.bitwise_and), (0, 0, None),
+                                   (6, 7, A.bitwise_and), (5, 7, A.bitwise_and), (0, 5, A.arith_shift_right)]):
+        if o is None:
+            ts(T.KJ[:, j:j + 1], T.KI[:, 0:1], 31, 2, A.bitwise_and, A.arith_shift_right, ["KI"], ["KJ%d" % j])
+        else:
+            ts(T.KJ[:, j:j + 1], T.KI[:, c:c + 1], s, None, o, None, ["KI"], ["KJ%d" % j])
+    op("v", lambda e: e.tensor_copy(T.KF[:, :], T.KJ[:, :]), ["KJ%d" % j for j in range(9)], ["KF"])
+    kr, kg, k3, ki, kd, kq, key, keyp, k5 = [T.KF[:, j:j + 1] for j in range(9)]
+    col = [T.KC[:, j:j + 1] for j in range(32)]
+    ts(T.M16[:, :], T.C16[:, :], kr, None, A.is_equal, None, ["C16", "KF"], ["M16"])
+    ts(T.MQ[:, :], T.C16[:, :], k3, None, A.is_equal, None, ["C16", "KF"], ["MQ"])
+    ts(T.GM[:, :], T.C16[:, 0:8], kg, None, A.is_equal, None, ["C16", "KF"], ["GM"])
+    ts(T.M3[:, :], T.C16[:, 0:4], k5, None, A.is_equal, None, ["C16", "KF"], ["M3"])
+    ts(col[23], ki, 6.0, K, A.is_lt, A.mult, ["KF"], ["c23"])
+    ts(col[24], ki, 6.0, -1.0, A.is_lt, A.mult, ["KF"], ["c24"])
+    ts(col[9], keyp, 3.0, None, A.is_lt, None, ["KF"], ["c9"])
+    ts(col[0], keyp, 6.0, col[9], A.is_ge, A.max, ["KF", "c9"], ["c0"])
+    ts(col[4], k3, -8.0, None, A.add, None, ["KF"], ["c4"])
+    ts(T.H1[:, :], T.CP[:, :], key, col[23], A.is_equal, A.mult, ["CP", "KF", "c23"], ["H1"], 128)
+    ts(T.H2[:, :], T.CPW[:, :], keyp, col[0], A.is_equal, A.mult, ["CPW", "KF", "c0"], ["H2"], 128)
+    ts(T.LO[:, :], T.CPW[:, :], key, col[24], A.is_equal, A.mult, ["CPW", "KF", "c24"], ["LO"], 128)
+    tt(T.HI[:, :], T.H1[:, :], T.H2[:, :], A.add, ["H1", "H2"], ["HI"], 256)
+    ts(T.BD[:, :], T.CG[:, :], col[4], None, A.is_equal, None, ["CG", "c4"], ["BD"], 128)
+    ts(col[2], kd, 0.0, None, A.is_equal, None, ["KF"], ["c2"])
+    ts(col[3], kd, 0.0, K, A.is_equal, A.mult, ["KF"], ["c3"])
+    ts(col[19], kd, 1.0, None, A.is_equal, None, ["KF"], ["c19"])
+    tt(col[1], col[3], col[19], A.subtract, ["c3", "c19"], ["c1"])
+    ts(col[5], ki, 7.0, K, A.is_equal, A.mult, ["KF"], ["c5"])
+    ts(col[6], ki, 6.0, K, A.is_equal, A.mult, ["KF"], ["c6"])
+    ts(col[7], ki, 7.0, None, A.is_equal, None, ["KF"], ["c7"])
+    tt(col[8], col[6], col[7], A.subtract, ["c6", "c7"], ["c8"])
+    act(col[10], T.M16[:, 7:8], ["M16"], ["c10"], bias=-K, scale=1537.0)
+    act(col[11], kg, ["KF"], ["c11"], bias=-1536.0 * K, scale=384.0 * K)
+    for t in range(3):
+        act(col[25 + t], T.M16[:, TAIL[t]:TAIL[t] + 1], ["M16"], ["c%d" % (25 + t)], bias=-K, scale=1537.0)
+    ts(col[20], kd, 3.0, col[19], A.is_equal, A.add, ["KF", "c19"], ["c20"])
+    act(col[12], col[20], ["c20"], ["c12"], bias=1.0, scale=-2.0)
+    ts(col[13], kr, 12.0, None, A.is_ge, None, ["KF"], ["c13"])
+    ts(col[15], T.M16[:, 14:15], -2.0, col[12], A.mult, A.add, ["M16", "c12"], ["c15"])
+    act(T.WT[:, 0:4], T.C16[:, 0:4], ["C16"], ["WT0"], bias=8.0, scale=2.0)
+    ts(T.WT[:, 4:8], T.WT[:, 0:4], kr, col[13], A.is_gt, A.max, ["WT0", "KF", "c13"], ["WT1"])
+    for t in range(3):
+        act(col[16 + t], T.WT[:, 4 + t:5 + t], ["WT1", "c12"], ["c%d" % (16 + t)], scale=col[12])
+    for q in range(8):
+        act(T.SWL[:, 128 * q:128 * q + 128], T.LO[:, :], ["LO", "MQ"], ["SWL%d" % q], 128, scale=T.MQ[:, q:q + 1])
+        act(T.SWH[:, 128 * q:128 * q + 128], T.HI[:, :], ["HI", "MQ"], ["SWH%d" % q], 128, scale=T.MQ[:, q:q + 1])
+    tt(T.SWL[:, 1024:1152], T.LO[:, :], T.BD[:, :], A.mult, ["LO", "BD"], ["SWL8"], 256)
+    tt(T.SWH[:, 1024:1152], T.HI[:, :], T.BD[:, :], A.mult, ["HI", "BD"], ["SWH8"], 256)
+    ts(T.ID[:, :], T.J[:, 0:128], 0.0, None, A.is_equal, None, ["J"], ["ID"], 128)
+    ts(T.WF[:, :], T.J[:, :], 15.0, None, A.is_equal, None, ["J"], ["WF"], 160)
+    act(T.WH[:, :], T.WF[:, :], ["WF"], ["WH"], 160)
+    act(T.MK[:, :], T.M16[:, :], ["M16"], ["MK"], scale=1.0 / K)
+    for j, r in enumerate(EDGE_ROWS):
+        act(T.WD[:, 160 * j:160 * j + 160], T.WF[:, :], ["WF", "M16"], ["WD%d" % j], 160, scale=T.M16[:, r:r + 1])
+    ms(T.R0[:, :], 4000.0, ["R0"], 192)
+    ms(T.R0[:, 0::8], -1536.0, ["R0"])
+    ts(T.CS[:, 6::8], T.CS[:, 6::8], -2.0, None, A.add, None, ["CS"], ["CS"])
+    ts(T.CS[:, 7::8], T.CS[:, 7::8], -4.0, None, A.add, None, ["CS"], ["CS"])
+    ts(T.P1[:, :], T.CS[:, :], 0.0, None, A.is_equal, None, ["CS"], ["P1"], 128)
+    ts(T.P2[:, :], T.CS[:, :], 0.0, -3584.0, A.is_equal, A.mult, ["CS"], ["P2"], 128)
+    ts(T.SY0[:, 0:128], T.CG[:, :], k3, col[5], A.is_equal, A.mult, ["CG", "KF", "c5"], ["SY00"], 128)
+    ts(T.SY0[:, 128:256], T.CG[:, :], col[4], col[5], A.is_equal, A.mult, ["CG", "c4", "c5"], ["SY01"], 128)
+    ts(T.SO0[:, :], T.CQ[:, :], k3, col[8], A.is_equal, A.mult, ["CQ", "KF", "c8"], ["SO0"], 128)
+    for t in range(4):
+        c = 16 + t if t < 3 else 15
+        act(T.SS[:, 8 * t:8 * t + 8], T.GM[:, :], ["GM", "c%d" % c], ["SS%d" % t], scale=col[c])
+    for t in range(1, 4):
+        act(T.TS[:, 8 * t - 8:8 * t], T.GM[:, :], ["GM", "M16"], ["TS%d" % t], scale=T.M16[:, 6 + 2 * t:7 + 2 * t])
+    ts(T.NS[:, :], T.SS[:, 0:8], 0.0, None, A.max, None, ["SS0"], ["NS"])
+    ms(T.W0[:, 384:385], -1537.0 * K, ["W0o"])
+    ms(T.RS[:, :], 1.0, ["RS"], 1056)
+    ts(T.SB[:, 0:128], T.CQ[:, :], kq, col[1], A.is_equal, A.mult, ["CQ", "KF", "c1"], ["SB0"], 128)
+    ts(T.SB[:, 128:192], T.CQ[:, 0:64], kq, col[2], A.is_equal, A.mult, ["CQ", "KF", "c2"], ["+SB1"])
+    ts(T.SB[:, 192:256], T.CQ[:, 0:64], kq, col[3], A.is_equal, A.mult, ["CQ", "KF", "c3"], ["+SB1"])
+    ts(T.SB[:, 256:384], T.CG[:, :], kq, col[3], A.is_equal, A.mult, ["CG", "KF", "c3"], ["SB2"], 128)
+    ms(T.SB[:, 384:768], 0.0, ["SB3", "SB4", "SB5"], 192)
+    for t in range(3):
+        for r, c in zip([7 + 2 * t, 8 + 2 * t, TAIL[t]], [2, 3, 1]):
+            ts(T.SB[:, 384 + 128 * t + r:512 + 128 * t:16], T.C16[:, 0:8], kq, col[c], A.is_equal, A.mult, ["C16", "KF", "c%d" % c],
+               ["+SB%d" % (3 + t)])
+    for j in range(6):
+        for b in range(3):
+            act(T.SM[:, 384 * j + 128 * b:384 * j + 128 * b + 128], T.SB[:, 128 * j:128 * j + 128], ["SB%d" % j, "M3"],
+                ["SM%d%d" % (j, b)], 128, scale=T.M3[:, b:b + 1])
+    act(T.SH3[:, :], T.SWH[:, 1024:1152], ["SWH8"], ["SH3"], 128)
+    ms(T.SH3[:, 12::16], 0.0, ["+SH3"])
+    ms(T.SH3[:, 14::16], 0.0, ["+SH3"])
+    act(T.OK[:, :], T.CV[:, :], ["CV", "c11"], ["OK"], 384, bias=col[11], scale=K)
+    act(T.OC[:, :], T.CO[:, :], ["CO"], ["OC"], scale=K)
+    for j in range(2):
+        ts(T.TC[:, 288 * j:288 * j + 288], T.R0[:, 0:288], 0.0, None, A.mult, None, ["R0"], ["TCz%d" % j], 144)
+
+    def nsrc(t, h):
+        return 8 + t - h
+
+    def reset(t, h):
+        o = 264 * (2 * t + h)
+        return T.RS[:, o:o + 24 * nsrc(t, h)]
+
+    def named(t):
+        o = 264 * 2 * t
+        return T.RS[:, o + 1:o + 24 * nsrc(t, 0):nsrc(t, 0)]
+
+    for t in range(4):
+        for h in range(2):
+            o = 264 * (2 * t + h)
+            op("v", lambda e, a=T.RS[:, o:o + 24 * nsrc(t, h):nsrc(t, h)]: e.memset(a, 0.0), ["RS"], ["RS%d%d" % (t, h)])
+    op("v", lambda e: e.tensor_copy(T.ownf[:, :], T.own[:, :]), ["own"], ["ownf"], 768)
+
+    ts(T.natf[0:96, :], T.nat[0:96, :], -1535.0, None, A.add, None, ["nat"], ["natf"], 384)
+    ts(T.natm[0:96, :], T.nat[0:96, :], 3071.5, None, A.is_gt, None, ["nat"], ["natm"], 384)
+    for b in range(3):
+        mm(B[PU][:, 128 * b:128 * b + 128], T.natf[0:96, 128 * b:128 * b + 128], T.P1[0:96, :], True, False, ["natf", "P1"], ["#4"], 128)
+        mm(B[PU][:, 128 * b:128 * b + 128], T.natm[0:96, 128 * b:128 * b + 128], T.P2[0:96, :], False, True, ["natm", "P2"], ["#4"], 128)
+    op("v", lambda e: e.tensor_tensor_scan(T.C[:, :], T.R0[:, :], B[PU][:, 0:384], -1536.0, A.min, A.max), ["R0", "#4"], ["C"], 384)
+    for b in range(3):
+        mm(B[PL][:, 128 * b:128 * b + 128], T.C[:, 128 * b:128 * b + 128], T.ID[:, :], True, True, ["C", "ID"], ["#7"], 128)
+    op("v", lambda e: e.tensor_copy(T.U[:, :], B[PL][:, 0:384]), ["#7"], ["U"], 384)
+    ts(T.La[:, :], T.L[:, :], 3071.5, 3457.0, A.is_lt, A.mult, ["L0", "L1", "L2", "L3"], ["La"], 144)
+    tt(T.Lb[:, :], T.L[:, :], T.La[:, :], A.add, ["La"], ["Lb"], 288)
+    ts(T.LI[:, :], T.Lb[:, :], -3072.0, None, A.add, None, ["Lb"], ["LI"], 144)
+    banks = [2, 3, 5, 6, 4, 0, 1]
+    for q in range(9):
+        b = banks[q % 7]
+        mm(B[b][:, 0:384], T.SWH[:, 128 * q:128 * q + 128], T.U[:, :], True, False, ["U", "SWH%d" % q], ["#%d" % b], 384)
+        mm(B[b][:, 0:384], T.SWL[:, 128 * q:128 * q + 128], T.U[:, :], False, True, ["U", "SWL%d" % q], ["#%d" % b], 384)
+        c0 = 385 + 384 * q if q < 8 else 0
+        if q % 2 == 0:
+            act(T.W0[:, c0:c0 + 384], B[b][:, 0:384], ["#%d" % b, "c10"], ["W0p%d" % q], 384, bias=col[10])
+        else:
+            ts(T.W0[:, c0:c0 + 384], B[b][:, 0:384], col[10], None, A.add, None, ["#%d" % b, "c10"], ["W0p%d" % q], 384)
+    first = ["W0p%d" % q for q in range(9)]
+    for h in range(2):
+        mm(B[YB[h]][:, 0:384], T.SY0[:, 128 * h:128 * h + 128], T.U[:, :], True, True, ["U", "SY0%d" % h], ["#%d" % YB[h]], 384)
+    dma("s", T.W1[:, 384:WW], T.W0[:, 384:WW], first[:8] + ["W0o"], ["W1o"], 8.0)
+
+    def wkeys(t, full):
+        w = "W%d" % (t % 2)
+        return (first if t == 0 else []) + [w + "o"] + ([w + "t"] if full else [])
+
+    def window(t, full):
+        return W[t % 2][:, 0:WW] if full else W[t % 2][:, 384:WW]
+
+    def ycopy(t, h):
+        if PAR["fused"][2 * t + h]:
+            act(T.YS[:, 384 * h:384 * h + 384], B[YB[h]][:, 0:384], ["#%d" % YB[h]], ["YS%d" % h], 384)
+
+    def edges(t, h):
+        if t == 0:
+            ts(T.EG[:, :], window(0, True).indirect(T.LI[:, 0:48]), 1.0 / K, None, A.mult, None, wkeys(0, True) + ["LI"],
+               ["EG0", "EG1"], 768 * gat)
+            for j in range(6):
+                for x in range(16):
+                    o = 160 * j + 15 + EDGE_ROWS[j] - x
+                    mm(B[PL][:, 48 * j:48 * j + 48], T.WD[:, o:o + 128], T.EG[:, x::16], x == 0, x == 15, ["EG0", "EG1", "WD%d" % j], ["#7"], 64)
+                if j in PAR["ecopy"]:
+                    j0 = max([-1] + [i for i in PAR["ecopy"] if i < j]) + 1
+                    ts(T.EL[:, 48 * j0:48 * j + 48], B[PL][:, 48 * j0:48 * j + 48], 1537.0, None, A.add, None, ["#7"],
+                       ["EL%d%d" % (i, hh) for i in range(j0, j + 1) for hh in range(2)], 48 * (j + 1 - j0))
+            return
+        src, rd = window(t, True).indirect(T.LI[:, 24 * h:24 * h + 24]), wkeys(t, True) + ["LI", "MK"]
+        mk = T.MK[:, 6 + 2 * t:7 + 2 * t]
+        by_act = PAR["edge_act"][2 * t + h]
+        if by_act:
+            act(T.EF[:, 384 * h:384 * h + 384], src, rd, ["EG%d" % h], 384 * gat, scale=mk)
+        else:
+            ts(T.EG[:, 384 * h:384 * h + 384], src, mk, None, A.mult, None, rd, ["EG%d" % h], 384 * gat)
+        for x in range(16):
+            o = 15 + 6 + 2 * t - x
+            l, r, k, n = (T.WF, T.EF, "WF", 256) if by_act else (T.WH, T.EG, "WH", 64)
+            mm(B[PL][:, 0:24], l[:, o:o + 128], r[:, 384 * h + x:384 * h + 384:16], x == 0, x == 15, ["EG%d" % h, k], ["#7"], n)
+        c = 48 * (5 + t) + 24 * h
+        ts(T.EL[:, c:c + 24], B[PL][:, 0:24], 1537.0, None, A.add, None, ["#7"], ["EL%d%d" % (5 + t, h)])
+
+    ring = [0]
+
+    def source(t, h, name, fused):
+        E = nsrc(t, h)
+        if name == "ys":
+            e, off, full, k = 0, T.LI[:, 120:144], True, "LI"
+        elif name == "cp":
+            e, off, full, k = 1 - h, T.LI[:, 48 + 24 * h:72 + 24 * h], True, "LI"
+        else:
+            e, off, full, k = 2 - h + name, T.EL[:, 48 * name + 24 * h:48 * name + 24 * h + 24], False, "EL%d%d" % (name, h)
+        s = ring[0] % RING
+        ring[0] += 1
+        gs = T.G[:, 384 * s:384 * s + 384]
+        gk = "G%d" % s
+        src = window(t, full).indirect(off)
+        if fused:
+            tt(gs, src, T.YS[:, 384 * h:384 * h + 384], A.max, wkeys(t, full) + [k, "YS%d" % h], [gk], 384 * gat)
+        else:
+            act(gs, src, wkeys(t, full) + [k], [gk], 384 * gat)
+            tt(gs, gs, B[YB[h]][:, 0:384], A.max, [gk, "#%d" % YB[h]], [gk], 384)
+        for b in range(3):
+            o = 8 * b * E + e
+            mm(B[DB[h]][:, o:o + 7 * E + 1:E], T.G[:, 384 * s + 128 * b:384 * s + 128 * b + 128], T.SS[:, 8 * t:8 * t + 8],
+               True, True, [gk, "SS%d" % t], ["#%d" % DB[h]], 256)
+
+    def stores(t):
+        src = window(t, True).indirect(T.LI[:, 96:120])
+        if t == 0:
+            tt(T.XB[:, :], src, T.OK[:, :], A.is_equal, wkeys(t, True) + ["LI", "OK"], ["XB"], 384 * gat)
+            for b in range(3):
+                mm(B[PS2][:, 8 * b:8 * b + 8], T.XB[:, 128 * b:128 * b + 128], T.NS[:, :], True, True, ["XB", "NS"], ["#6"], 64)
+            ts(named(0), B[PS2][:, 0:24], 1.0, None, A.min, None, ["#6", "RS"], ["nm0"])
+        else:
+            act(T.XG[:, :], src, wkeys(t, True) + ["LI"], ["XG"], 384 * gat)
+            for b in range(3):
+                mm(B[PS2][:, 8 * b:8 * b + 8], T.XG[:, 128 * b:128 * b + 128], T.TS[:, 8 * t - 8:8 * t], True, True,
+                   ["XG", "TS%d" % t], ["#6"], 256)
+            tt(T.NE[:, :], B[PS2][:, 0:24], T.OC[:, :], A.is_equal, ["#6", "OC"], ["NE"])
+            tt(named(t), T.NE[:, :], named(t - 1), A.max, ["NE", "nm%d" % (t - 1), "RS"], ["nm%d" % t])
+
+    def tops0():
+        for h in range(2):
+            for b in range(3):
+                o = 128 * b + 64 * h + 7
+                ts(T.TN[:, 24 * h + 8 * b:24 * h + 8 * b + 8], T.C[:, o:o + 57:8], -1537.0, None, A.add, None, ["C"], ["TN0%d%d" % (h, b)])
+
+    def put(q, w, t, kinds, rd=()):
+        for kind in kinds:
+            r = [7 + 2 * t, 8 + 2 * t, TAIL[t]][kind]
+            if kind < 2:
+                in_, k = T.S1[64 * kind:64 * kind + 64, 384 * t:384 * t + 384], "S1%d" % t
+            else:
+                in_, k = T.S2[0:64, 384 * t:384 * t + 384], "S2%d" % t
+            dma(q, W[w][r::16, 385:WW], in_, [k] + list(rd), ["+W%do" % w])
+
+    def sel(j, b, m=128):
+        return T.SM[0:96, 384 * j + 128 * b:384 * j + 128 * b + m]
+
+    def ut(p):
+        return T.UT[0:96, 128 * p:128 * p + 128]
+
+    def gains(t, h):
+        p = 2 * t + h
+        E = nsrc(t, h)
+        n = 24 * E
+        d, dk = B[DB[h]][:, 0:n], "#%d" % DB[h]
+        if t == 3:
+            ma, mb, mc = [m[:, 264 * h:264 * h + n] for m in (T.MA, T.MB, T.MC)]
+            ts(ma, d, 1536.0, MAGIC, A.add, A.add, [dk], ["MA%d" % h], n)
+            if h == 0 and PAR["mod_act"]:
+                act(mb, ma, ["MA%d" % h], ["MB%d" % h], n, bias=-MAGIC)
+            else:
+                ts(mb, ma, -MAGIC, None, A.add, None, ["MA%d" % h], ["MB%d" % h], n)
+            tt(mc, d, mb, A.subtract, [dk, "MB%d" % h], ["MC%d" % h], n)
+            d, dk = mc, "MC%d" % h
+        sc = T.SC[:, 264 * h:264 * h + n]
+        rk = ["RS%d%d" % (t, h)] + (["nm%d" % t] if h == 0 else [])
+        op("v", lambda e: e.tensor_tensor_scan(sc, reset(t, h), d, 0.0, A.mult, A.min), rk + [dk], ["SC%d" % h], n)
+        x = T.SC[:, 264 * h + E - 1:264 * h + n:E]
+        a, bs = T.SA[:, 24 * p:24 * p + 24], T.BS[:, 24 * p:24 * p + 24]
+        ts(a, x, 0.0, -4000.0 if t < 3 else 384.0, A.is_equal, A.mult, ["SC%d" % h], ["SA%d" % p])
+        tt(bs, x, a, A.add, ["SC%d" % h, "SA%d" % p], ["BS%d" % p])
+        if t == 3:
+            for b in range(3):
+                o = 18 + 3 * h + b
+                ts(T.SG[:, o:o + 169:24], T.BS[:, 24 * p + 8 * b:24 * p + 8 * b + 8], 1536.0, None, A.add, None, ["BS%d" % p],
+                   ["SG%d%d" % (h, b)])
+            return
+        old = ["TN0%d%d" % (h, b) for b in range(3)] if t == 0 else ["TN%d" % p]
+        new = T.TN[:, 24 * p + 48:24 * p + 72]
+        tt(new, T.TN[:, 24 * p:24 * p + 24], bs, A.max, old + ["BS%d" % p], ["TN%d" % (p + 2)])
+        for d2 in range(2):
+            ts(T.TC[:, 96 * p + d2:96 * p + 96:4], new, 1537.0, None, A.add, None, ["TN%d" % (p + 2), "TCz0", "TCz1"], ["TC%d%d" % (p, d2)])
+        mm(B[PU][0:96, 0:128], T.TC[:, 96 * p:96 * p + 96], T.ID[:, :], True, True, ["TC%d0" % p, "TC%d1" % p, "ID"], ["#4"], 128)
+        op("v", lambda e: e.tensor_copy(ut(p), B[PU][0:96, 0:128]), ["#4"], ["UT%d" % p], 128)
+        cs = [slice(128 * b, 128 * b + 128) for b in range(3)]
+        if h == 0:
+            for b in range(3):
+                if t == 0:
+                    mm(B[PS1][:, cs[b]], T.SO0[:, :], T.U[:, cs[b]], True, False, ["U", "SO0"], ["#5"], 128)
+                else:
+                    mm(B[PS1][:, cs[b]], sel(0, b), ut(p - 2), True, False, ["UT%d" % (p - 2), "SM0%d" % b], ["#5"], 128)
+                mm(B[PS1][:, cs[b]], sel(1, b), ut(p), False, True, ["UT%d" % p, "SM1%d" % b], ["#5"], 128)
+            for b in range(3):
+                mm(B[PS2][0:64, cs[b]], sel(0, b, 64), ut(p), True, True, ["UT%d" % p, "SM0%d" % b], ["#6"], 128)
+            act(T.S1[:, 384 * t:384 * t + 384], B[PS1][:, 0:384], ["#5"], ["S1%d" % t], 384, bias=-K)
+            if PAR["s2v"]:
+                ts(T.S2[0:64, 384 * t:384 * t + 384], B[PS2][0:64, 0:384], 1537.0 - K, None, A.add, None, ["#6"], ["S2%d" % t], 384)
+            else:
+                act(T.S2[0:64, 384 * t:384 * t + 384], B[PS2][0:64, 0:384], ["#6"], ["S2%d" % t], 384, bias=1537.0 - K)
+            put("s", (t + 1) % 2, t, [0, 1, 2])
+        else:
+            for b in range(3):
+                hi, hk = (T.SH3[:, :], "SH3") if t == 2 else (T.SWH[:, 1024:1152], "SWH8")
+                mm(B[PS1][:, cs[b]], hi, T.U[:, cs[b]], True, False, ["U", hk], ["#5"], 128)
+                mm(B[PS1][:, cs[b]], T.SWL[:, 1024:1152], T.U[:, cs[b]], False, False, ["U", "SWL8"], ["#5"], 128)
+                for u in range(t + 1):
+                    mm(B[PS1][:, cs[b]], sel(3 + u, b), ut(2 * u + 1), False, u == t, ["UT%d" % (2 * u + 1), "SM%d%d" % (3 + u, b)],
+                       ["#5"], 128)
+            act(W[(t + 1) % 2][:, 0:384], B[PS1][:, 0:384], ["#5", "c%d" % (25 + t)], ["W%dt" % ((t + 1) % 2)], 384, bias=col[25 + t])
+        for b in range(3):
+            mm(B[YB[h]][:, cs[b]], sel(2, b), ut(p), True, True, ["UT%d" % p, "SM2%d" % b], ["#%d" % YB[h]], 128)
+        ycopy(t + 1, h)
+
+    def early_gains():
+        ks = ["BS%d" % p for p in range(6)]
+        ts(T.GA[:, :], T.BS[:, 0:144], -3500.0, 4384.0, A.is_lt, A.mult, ks, ["GA"], 144)
+        tt(T.GB[:, :], T.BS[:, 0:144], T.GA[:, :], A.add, ks + ["GA"], ["GB"], 288)
+        for q in range(8):
+            ts(T.SG[:, 24 * q:24 * q + 18], T.GB[:, q::8], 1536.0, None, A.add, None, ["GB"], ["SGq%d" % q])
+
+    def phase(t, h, names):
+        nf, n = PAR["fused"][2 * t + h], len(names)
+        fz = set(((2 * j + 1) * n) // (2 * nf) for j in range(nf))
+        for i, name in enumerate(names):
+            if name == "ys" and t:
+                stores(t)
+            source(t, h, name, i in fz)
+
+    ycopy(0, 0)
+    edges(0, 0)
+    stores(0)
+    ycopy(0, 1)
+    for t in range(RO):
+        if t:
+            gains(t - 1, 1)
+            edges(t, 0)
+        phase(t, 0, ["cp", "ys", 0, 1, 2, 3, 4, 5] if t == 0 else list(range(5 + t)) + ["cp", "ys", 5 + t])
+        if t == 0:
+            tops0()
+        gains(t, 0)
+        if t in (1, 2):
+            put("g", (t + 1) % 2, t - 1, [0, 1], ["EL%d0" % (5 + t)])
+        if t == 1:
+            dma("g", T.yp[:, :], T.ownf[:, :], ["ownf"], ["yp"])
+        if t:
+            edges(t, 1)
+        if t == 3:
+            early_gains()
+        phase(t, 1, ["cp"] + list(range(6 + t)))
+    gains(3, 1)
+
+    sg = ["SGq%d" % q for q in range(8)] + ["SG%d%d" % (h, b) for h in range(2) for b in range(3)]
+    tr1 = [RemoteDMATransfer(dst_ids=[dst(topo, hc, core)], dma_engine_mask=bits(inner[4 * j:4 * j + 4]), remote_sem=T.sem.h1,
+                             src=T.SG[:, 24 * span_start(qs):24 * span_start(qs) + 96], dst=T.handg[:, :])
+           for j, (hc, qs) in enumerate(helpers)]
+    tr2 = [RemoteDMATransfer(dst_ids=[dst(topo, cores[q], core)], dma_engine_mask=bits(dm[j]), remote_sem=T.sem.arrg,
+                             src=T.SG[:, 24 * q:24 * q + 24], dst=T.RG[:, 24 * rank:24 * rank + 24]) for j, q in enumerate(direct)]
+    sent[0] += 4 * len(helpers) + sum(len(m) for m in dm)
+    raw("g", lambda e: e.remote_dma_fused(tr1, local_sem=T.sem.sent), sg, ["away1"], 1.0)
+    raw("g", lambda e: e.remote_dma_fused(tr2, local_sem=T.sem.sent), sg, ["away2"], 1.0)
+    op("v", lambda e: e.tensor_copy(T.RG[:, 24 * rank:24 * rank + 24], T.SG[:, 24 * rank:24 * rank + 24]), sg, ["RG"])
+    raw("p", lambda e: e.wait_ge(T.sem.arrg, narr), ["away1", "away2"], ["home"], 6.0)
+    for j in range(2):
+        mm(B[j][0:96, 0:128], T.RG[:, 96 * j:96 * j + 96], T.ID[:, :], True, True, ["RG", "ID", "home"], ["#%d" % j], 128)
+    act(T.OG[0:96, 0:128], B[0][0:96, 0:128], ["#0"], ["OG0"], 128, bias=1536.0)
+    ts(T.OG[0:96, 128:256], B[1][0:96, 0:128], 1536.0, None, A.add, None, ["#1"], ["OG1"], 128)
+    for j in range(8):
+        q = (j % 2) * 4 + j // 2
+        dma("as"[j % 2], T.yp[16 * q + 6:16 * q + 10, :], T.OG[24 * (q % 4):24 * (q % 4) + 24, 128 * (q // 4):128 * (q // 4) + 128],
+            ["OG%d" % (q // 4)], ["+yp"])
+    raw("g", lambda e: e.wait_ge(T.sem.sent, sent[0]), [], [], 0.0)
+    emit(g, T, ops)
+
+
+def depends(ops):
+    writers, readers, base, bank, tail = {}, {}, {}, {}, {}
+    deps = []
+    for i, o in enumerate(ops):
+        d = set()
+        if o["q"] in "gs" or (o["q"] == "a" and o["kind"] == "dma"):
+            d.update(tail.get(o["q"], []))
+            tail[o["q"]] = [i]
+        for k in o["rd"] + o["wr"]:
+            if k[0] == "#":
+                last = bank.setdefault(k, {})
+                d.update(last.values())
+                last[o["q"]] = i
+        soft = set(j for j in d if ops[j]["q"] == o["q"])
+        hard = d - soft
+        for k in o["rd"]:
+            if k[0] != "#":
+                hard.update(writers.get(k, []))
+        for k in o["wr"]:
+            if k[0] == "#":
+                continue
+            if k[0] == "+":
+                k = k[1:]
+                if readers.get(k) or k not in base:
+                    base[k] = list(writers.get(k, [])) + list(readers.get(k, []))
+                    writers[k] = list(writers.get(k, []))
+                    readers[k] = []
+                hard.update(base[k])
+                writers[k].append(i)
+            else:
+                hard.update(writers.get(k, []))
+                hard.update(readers.get(k, []))
+                writers[k] = [i]
+                readers[k] = []
+                base.pop(k, None)
+        for k in o["rd"]:
+            if k[0] != "#":
+                readers.setdefault(k, []).append(i)
+        hard.discard(i)
+        soft.discard(i)
+        deps.append((hard, soft - hard))
+    return deps
+
+
+def arrange(ops, deps):
+    n = len(ops)
+    after = [[] for i in range(n)]
+    for i, (hard, soft) in enumerate(deps):
+        for j in hard | soft:
+            after[j].append(i)
+    left = [len(h | s) for h, s in deps]
+    ready = {q: [] for q in "gvaps"}
+    can = [0.0] * n
+    free = {q: 0.0 for q in "gvaps"}
+    for i in range(n):
+        if not left[i]:
+            ready[ops[i]["q"]].append(i)
+    order = []
+    while len(order) < n:
+        t0, q = min((max(free[q], min(can[i] for i in ready[q])), q) for q in ready if ready[q])
+        i = min(i for i in ready[q] if can[i] <= t0 + PAR["slack"])
+        ready[q].remove(i)
+        start = max(free[q], can[i])
+        end = start + ops[i]["cost"]
+        free[q] = start + ((1.0 if q == "g" else 0.1) if ops[i]["kind"] == "dma" else ops[i]["cost"])
+        order.append(i)
+        for j in after[i]:
+            can[j] = max(can[j], end + 0.08 if i in deps[j][0] or ops[i]["kind"] == "raw" else start)
+            left[j] -= 1
+            if not left[j]:
+                ready[ops[j]["q"]].append(j)
+    return order
+
+
+def emit(g, T, ops):
+    eng = {"g": g, "v": g.vector, "a": g.scalar, "p": g.tensor, "s": g.sync}
+    deps = depends(ops)
+    order = arrange(ops, deps)
+    place = {i: n for n, i in enumerate(order)}
+    seen = {q: {} for q in eng}
+    need, waits = set(), {}
+    for i in order:
+        late = {}
+        for j in deps[i][0]:
+            if ops[j]["kind"] == "dma":
+                late[("d", j)] = j
+            elif ops[j]["kind"] == "c":
+                k = ops[j]["q"]
+                if k not in late or place[late[k]] < place[j]:
+                    late[k] = j
+        waits[i] = []
+        for k, j in late.items():
+            if seen[ops[i]["q"]].get(k, -1) < place[j]:
+                seen[ops[i]["q"]][k] = place[j]
+                waits[i].append(j)
+                need.add(j)
+    count = {q: 0 for q in eng}
+    mark = {}
+    nd = 0
+    for i in order:
+        o = ops[i]
+        e = eng[o["q"]]
+        for j in waits[i]:
+            e.wait_ge(mark[j][0], mark[j][1])
+        ins = o["fn"](e)
+        if o["kind"] == "dma":
+            mark[i] = (T.sem["d%d" % nd], 16)
+            nd += 1
+            ins.then_inc(mark[i][0], 16)
+        elif i in need:
+            count[o["q"]] += 1
+            mark[i] = (T.sem["c" + o["q"]], count[o["q"]])
+            ins.then_inc(mark[i][0], 1)
+    for i in order:
+        if ops[i]["kind"] == "dma" and i not in need:
+            g.wait_ge(mark[i][0], 16)

@@ -8,47 +8,24 @@ RING = 10
 MAGIC = 1.5 * 2.0 ** 35
 EDGE_ROWS = [0, 2, 4, 6, 12, 14]
 TAIL = [9, 11, 14]
-PAR = {"fused": [3, 1, 3, 0, 3, 0, 2, 0], "edge_act": [0] * 8, "ecopy": [0, 1, 3, 5], "s2v": 0, "gat": 1.56, "cyc": 0.00104,
-       "pe": 0.00052, "dma": 4.0, "slack": 0.12, "mod_act": 1}
+PAR = {"fused": [3, 0, 3, 0, 3, 0, 1, 0], "gat": 1.56, "cyc": 0.00104, "pe": 0.00052, "dma": 3.0, "slack": 0.12, "arr": 4.0}
 
 f32, f16, bf16, i32, u16 = "float32", "float16", "bfloat16", "int32", "uint16"
-SCRATCH = {
-    "stage": ("dram", [8, 128, 64], i32), "land": ("dram", [8, 128, 64], i32), "hand": ("dram", [2, 128, 64], i32),
-    "handg": ("sbuf", [128, 96], f16), "SG": ("sbuf", [128, 192], f16), "RG": ("sbuf", [128, 192], f16),
-    "OG": ("sbuf", [128, 256], f32),
-    "own": ("sbuf", [128, 768], i32), "ownf": ("sbuf", [128, 768], f32),
-    "nat": ("sbuf", [128, 384], i32), "natf": ("sbuf", [128, 384], f16), "natm": ("sbuf", [128, 384], f16),
-    "L": ("sbuf", [128, 144], i32), "La": ("sbuf", [128, 144], f32), "Lb": ("sbuf", [128, 144], f32),
-    "LI": ("sbuf", [128, 144], u16), "EL": ("sbuf", [128, 432], u16), "EG": ("sbuf", [128, 768], f16),
-    "EF": ("sbuf", [128, 768], f32),
-    "C": ("sbuf", [128, 384], f16), "U": ("sbuf", [128, 384], f16),
-    "W0": ("sbuf", [128, 3464], f32), "W1": ("sbuf", [128, 3464], f32),
-    "KI": ("sbuf", [128, 8], i32), "KJ": ("sbuf", [128, 9], i32), "KF": ("sbuf", [128, 9], f32), "KC": ("sbuf", [128, 32], f32),
-    "J": ("sbuf", [128, 160], f32), "CP": ("sbuf", [128, 128], f32), "CPW": ("sbuf", [128, 128], f32),
-    "CG": ("sbuf", [128, 128], f32), "C16": ("sbuf", [128, 16], f32), "CS": ("sbuf", [128, 128], f32),
-    "CQ": ("sbuf", [128, 128], f32), "CV": ("sbuf", [128, 384], f32), "CO": ("sbuf", [128, 24], f32),
-    "ID": ("sbuf", [128, 128], f16), "P1": ("sbuf", [128, 128], f16), "P2": ("sbuf", [128, 128], f16),
-    "H1": ("sbuf", [128, 128], bf16), "H2": ("sbuf", [128, 128], bf16), "HI": ("sbuf", [128, 128], bf16),
-    "LO": ("sbuf", [128, 128], bf16), "BD": ("sbuf", [128, 128], bf16),
-    "SWH": ("sbuf", [128, 1152], bf16), "SWL": ("sbuf", [128, 1152], bf16),
-    "M16": ("sbuf", [128, 16], f32), "MK": ("sbuf", [128, 16], f32), "MQ": ("sbuf", [128, 16], f32), "GM": ("sbuf", [128, 8], f32),
-    "WT": ("sbuf", [128, 8], f32), "SS": ("sbuf", [128, 32], f32), "TS": ("sbuf", [128, 24], f32), "NS": ("sbuf", [128, 8], bf16),
-    "WF": ("sbuf", [128, 160], f32), "WH": ("sbuf", [128, 160], bf16), "WD": ("sbuf", [128, 960], bf16),
-    "SB": ("sbuf", [128, 768], bf16), "SM": ("sbuf", [128, 2304], bf16), "SH3": ("sbuf", [128, 128], bf16), "M3": ("sbuf", [128, 4], f32),
-    "SO0": ("sbuf", [128, 128], f16), "SY0": ("sbuf", [128, 256], f16),
-    "OK": ("sbuf", [128, 384], f32), "OC": ("sbuf", [128, 24], f32), "R0": ("sbuf", [128, 384], bf16),
-    "RS": ("sbuf", [128, 8 * 264], bf16), "SC": ("sbuf", [128, 2 * 264], f32), "MA": ("sbuf", [128, 528], f32),
-    "MB": ("sbuf", [128, 528], f32), "MC": ("sbuf", [128, 528], f32),
-    "TN": ("sbuf", [128, 192], f32), "SA": ("sbuf", [128, 192], f32), "BS": ("sbuf", [128, 192], f32),
-    "GA": ("sbuf", [128, 144], f32), "GB": ("sbuf", [128, 144], f32), "TC": ("sbuf", [128, 576], f16),
-    "UT": ("sbuf", [128, 6 * 128], f16), "S1": ("sbuf", [128, 3 * 384], f32), "S2": ("sbuf", [128, 3 * 384], f32),
-    "YS": ("sbuf", [128, 768], f32), "G": ("sbuf", [128, RING * 384], f32), "XG": ("sbuf", [128, 384], f32),
-    "XB": ("sbuf", [128, 384], bf16), "NE": ("sbuf", [128, 24], f32),
-}
+SCRATCH = {"stage": ("dram", [8, 128, 64], i32), "land": ("dram", [8, 128, 64], i32), "hand": ("dram", [2, 128, 64], i32)}
+for _d, _l in [
+    (f16, "handg 96 SG 192 RG 192 natf 384 natm 384 EG 768 U2 384 C 384 U 384 ID 128 P1 128 P2 128 SO0 128 SY0 256 TC 576 UT 768"),
+    (f32, "OG 256 ownf 768 La 144 Lb 144 MQ2 8 W0 3464 W1 3464 KF 9 KC 32 J 160 CP 128 CPW 128 CG 128 C16 16 CS 128 CQ 128 CV 384 "
+          "CO 24 M16 16 MK 16 MQ 16 GM 8 WT 8 SS 32 TS 24 WF 160 TE 768 M3 4 OK 384 OC 24 SC 528 MA 528 MB 528 MC 528 TN 192 SA 192 "
+          "BS 192 GA 144 GB 144 S1 1152 S2 1152 YS 768 G 3840 XG 384 NE 24"),
+    (bf16, "DUP 128 HL 128 H1 128 H2 128 HI 128 LO 128 BD 128 SWH 1152 SWL 1152 NS 8 WH 160 WD 48 SB 768 SM 2304 SH3 128 R0 384 "
+           "ONE 264 RS 2112 XB 384"),
+    (i32, "own 768 nat 384 L 144 KI 8 KJ 9"), (u16, "LI 144 EL 432")]:
+    _w = _l.split()
+    for _i in range(0, len(_w), 2):
+        SCRATCH[_w[_i]] = ("sbuf", [128, int(_w[_i + 1])], _d)
 for _b in range(8):
     SCRATCH["B%d" % _b] = ("psum", [128, 512], f32)
-NDMA = 56
-SEMAPHORES = ["cv", "ca", "cp", "cg", "sent", "arr", "arrg", "h0", "h1"] + ["d%d" % _i for _i in range(NDMA)]
+SEMAPHORES = ["cv", "ca", "cp", "cg", "sent", "arr", "arrg", "h0", "h1"] + ["d%d" % _i for _i in range(56)]
 
 A = AluOpType
 IDENT = ActivationFunctionType.Identity
@@ -198,8 +175,14 @@ def rank_program(g, core, T, topo):
     iota(T.CQ[:, :], [[100, 2], [0, 8], [1, 8]], 0, 0, ["CQ"], 128)
     iota(T.CO[:, :], [[128, 3], [384, 8]], -1536, 1, ["CO"], 24)
     iota(T.CV[:, :], [[1, 384]], 0, 0, ["CV"], 384)
+    iota(T.SB[:, 384:768], [[0, 384]], 0, 0, ["SB3", "SB4", "SB5"], 384)
+    iota(T.ONE[:, :], [[0, 264]], 1, 0, ["ONE"], 264)
+    for p in range(8):
+        n = 8 + p // 2 - p % 2
+        op("g", lambda e, p=p, n=n: e.affine_select(T.RS[:, 264 * p:264 * p + 24 * n], T.ONE[:, 0:24 * n], [[0, 24], [1, n]], A.is_gt, 0.0, 0, 0),
+           ["ONE"], ["RS%d%d" % (p // 2, p % 2)], cost=0.17 + 48 * n * cyc)
     narr = arrivals(T, topo, rank)
-    raw("s", lambda e: e.wait_ge(T.sem.arr, narr), ["away"], [], 8.0)
+    raw("s", lambda e: e.wait_ge(T.sem.arr, narr), ["away"], [], PAR["arr"])
     dma("s", T.nat[0:96, :], T.land[:, 0:72, :], ["landown"], ["nat"])
     dma("s", T.L[:, 0:48], T.land[:, 72:84, :], ["landown"], ["L0"])
     dma("s", T.L[:, 48:96], T.land[:, 84:96, :], ["landown"], ["L1"])
@@ -250,7 +233,12 @@ def rank_program(g, core, T, topo):
     ts(T.WT[:, 4:8], T.WT[:, 0:4], kr, col[13], A.is_gt, A.max, ["WT0", "KF", "c13"], ["WT1"])
     for t in range(3):
         act(col[16 + t], T.WT[:, 4 + t:5 + t], ["WT1", "c12"], ["c%d" % (16 + t)], scale=col[12])
-    for q in range(8):
+    tt(T.MQ2[:, :], T.MQ[:, 0:8], T.MQ[:, 8:16], A.add, ["MQ"], ["MQ2"])
+    act(T.HL[0:64, :], T.HI[0:64, :], ["HI"], ["+HL"], 128)
+    act(T.HL[64:128, :], T.LO[64:128, :], ["LO"], ["+HL"], 128)
+    for q in range(2, 8):
+        act(T.SWH[:, 128 * q:128 * q + 128], T.HL[:, :], ["HL", "MQ2"], ["SWH%d" % q], 128, scale=T.MQ2[:, q:q + 1])
+    for q in range(2):
         act(T.SWL[:, 128 * q:128 * q + 128], T.LO[:, :], ["LO", "MQ"], ["SWL%d" % q], 128, scale=T.MQ[:, q:q + 1])
         act(T.SWH[:, 128 * q:128 * q + 128], T.HI[:, :], ["HI", "MQ"], ["SWH%d" % q], 128, scale=T.MQ[:, q:q + 1])
     tt(T.SWL[:, 1024:1152], T.LO[:, :], T.BD[:, :], A.mult, ["LO", "BD"], ["SWL8"], 256)
@@ -258,9 +246,11 @@ def rank_program(g, core, T, topo):
     ts(T.ID[:, :], T.J[:, 0:128], 0.0, None, A.is_equal, None, ["J"], ["ID"], 128)
     ts(T.WF[:, :], T.J[:, :], 15.0, None, A.is_equal, None, ["J"], ["WF"], 160)
     act(T.WH[:, :], T.WF[:, :], ["WF"], ["WH"], 160)
+    for j in range(2):
+        act(T.DUP[:, 64 * j:64 * j + 64], T.WF[:, 15:79], ["WF"], ["+DUP"])
     act(T.MK[:, :], T.M16[:, :], ["M16"], ["MK"], scale=1.0 / K)
     for j, r in enumerate(EDGE_ROWS):
-        act(T.WD[:, 160 * j:160 * j + 160], T.WF[:, :], ["WF", "M16"], ["WD%d" % j], 160, scale=T.M16[:, r:r + 1])
+        act(T.WD[:, 8 * j:8 * j + 8], T.GM[:, :], ["GM", "M16"], ["+WD"], scale=T.M16[:, r:r + 1])
     ms(T.R0[:, :], 4000.0, ["R0"], 192)
     ms(T.R0[:, 0::8], -1536.0, ["R0"])
     ts(T.CS[:, 6::8], T.CS[:, 6::8], -2.0, None, A.add, None, ["CS"], ["CS"])
@@ -270,19 +260,62 @@ def rank_program(g, core, T, topo):
     ts(T.SY0[:, 0:128], T.CG[:, :], k3, col[5], A.is_equal, A.mult, ["CG", "KF", "c5"], ["SY00"], 128)
     ts(T.SY0[:, 128:256], T.CG[:, :], col[4], col[5], A.is_equal, A.mult, ["CG", "c4", "c5"], ["SY01"], 128)
     ts(T.SO0[:, :], T.CQ[:, :], k3, col[8], A.is_equal, A.mult, ["CQ", "KF", "c8"], ["SO0"], 128)
+    ms(T.W0[:, 384:385], -1537.0 * K, ["W0o"])
+
+    def nsrc(t, h):
+        return 8 + t - h
+
+    def reset(t, h):
+        o = 264 * (2 * t + h)
+        return T.RS[:, o:o + 24 * nsrc(t, h)]
+
+    def named(t):
+        o = 264 * 2 * t
+        return T.RS[:, o + 1:o + 24 * nsrc(t, 0):nsrc(t, 0)]
+
+    ts(T.natf[0:96, :], T.nat[0:96, :], -1535.0, None, A.add, None, ["nat"], ["natf"], 384)
+    ts(T.natm[0:96, :], T.nat[0:96, :], 3071.5, None, A.is_gt, None, ["nat"], ["natm"], 384)
+    for b in range(3):
+        mm(B[PU][:, 128 * b:128 * b + 128], T.natf[0:96, 128 * b:128 * b + 128], T.P1[0:96, :], True, False, ["natf", "P1"], ["#4"], 128)
+        mm(B[PU][:, 128 * b:128 * b + 128], T.natm[0:96, 128 * b:128 * b + 128], T.P2[0:96, :], False, True, ["natm", "P2"], ["#4"], 128)
+    op("v", lambda e: e.tensor_tensor_scan(T.C[:, :], T.R0[:, :], B[PU][:, 0:384], -1536.0, A.min, A.max), ["R0", "#4"], ["C"], 384)
+    for b in range(3):
+        mm(B[PL][:, 128 * b:128 * b + 128], T.C[:, 128 * b:128 * b + 128], T.ID[:, :], True, True, ["C", "ID"], ["#7"], 128)
+    op("v", lambda e: e.tensor_copy(T.U[:, :], B[PL][:, 0:384]), ["#7"], ["U"], 384)
+    for b in range(3):
+        mm(B[1][:, 128 * b:128 * b + 128], T.DUP[0:64, :], T.U[0:64, 128 * b:128 * b + 128], True, True, ["U", "DUP"], ["#1"], 128)
+    op("v", lambda e: e.tensor_copy(T.U2[:, :], B[1][:, 0:384]), ["#1"], ["U2"], 384)
+    ts(T.La[:, :], T.L[:, :], 3071.5, 3457.0, A.is_lt, A.mult, ["L0", "L1", "L2", "L3"], ["La"], 144)
+    tt(T.Lb[:, :], T.L[:, :], T.La[:, :], A.add, ["La"], ["Lb"], 288)
+    ts(T.LI[:, :], T.Lb[:, :], -3072.0, None, A.add, None, ["Lb"], ["LI"], 144)
+    banks = [2, 3, 5, 6, 4, 0, 1]
+    for j, q in enumerate([8, 0, 1, 2, 3, 4, 5, 6, 7]):
+        b = banks[j % 7]
+        if j < 3:
+            mm(B[b][:, 0:384], T.SWH[:, 128 * q:128 * q + 128], T.U[:, :], True, False, ["U", "SWH%d" % q], ["#%d" % b], 384)
+            mm(B[b][:, 0:384], T.SWL[:, 128 * q:128 * q + 128], T.U[:, :], False, True, ["U", "SWL%d" % q], ["#%d" % b], 384)
+        else:
+            mm(B[b][:, 0:384], T.SWH[:, 128 * q:128 * q + 128], T.U2[:, :], True, True, ["U2", "SWH%d" % q], ["#%d" % b], 384)
+        c0 = 385 + 384 * q if q < 8 else 0
+        if j in (0, 1, 3, 5, 7):
+            act(T.W0[:, c0:c0 + 384], B[b][:, 0:384], ["#%d" % b, "c10"], ["W0p%d" % q], 384, bias=col[10])
+        else:
+            ts(T.W0[:, c0:c0 + 384], B[b][:, 0:384], col[10], None, A.add, None, ["#%d" % b, "c10"], ["W0p%d" % q], 384)
+    first = ["W0p%d" % q for q in range(9)]
+    for h in range(2):
+        mm(B[YB[h]][:, 0:384], T.SY0[:, 128 * h:128 * h + 128], T.U[:, :], True, True, ["U", "SY0%d" % h], ["#%d" % YB[h]], 384)
+    dma("s", T.W1[:, 384:WW], T.W0[:, 384:WW], first[:8] + ["W0o"], ["W1o"], 8.0)
+
     for t in range(4):
         c = 16 + t if t < 3 else 15
         act(T.SS[:, 8 * t:8 * t + 8], T.GM[:, :], ["GM", "c%d" % c], ["SS%d" % t], scale=col[c])
     for t in range(1, 4):
         act(T.TS[:, 8 * t - 8:8 * t], T.GM[:, :], ["GM", "M16"], ["TS%d" % t], scale=T.M16[:, 6 + 2 * t:7 + 2 * t])
     ts(T.NS[:, :], T.SS[:, 0:8], 0.0, None, A.max, None, ["SS0"], ["NS"])
-    ms(T.W0[:, 384:385], -1537.0 * K, ["W0o"])
-    ms(T.RS[:, :], 1.0, ["RS"], 1056)
     ts(T.SB[:, 0:128], T.CQ[:, :], kq, col[1], A.is_equal, A.mult, ["CQ", "KF", "c1"], ["SB0"], 128)
     ts(T.SB[:, 128:192], T.CQ[:, 0:64], kq, col[2], A.is_equal, A.mult, ["CQ", "KF", "c2"], ["+SB1"])
     ts(T.SB[:, 192:256], T.CQ[:, 0:64], kq, col[3], A.is_equal, A.mult, ["CQ", "KF", "c3"], ["+SB1"])
     ts(T.SB[:, 256:384], T.CG[:, :], kq, col[3], A.is_equal, A.mult, ["CG", "KF", "c3"], ["SB2"], 128)
-    ms(T.SB[:, 384:768], 0.0, ["SB3", "SB4", "SB5"], 192)
     for t in range(3):
         for r, c in zip([7 + 2 * t, 8 + 2 * t, TAIL[t]], [2, 3, 1]):
             ts(T.SB[:, 384 + 128 * t + r:512 + 128 * t:16], T.C16[:, 0:8], kq, col[c], A.is_equal, A.mult, ["C16", "KF", "c%d" % c],
@@ -298,50 +331,7 @@ def rank_program(g, core, T, topo):
     act(T.OC[:, :], T.CO[:, :], ["CO"], ["OC"], scale=K)
     for j in range(2):
         ts(T.TC[:, 288 * j:288 * j + 288], T.R0[:, 0:288], 0.0, None, A.mult, None, ["R0"], ["TCz%d" % j], 144)
-
-    def nsrc(t, h):
-        return 8 + t - h
-
-    def reset(t, h):
-        o = 264 * (2 * t + h)
-        return T.RS[:, o:o + 24 * nsrc(t, h)]
-
-    def named(t):
-        o = 264 * 2 * t
-        return T.RS[:, o + 1:o + 24 * nsrc(t, 0):nsrc(t, 0)]
-
-    for t in range(4):
-        for h in range(2):
-            o = 264 * (2 * t + h)
-            op("v", lambda e, a=T.RS[:, o:o + 24 * nsrc(t, h):nsrc(t, h)]: e.memset(a, 0.0), ["RS"], ["RS%d%d" % (t, h)])
     op("v", lambda e: e.tensor_copy(T.ownf[:, :], T.own[:, :]), ["own"], ["ownf"], 768)
-
-    ts(T.natf[0:96, :], T.nat[0:96, :], -1535.0, None, A.add, None, ["nat"], ["natf"], 384)
-    ts(T.natm[0:96, :], T.nat[0:96, :], 3071.5, None, A.is_gt, None, ["nat"], ["natm"], 384)
-    for b in range(3):
-        mm(B[PU][:, 128 * b:128 * b + 128], T.natf[0:96, 128 * b:128 * b + 128], T.P1[0:96, :], True, False, ["natf", "P1"], ["#4"], 128)
-        mm(B[PU][:, 128 * b:128 * b + 128], T.natm[0:96, 128 * b:128 * b + 128], T.P2[0:96, :], False, True, ["natm", "P2"], ["#4"], 128)
-    op("v", lambda e: e.tensor_tensor_scan(T.C[:, :], T.R0[:, :], B[PU][:, 0:384], -1536.0, A.min, A.max), ["R0", "#4"], ["C"], 384)
-    for b in range(3):
-        mm(B[PL][:, 128 * b:128 * b + 128], T.C[:, 128 * b:128 * b + 128], T.ID[:, :], True, True, ["C", "ID"], ["#7"], 128)
-    op("v", lambda e: e.tensor_copy(T.U[:, :], B[PL][:, 0:384]), ["#7"], ["U"], 384)
-    ts(T.La[:, :], T.L[:, :], 3071.5, 3457.0, A.is_lt, A.mult, ["L0", "L1", "L2", "L3"], ["La"], 144)
-    tt(T.Lb[:, :], T.L[:, :], T.La[:, :], A.add, ["La"], ["Lb"], 288)
-    ts(T.LI[:, :], T.Lb[:, :], -3072.0, None, A.add, None, ["Lb"], ["LI"], 144)
-    banks = [2, 3, 5, 6, 4, 0, 1]
-    for q in range(9):
-        b = banks[q % 7]
-        mm(B[b][:, 0:384], T.SWH[:, 128 * q:128 * q + 128], T.U[:, :], True, False, ["U", "SWH%d" % q], ["#%d" % b], 384)
-        mm(B[b][:, 0:384], T.SWL[:, 128 * q:128 * q + 128], T.U[:, :], False, True, ["U", "SWL%d" % q], ["#%d" % b], 384)
-        c0 = 385 + 384 * q if q < 8 else 0
-        if q % 2 == 0:
-            act(T.W0[:, c0:c0 + 384], B[b][:, 0:384], ["#%d" % b, "c10"], ["W0p%d" % q], 384, bias=col[10])
-        else:
-            ts(T.W0[:, c0:c0 + 384], B[b][:, 0:384], col[10], None, A.add, None, ["#%d" % b, "c10"], ["W0p%d" % q], 384)
-    first = ["W0p%d" % q for q in range(9)]
-    for h in range(2):
-        mm(B[YB[h]][:, 0:384], T.SY0[:, 128 * h:128 * h + 128], T.U[:, :], True, True, ["U", "SY0%d" % h], ["#%d" % YB[h]], 384)
-    dma("s", T.W1[:, 384:WW], T.W0[:, 384:WW], first[:8] + ["W0o"], ["W1o"], 8.0)
 
     def wkeys(t, full):
         w = "W%d" % (t % 2)
@@ -358,26 +348,24 @@ def rank_program(g, core, T, topo):
         if t == 0:
             ts(T.EG[:, :], window(0, True).indirect(T.LI[:, 0:48]), 1.0 / K, None, A.mult, None, wkeys(0, True) + ["LI"],
                ["EG0", "EG1"], 768 * gat)
-            for j in range(6):
+            for j in range(2):
+                b = [PL, PU][j]
                 for x in range(16):
-                    o = 160 * j + 15 + EDGE_ROWS[j] - x
-                    mm(B[PL][:, 48 * j:48 * j + 48], T.WD[:, o:o + 128], T.EG[:, x::16], x == 0, x == 15, ["EG0", "EG1", "WD%d" % j], ["#7"], 64)
-                if j in PAR["ecopy"]:
-                    j0 = max([-1] + [i for i in PAR["ecopy"] if i < j]) + 1
-                    ts(T.EL[:, 48 * j0:48 * j + 48], B[PL][:, 48 * j0:48 * j + 48], 1537.0, None, A.add, None, ["#7"],
-                       ["EL%d%d" % (i, hh) for i in range(j0, j + 1) for hh in range(2)], 48 * (j + 1 - j0))
+                    mm(B[b][0:48, x:384:16], T.EG[:, x::16], T.WD[:, 24 * j:24 * j + 24], True, True, ["EG0", "EG1", "WD"], ["#%d" % b], 48)
+                act(T.TE[0:48, 384 * j:384 * j + 384], B[b][0:48, 0:384], ["#%d" % b], ["TE%d" % j], 384)
+            for j in range(2):
+                b = [PS1, PL][j]
+                for i in range(3 * j, 3 * j + 3):
+                    mm(B[b][:, 48 * i:48 * i + 48], T.TE[0:48, 128 * i:128 * i + 128], T.WF[0:48, 15:63], True, True, ["TE%d" % j, "WF"],
+                       ["#%d" % b], 256)
+                ts(T.EL[:, 144 * j:144 * j + 144], B[b][:, 144 * j:144 * j + 144], 1537.0, None, A.add, None, ["#%d" % b],
+                   ["EL%d%d" % (i, hh) for i in range(3 * j, 3 * j + 3) for hh in range(2)], 144)
             return
         src, rd = window(t, True).indirect(T.LI[:, 24 * h:24 * h + 24]), wkeys(t, True) + ["LI", "MK"]
-        mk = T.MK[:, 6 + 2 * t:7 + 2 * t]
-        by_act = PAR["edge_act"][2 * t + h]
-        if by_act:
-            act(T.EF[:, 384 * h:384 * h + 384], src, rd, ["EG%d" % h], 384 * gat, scale=mk)
-        else:
-            ts(T.EG[:, 384 * h:384 * h + 384], src, mk, None, A.mult, None, rd, ["EG%d" % h], 384 * gat)
+        ts(T.EG[:, 384 * h:384 * h + 384], src, T.MK[:, 6 + 2 * t:7 + 2 * t], None, A.mult, None, rd, ["EG%d" % h], 384 * gat)
         for x in range(16):
             o = 15 + 6 + 2 * t - x
-            l, r, k, n = (T.WF, T.EF, "WF", 256) if by_act else (T.WH, T.EG, "WH", 64)
-            mm(B[PL][:, 0:24], l[:, o:o + 128], r[:, 384 * h + x:384 * h + 384:16], x == 0, x == 15, ["EG%d" % h, k], ["#7"], n)
+            mm(B[PL][:, 0:24], T.WH[:, o:o + 128], T.EG[:, 384 * h + x:384 * h + 384:16], x == 0, x == 15, ["EG%d" % h, "WH"], ["#7"], 64)
         c = 48 * (5 + t) + 24 * h
         ts(T.EL[:, c:c + 24], B[PL][:, 0:24], 1537.0, None, A.add, None, ["#7"], ["EL%d%d" % (5 + t, h)])
 
@@ -412,14 +400,14 @@ def rank_program(g, core, T, topo):
             tt(T.XB[:, :], src, T.OK[:, :], A.is_equal, wkeys(t, True) + ["LI", "OK"], ["XB"], 384 * gat)
             for b in range(3):
                 mm(B[PS2][:, 8 * b:8 * b + 8], T.XB[:, 128 * b:128 * b + 128], T.NS[:, :], True, True, ["XB", "NS"], ["#6"], 64)
-            ts(named(0), B[PS2][:, 0:24], 1.0, None, A.min, None, ["#6", "RS"], ["nm0"])
+            ts(named(0), B[PS2][:, 0:24], 1.0, None, A.min, None, ["#6", "RS00"], ["nm0"])
         else:
             act(T.XG[:, :], src, wkeys(t, True) + ["LI"], ["XG"], 384 * gat)
             for b in range(3):
                 mm(B[PS2][:, 8 * b:8 * b + 8], T.XG[:, 128 * b:128 * b + 128], T.TS[:, 8 * t - 8:8 * t], True, True,
                    ["XG", "TS%d" % t], ["#6"], 256)
             tt(T.NE[:, :], B[PS2][:, 0:24], T.OC[:, :], A.is_equal, ["#6", "OC"], ["NE"])
-            tt(named(t), T.NE[:, :], named(t - 1), A.max, ["NE", "nm%d" % (t - 1), "RS"], ["nm%d" % t])
+            tt(named(t), T.NE[:, :], named(t - 1), A.max, ["NE", "nm%d" % (t - 1), "RS%d0" % t], ["nm%d" % t])
 
     def tops0():
         for h in range(2):
@@ -450,7 +438,7 @@ def rank_program(g, core, T, topo):
         if t == 3:
             ma, mb, mc = [m[:, 264 * h:264 * h + n] for m in (T.MA, T.MB, T.MC)]
             ts(ma, d, 1536.0, MAGIC, A.add, A.add, [dk], ["MA%d" % h], n)
-            if h == 0 and PAR["mod_act"]:
+            if h == 0:
                 act(mb, ma, ["MA%d" % h], ["MB%d" % h], n, bias=-MAGIC)
             else:
                 ts(mb, ma, -MAGIC, None, A.add, None, ["MA%d" % h], ["MB%d" % h], n)
@@ -487,10 +475,7 @@ def rank_program(g, core, T, topo):
             for b in range(3):
                 mm(B[PS2][0:64, cs[b]], sel(0, b, 64), ut(p), True, True, ["UT%d" % p, "SM0%d" % b], ["#6"], 128)
             act(T.S1[:, 384 * t:384 * t + 384], B[PS1][:, 0:384], ["#5"], ["S1%d" % t], 384, bias=-K)
-            if PAR["s2v"]:
-                ts(T.S2[0:64, 384 * t:384 * t + 384], B[PS2][0:64, 0:384], 1537.0 - K, None, A.add, None, ["#6"], ["S2%d" % t], 384)
-            else:
-                act(T.S2[0:64, 384 * t:384 * t + 384], B[PS2][0:64, 0:384], ["#6"], ["S2%d" % t], 384, bias=1537.0 - K)
+            ts(T.S2[0:64, 384 * t:384 * t + 384], B[PS2][0:64, 0:384], 1537.0 - K, None, A.add, None, ["#6"], ["S2%d" % t], 384)
             put("s", (t + 1) % 2, t, [0, 1, 2])
         else:
             for b in range(3):

@@ -1,31 +1,34 @@
 from concourse.bass import DstId, RemoteDMATransfer
-from concourse.mybir import AluOpType, ActivationFunctionType
+from concourse.mybir import AluOpType, ActivationFunctionType, AxisListType
 
 N, V, RO = 8, 384, 4
 K = 4096.0
-WW = 3457
-RING = 10
-MAGIC = 1.5 * 2.0 ** 35
-EDGE_ROWS = [0, 2, 4, 6, 12, 14]
-TAIL = [9, 11, 14]
-PAR = {"fused": [3, 0, 3, 0, 3, 0, 1, 0], "gat": 1.56, "cyc": 0.00104, "pe": 0.00052, "dma": 3.0, "slack": 0.12, "arr": 4.0}
+OB, TM, WW = 8, 3080, 3465
+RING = 12
+BIG = 8192.0
+AROWS = [12, 13, 0, 2, 4, 6]
+PLAN = ["v1 v1 a2 v1 a2 a1", "a2 v1 a2 v1 a1", "a2 v1 a2 v1 a2 v1", "a2 v1 a2 v1 a1 v1", "a2 v1 a2 v1 a1 a2 v1", "a2 v1 a2 v1 a2 v1",
+        "a2 v1 a2 v1 a2 a2 v1", "a2 v1 a2 a2 a2 v1"]
+PAR = {"gat": 1.56, "cyc": 0.0009, "fix": 0.04, "pe": 0.00045, "dma": 2.4, "put": 3.6, "slack": 0.12, "arr": 3.5, "arrf": 4.0,
+       "gcopy": 3}
 
 f32, f16, bf16, i32, u16 = "float32", "float16", "bfloat16", "int32", "uint16"
-SCRATCH = {"stage": ("dram", [8, 128, 64], i32), "land": ("dram", [8, 128, 64], i32), "hand": ("dram", [2, 128, 64], i32)}
+SCRATCH = {"stage": ("dram", [8, 128, 64], i32), "land": ("dram", [8, 128, 64], i32), "hand": ("dram", [128, 64], i32),
+           "gst": ("dram", [8, 128, 24], f32), "land2": ("dram", [8, 128, 24], f32), "hand2": ("dram", [128, 24], f32),
+           "land3": ("dram", [8, 128, 3], f32), "hand3": ("dram", [128, 3], f32),
+           "LI": ("sbuf", [128, 2, 264], u16), "L": ("sbuf", [128, 2, 48], i32)}
 for _d, _l in [
-    (f16, "handg 96 SG 192 RG 192 natf 384 natm 384 EG 768 U2 384 C 384 U 384 ID 128 P1 128 P2 128 SO0 128 SY0 256 TC 576 UT 768"),
-    (f32, "OG 256 ownf 768 La 144 Lb 144 MQ2 8 W0 3464 W1 3464 KF 9 KC 32 J 160 CP 128 CPW 128 CG 128 C16 16 CS 128 CQ 128 CV 384 "
-          "CO 24 M16 16 MK 16 MQ 16 GM 8 WT 8 SS 32 TS 24 WF 160 TE 768 M3 4 OK 384 OC 24 SC 528 MA 528 MB 528 MC 528 TN 192 SA 192 "
-          "BS 192 GA 144 GB 144 S1 1152 S2 1152 YS 768 G 3840 XG 384 NE 24"),
-    (bf16, "DUP 128 HL 128 H1 128 H2 128 HI 128 LO 128 BD 128 SWH 1152 SWL 1152 NS 8 WH 160 WD 48 SB 768 SM 2304 SH3 128 R0 384 "
-           "ONE 264 RS 2112 XB 384"),
-    (i32, "own 768 nat 384 L 144 KI 8 KJ 9"), (u16, "LI 144 EL 432")]:
+    (f16, "natf 768 natm 768 D 768 EG 768 TE 768 TC 1512 UT 1024 ID 128 ZF 128 ZM 128 Z1 128 Z2 128"),
+    (f32, "ownf 768 W0 3472 W1 3472 KF 8 KC 40 J 160 CK 128 SL 128 WN 128 CY 128 C16 16 CV 384 M16 16 MK 16 GM 8 SS 32 OK 384 "
+          "SC 528 MC 528 EE 24 S 896 YS 768 G 4608 SG 24 B1 128 B2 128"),
+    (bf16, "BP 128 SW 512 ST 256 SY 384 KID 128 NID 128 WH 160 WD 48 NS 32 ZE 264 RS 2112 XB 1536"),
+    (i32, "own 768 nat 768 LD 48 KI 2 KJ 8 MQ 528"), (u16, "LJ 48")]:
     _w = _l.split()
     for _i in range(0, len(_w), 2):
         SCRATCH[_w[_i]] = ("sbuf", [128, int(_w[_i + 1])], _d)
 for _b in range(8):
-    SCRATCH["B%d" % _b] = ("psum", [128, 512], f32)
-SEMAPHORES = ["cv", "ca", "cp", "cg", "sent", "arr", "arrg", "h0", "h1"] + ["d%d" % _i for _i in range(56)]
+    SCRATCH["B%d" % _b + "p"] = ("psum", [128, 512], f32)
+SEMAPHORES = ["cv", "ca", "cp", "cg", "sent", "arr", "arrf", "arr2", "arr3", "h0", "h1", "h2"] + ["d%d" % _i for _i in range(60)]
 
 A = AluOpType
 IDENT = ActivationFunctionType.Identity
@@ -36,8 +39,7 @@ def routes(T, topo, core):
     direct = [q for q in range(N) if cores[q] != core and topo.may_write(core, cores[q])]
     far = [q for q in range(N) if cores[q] != core and q not in direct]
     able = [c for c in topo.cores_of(core) if c not in cores and all(topo.may_write(c, cores[q]) for q in far)]
-    able.sort(key=lambda c: topo.die(c) == topo.die(core))
-    return direct, [(able[j], far[2 * j:2 * j + 2]) for j in range((len(far) + 1) // 2)]
+    return direct, list(zip(able, far))
 
 
 def bits(es):
@@ -49,46 +51,33 @@ def dst(topo, d, s):
     return DstId(rid=rid, pnc=pid)
 
 
-def span_start(qs):
-    return min(qs[0], N - 4)
-
-
-def helper_program(g, core, T, topo, rank, qs):
-    cores = list(T.cores)
-    es = topo.engines(core, cores[qs[0]])
-    n = len(es) // 2
-    g.wait_ge(T.sem.h0, 2 * len(qs))
-    g.remote_dma_fused([RemoteDMATransfer(dst_ids=[dst(topo, cores[q], core)], dma_engine_mask=bits(es[n * j:n * j + n]),
-                                          remote_sem=T.sem.arr, src=T.hand[j], dst=T.land[rank]) for j, q in enumerate(qs)],
-                       local_sem=T.sem.sent)
-    g.wait_ge(T.sem.h1, 4)
-    s = span_start(qs)
-    g.remote_dma_fused([RemoteDMATransfer(dst_ids=[dst(topo, cores[q], core)], dma_engine_mask=bits(es[n * j:n * j + n]),
-                                          remote_sem=T.sem.arrg, src=T.handg[:, 24 * (q - s):24 * (q - s) + 24],
-                                          dst=T.RG[:, 24 * rank:24 * rank + 24]) for j, q in enumerate(qs)],
-                       local_sem=T.sem.sent)
-    g.wait_ge(T.sem.sent, 2 * n * len(qs))
+def helper_program(g, core, T, topo, rank, q):
+    to = T.cores[q]
+    es = topo.engines(core, to)
+    rid, pid = topo.addr(to, core)
+    for sem, n, out, in_, arr in [(T.sem.h0, 2, T.land, T.hand, T.sem.arrf), (T.sem.h1, 2, T.land2, T.hand2, T.sem.arr2),
+                                  (T.sem.h2, 4, T.land3, T.hand3, T.sem.arr3)]:
+        g.wait_ge(sem, n)
+        g.remote_dma(out[rank], in_[:, :], arr, T.sem.sent, pid, rid, bits(es))
+    g.wait_ge(T.sem.sent, 3 * len(es))
 
 
 def direct_masks(topo, core, cores, direct):
     es = topo.engines(core, cores[direct[0]])
-    cut = [es[0:4], es[4:6], es[6:8]]
-    return [cut[j] for j in range(len(direct))]
+    return [es[0:4], es[4:6], es[6:8]]
 
 
 def arrivals(T, topo, rank):
     cores = list(T.cores)
-    total = 0
+    near = far = 0
     for s in range(N):
-        if s == rank:
-            continue
-        direct, helpers = routes(T, topo, cores[s])
-        if rank in direct:
-            total += len(direct_masks(topo, cores[s], cores, direct)[direct.index(rank)])
-        else:
-            hc = [c for c, qs in helpers if rank in qs][0]
-            total += len(topo.engines(hc, cores[rank])) // 2
-    return total
+        if s != rank:
+            direct, helpers = routes(T, topo, cores[s])
+            if rank in direct:
+                near += len(direct_masks(topo, cores[s], cores, direct)[direct.index(rank)])
+            else:
+                far += len(topo.engines([c for c, q in helpers if q == rank][0], cores[rank]))
+    return near, far
 
 
 def rank_program(g, core, T, topo):
@@ -96,23 +85,24 @@ def rank_program(g, core, T, topo):
     if rank is None:
         for r, c in enumerate(T.cores):
             if c in topo.cores_of(core):
-                for hc, qs in routes(T, topo, c)[1]:
+                for hc, q in routes(T, topo, c)[1]:
                     if hc == core:
-                        helper_program(g, core, T, topo, r, qs)
+                        helper_program(g, core, T, topo, r, q)
         return
     cores = list(T.cores)
     direct, helpers = routes(T, topo, core)
+    waves = [sorted(direct + [rank]), [q for hc, q in helpers]]
     ops = []
     cyc, gat = PAR["cyc"], PAR["gat"]
 
     def op(q, fn, rd, wr, n=64, kind="c", cost=None):
-        ops.append({"q": q, "fn": fn, "rd": rd, "wr": wr, "kind": kind, "cost": 0.05 + max(n, 64) * cyc if cost is None else cost})
+        ops.append({"q": q, "fn": fn, "rd": rd, "wr": wr, "kind": kind, "cost": PAR["fix"] + max(n, 64) * cyc if cost is None else cost})
 
     def raw(q, fn, rd, wr, cost):
         op(q, fn, rd, wr, kind="raw", cost=cost)
 
-    def dma(q, out, in_, rd, wr, cost=None):
-        op(q, lambda e: e.dma_start(out, in_), rd, wr, kind="dma", cost=PAR["dma"] if cost is None else cost)
+    def dma(q, pairs, rd, wr, cost=None):
+        op(q, pairs, rd, wr, kind="dma", cost=PAR["dma"] if cost is None else cost)
 
     def ts(out, in0, s1, s2, o0, o1, rd, wr, n=64):
         if o1 is None:
@@ -132,135 +122,24 @@ def rank_program(g, core, T, topo):
     def act(out, in_, rd, wr, n=64, bias=0.0, scale=1.0):
         op("a", lambda e: e.activation(out, in_, IDENT, bias=bias, scale=scale), rd, wr, n)
 
+    def lin(q, out, in_, rd, wr, n, bias):
+        if q == "a":
+            act(out, in_, rd, wr, n, bias=bias)
+        else:
+            ts(out, in_, bias, None, A.add, None, rd, wr, n)
+
     def iota(out, pat, base, cm, wr, n, flt=True):
         if flt:
             op("g", lambda e: e.iota(out, pat, base, cm, allow_small_or_imprecise_dtypes=True), [], wr, cost=0.13 + 2 * n * cyc)
         else:
             op("g", lambda e: e.iota(out, pat, base, cm), [], wr, cost=0.13 + 2 * n * cyc)
 
-    B = [T["B%d" % b] for b in range(8)]
+    def gcopy(out, in_, rd, wr, n):
+        op("g", lambda e: e.affine_select(out, in_, [[0, n]], A.is_ge, 0.0, 0, 0), rd, wr, cost=0.17 + 2 * n * cyc)
+
+    B = [T["B%dp" % b] for b in range(8)]
     W = [T.W0, T.W1]
-    YB, DB, PU, PS1, PS2, PL = [0, 1], [2, 3], 4, 5, 6, 7
-
-    for i in range(6):
-        dma("sa"[i % 2], T.stage[:, 12 * i:12 * i + 12, :], T.pts[i::16, :], [], ["st%d" % i])
-    dma("s", T.stage[:, 72:84, :], T.ld[:, :], [], ["st6"])
-    dma("a", T.stage[:, 84:96, :], T.cp[:, :], [], ["st7"])
-    dma("s", T.stage[:, 96:102, :], T.xs[:, :], [], ["st8"])
-    dma("a", T.stage[:, 102:108, :], T.ys[:, :], [], ["st9"])
-    dma("s", T.stage[:, 108:120, :], T.pts[6::16, :], [], ["st10"])
-    dma("a", T.stage[:, 120:128, :], T.pts[7::16, 0:512], [], ["st11"])
-    st = ["st%d" % i for i in range(12)]
-    iota(T.KI[:, :], [[1, 8]], 0, 1, ["KI"], 8, False)
-    iota(T.C16[:, :], [[1, 16]], 0, 0, ["C16"], 16)
-    iota(T.CP[:, :], [[0, 8], [1, 8], [0, 2]], 0, 0, ["CP"], 128)
-    iota(T.CPW[:, :], [[0, 8], [1, 8], [100, 2]], -100, 0, ["CPW"], 128)
-    iota(T.J[:, :], [[1, 160]], 0, -1, ["J"], 160)
-    iota(T.CG[:, :], [[1, 8], [0, 16]], 0, 0, ["CG"], 128)
-    dm = direct_masks(topo, core, cores, direct)
-    inner = [e for e in topo.engines(core, helpers[0][0]) if e not in topo.engines(core, cores[direct[0]])]
-    tr = []
-    for j, (hc, qs) in enumerate(helpers):
-        for i, q in enumerate(qs):
-            tr.append(RemoteDMATransfer(dst_ids=[dst(topo, hc, core)], dma_engine_mask=bits(inner[4 * j + 2 * i:4 * j + 2 * i + 2]),
-                                        remote_sem=T.sem.h0, src=T.stage[q], dst=T.hand[i]))
-    for j, q in enumerate(direct):
-        tr.append(RemoteDMATransfer(dst_ids=[dst(topo, cores[q], core)], dma_engine_mask=bits(dm[j]),
-                                    remote_sem=T.sem.arr, src=T.stage[q], dst=T.land[rank]))
-    sent = [sum(2 * len(qs) for hc, qs in helpers) + sum(len(m) for m in dm)]
-    raw("g", lambda e: e.remote_dma_fused(tr, local_sem=T.sem.sent), st, ["away"], 1.0)
-    dma("s", T.land[rank], T.stage[rank], st, ["landown"])
-    dma("s", T.own[:, :], T.pts[:, :], [], ["own"])
-    iota(T.CS[:, :], [[1, 2], [12, 8], [2, 8]], 0, -1, ["CS"], 128)
-    iota(T.CQ[:, :], [[100, 2], [0, 8], [1, 8]], 0, 0, ["CQ"], 128)
-    iota(T.CO[:, :], [[128, 3], [384, 8]], -1536, 1, ["CO"], 24)
-    iota(T.CV[:, :], [[1, 384]], 0, 0, ["CV"], 384)
-    iota(T.SB[:, 384:768], [[0, 384]], 0, 0, ["SB3", "SB4", "SB5"], 384)
-    iota(T.ONE[:, :], [[0, 264]], 1, 0, ["ONE"], 264)
-    for p in range(8):
-        n = 8 + p // 2 - p % 2
-        op("g", lambda e, p=p, n=n: e.affine_select(T.RS[:, 264 * p:264 * p + 24 * n], T.ONE[:, 0:24 * n], [[0, 24], [1, n]], A.is_gt, 0.0, 0, 0),
-           ["ONE"], ["RS%d%d" % (p // 2, p % 2)], cost=0.17 + 48 * n * cyc)
-    narr = arrivals(T, topo, rank)
-    raw("s", lambda e: e.wait_ge(T.sem.arr, narr), ["away"], [], PAR["arr"])
-    dma("s", T.nat[0:96, :], T.land[:, 0:72, :], ["landown"], ["nat"])
-    dma("s", T.L[:, 0:48], T.land[:, 72:84, :], ["landown"], ["L0"])
-    dma("s", T.L[:, 48:96], T.land[:, 84:96, :], ["landown"], ["L1"])
-    dma("s", T.L[:, 96:120], T.land[:, 96:102, :], ["landown"], ["L2"])
-    dma("s", T.L[:, 120:144], T.land[:, 102:108, :], ["landown"], ["L3"])
-
-    for j, (c, s, o) in enumerate([(0, 15, A.bitwise_and), (0, 4, A.arith_shift_right), (0, 3, A.arith_shift_right),
-                                   (0, 7, A.bitwise_and), (0, 3, A.bitwise_and), (0, 0, None),
-                                   (6, 7, A.bitwise_and), (5, 7, A.bitwise_and), (0, 5, A.arith_shift_right)]):
-        if o is None:
-            ts(T.KJ[:, j:j + 1], T.KI[:, 0:1], 31, 2, A.bitwise_and, A.arith_shift_right, ["KI"], ["KJ%d" % j])
-        else:
-            ts(T.KJ[:, j:j + 1], T.KI[:, c:c + 1], s, None, o, None, ["KI"], ["KJ%d" % j])
-    op("v", lambda e: e.tensor_copy(T.KF[:, :], T.KJ[:, :]), ["KJ%d" % j for j in range(9)], ["KF"])
-    kr, kg, k3, ki, kd, kq, key, keyp, k5 = [T.KF[:, j:j + 1] for j in range(9)]
-    col = [T.KC[:, j:j + 1] for j in range(32)]
-    ts(T.M16[:, :], T.C16[:, :], kr, None, A.is_equal, None, ["C16", "KF"], ["M16"])
-    ts(T.MQ[:, :], T.C16[:, :], k3, None, A.is_equal, None, ["C16", "KF"], ["MQ"])
-    ts(T.GM[:, :], T.C16[:, 0:8], kg, None, A.is_equal, None, ["C16", "KF"], ["GM"])
-    ts(T.M3[:, :], T.C16[:, 0:4], k5, None, A.is_equal, None, ["C16", "KF"], ["M3"])
-    ts(col[23], ki, 6.0, K, A.is_lt, A.mult, ["KF"], ["c23"])
-    ts(col[24], ki, 6.0, -1.0, A.is_lt, A.mult, ["KF"], ["c24"])
-    ts(col[9], keyp, 3.0, None, A.is_lt, None, ["KF"], ["c9"])
-    ts(col[0], keyp, 6.0, col[9], A.is_ge, A.max, ["KF", "c9"], ["c0"])
-    ts(col[4], k3, -8.0, None, A.add, None, ["KF"], ["c4"])
-    ts(T.H1[:, :], T.CP[:, :], key, col[23], A.is_equal, A.mult, ["CP", "KF", "c23"], ["H1"], 128)
-    ts(T.H2[:, :], T.CPW[:, :], keyp, col[0], A.is_equal, A.mult, ["CPW", "KF", "c0"], ["H2"], 128)
-    ts(T.LO[:, :], T.CPW[:, :], key, col[24], A.is_equal, A.mult, ["CPW", "KF", "c24"], ["LO"], 128)
-    tt(T.HI[:, :], T.H1[:, :], T.H2[:, :], A.add, ["H1", "H2"], ["HI"], 256)
-    ts(T.BD[:, :], T.CG[:, :], col[4], None, A.is_equal, None, ["CG", "c4"], ["BD"], 128)
-    ts(col[2], kd, 0.0, None, A.is_equal, None, ["KF"], ["c2"])
-    ts(col[3], kd, 0.0, K, A.is_equal, A.mult, ["KF"], ["c3"])
-    ts(col[19], kd, 1.0, None, A.is_equal, None, ["KF"], ["c19"])
-    tt(col[1], col[3], col[19], A.subtract, ["c3", "c19"], ["c1"])
-    ts(col[5], ki, 7.0, K, A.is_equal, A.mult, ["KF"], ["c5"])
-    ts(col[6], ki, 6.0, K, A.is_equal, A.mult, ["KF"], ["c6"])
-    ts(col[7], ki, 7.0, None, A.is_equal, None, ["KF"], ["c7"])
-    tt(col[8], col[6], col[7], A.subtract, ["c6", "c7"], ["c8"])
-    act(col[10], T.M16[:, 7:8], ["M16"], ["c10"], bias=-K, scale=1537.0)
-    act(col[11], kg, ["KF"], ["c11"], bias=-1536.0 * K, scale=384.0 * K)
-    for t in range(3):
-        act(col[25 + t], T.M16[:, TAIL[t]:TAIL[t] + 1], ["M16"], ["c%d" % (25 + t)], bias=-K, scale=1537.0)
-    ts(col[20], kd, 3.0, col[19], A.is_equal, A.add, ["KF", "c19"], ["c20"])
-    act(col[12], col[20], ["c20"], ["c12"], bias=1.0, scale=-2.0)
-    ts(col[13], kr, 12.0, None, A.is_ge, None, ["KF"], ["c13"])
-    ts(col[15], T.M16[:, 14:15], -2.0, col[12], A.mult, A.add, ["M16", "c12"], ["c15"])
-    act(T.WT[:, 0:4], T.C16[:, 0:4], ["C16"], ["WT0"], bias=8.0, scale=2.0)
-    ts(T.WT[:, 4:8], T.WT[:, 0:4], kr, col[13], A.is_gt, A.max, ["WT0", "KF", "c13"], ["WT1"])
-    for t in range(3):
-        act(col[16 + t], T.WT[:, 4 + t:5 + t], ["WT1", "c12"], ["c%d" % (16 + t)], scale=col[12])
-    tt(T.MQ2[:, :], T.MQ[:, 0:8], T.MQ[:, 8:16], A.add, ["MQ"], ["MQ2"])
-    act(T.HL[0:64, :], T.HI[0:64, :], ["HI"], ["+HL"], 128)
-    act(T.HL[64:128, :], T.LO[64:128, :], ["LO"], ["+HL"], 128)
-    for q in range(2, 8):
-        act(T.SWH[:, 128 * q:128 * q + 128], T.HL[:, :], ["HL", "MQ2"], ["SWH%d" % q], 128, scale=T.MQ2[:, q:q + 1])
-    for q in range(2):
-        act(T.SWL[:, 128 * q:128 * q + 128], T.LO[:, :], ["LO", "MQ"], ["SWL%d" % q], 128, scale=T.MQ[:, q:q + 1])
-        act(T.SWH[:, 128 * q:128 * q + 128], T.HI[:, :], ["HI", "MQ"], ["SWH%d" % q], 128, scale=T.MQ[:, q:q + 1])
-    tt(T.SWL[:, 1024:1152], T.LO[:, :], T.BD[:, :], A.mult, ["LO", "BD"], ["SWL8"], 256)
-    tt(T.SWH[:, 1024:1152], T.HI[:, :], T.BD[:, :], A.mult, ["HI", "BD"], ["SWH8"], 256)
-    ts(T.ID[:, :], T.J[:, 0:128], 0.0, None, A.is_equal, None, ["J"], ["ID"], 128)
-    ts(T.WF[:, :], T.J[:, :], 15.0, None, A.is_equal, None, ["J"], ["WF"], 160)
-    act(T.WH[:, :], T.WF[:, :], ["WF"], ["WH"], 160)
-    for j in range(2):
-        act(T.DUP[:, 64 * j:64 * j + 64], T.WF[:, 15:79], ["WF"], ["+DUP"])
-    act(T.MK[:, :], T.M16[:, :], ["M16"], ["MK"], scale=1.0 / K)
-    for j, r in enumerate(EDGE_ROWS):
-        act(T.WD[:, 8 * j:8 * j + 8], T.GM[:, :], ["GM", "M16"], ["+WD"], scale=T.M16[:, r:r + 1])
-    ms(T.R0[:, :], 4000.0, ["R0"], 192)
-    ms(T.R0[:, 0::8], -1536.0, ["R0"])
-    ts(T.CS[:, 6::8], T.CS[:, 6::8], -2.0, None, A.add, None, ["CS"], ["CS"])
-    ts(T.CS[:, 7::8], T.CS[:, 7::8], -4.0, None, A.add, None, ["CS"], ["CS"])
-    ts(T.P1[:, :], T.CS[:, :], 0.0, None, A.is_equal, None, ["CS"], ["P1"], 128)
-    ts(T.P2[:, :], T.CS[:, :], 0.0, -3584.0, A.is_equal, A.mult, ["CS"], ["P2"], 128)
-    ts(T.SY0[:, 0:128], T.CG[:, :], k3, col[5], A.is_equal, A.mult, ["CG", "KF", "c5"], ["SY00"], 128)
-    ts(T.SY0[:, 128:256], T.CG[:, :], col[4], col[5], A.is_equal, A.mult, ["CG", "c4", "c5"], ["SY01"], 128)
-    ts(T.SO0[:, :], T.CQ[:, :], k3, col[8], A.is_equal, A.mult, ["CQ", "KF", "c8"], ["SO0"], 128)
-    ms(T.W0[:, 384:385], -1537.0 * K, ["W0o"])
+    YB, DB, PS, PU, PL, PX = [0, 1], [2, 3], 4, 5, 6, 7
 
     def nsrc(t, h):
         return 8 + t - h
@@ -269,166 +148,275 @@ def rank_program(g, core, T, topo):
         o = 264 * (2 * t + h)
         return T.RS[:, o:o + 24 * nsrc(t, h)]
 
-    def named(t):
-        o = 264 * 2 * t
-        return T.RS[:, o + 1:o + 24 * nsrc(t, 0):nsrc(t, 0)]
+    dma("s", [(T.stage[:, 12 * i:12 * i + 12, :], T.pts[i::16, :]) for i in (0, 2, 4)] +
+        [(T.stage[:, 72:84, :], T.ld[:, :]), (T.stage[:, 96:102, :], T.xs[:, :]), (T.stage[:, 108:120, :], T.pts[6::16, :])], [], ["st0"])
+    dma("a", [(T.stage[:, 12 * i:12 * i + 12, :], T.pts[i::16, :]) for i in (1, 3, 5)] +
+        [(T.stage[:, 84:96, :], T.cp[:, :]), (T.stage[:, 102:108, :], T.ys[:, :]), (T.stage[:, 120:128, :], T.pts[7::16, 0:512])], [], ["st1"])
+    st = ["st0", "st1"]
+    iota(T.KI[:, 0:1], [[1, 1]], 0, 1, ["KI"], 1, False)
+    iota(T.C16[:, :], [[1, 16]], 0, 0, ["C16"], 16)
+    iota(T.CK[:, :], [[2, 64], [0, 2]], 0, 0, ["CK"], 128)
+    iota(T.SL[:, :], [[0, 8], [1, 8], [0, 2]], 2, 0, ["SL"], 128)
+    iota(T.WN[:, :], [[0, 8], [1, 8], [100, 2]], -97, 0, ["WN"], 128)
+    iota(T.J[:, :], [[1, 160]], 0, -1, ["J"], 160)
+    dm = direct_masks(topo, core, cores, direct)
+    every = topo.engines(core, helpers[0][0])
+    inner = [e for e in every if e not in topo.engines(core, cores[direct[0]])]
 
-    ts(T.natf[0:96, :], T.nat[0:96, :], -1535.0, None, A.add, None, ["nat"], ["natf"], 384)
-    ts(T.natm[0:96, :], T.nat[0:96, :], 3071.5, None, A.is_gt, None, ["nat"], ["natm"], 384)
-    for b in range(3):
-        mm(B[PU][:, 128 * b:128 * b + 128], T.natf[0:96, 128 * b:128 * b + 128], T.P1[0:96, :], True, False, ["natf", "P1"], ["#4"], 128)
-        mm(B[PU][:, 128 * b:128 * b + 128], T.natm[0:96, 128 * b:128 * b + 128], T.P2[0:96, :], False, True, ["natm", "P2"], ["#4"], 128)
-    op("v", lambda e: e.tensor_tensor_scan(T.C[:, :], T.R0[:, :], B[PU][:, 0:384], -1536.0, A.min, A.max), ["R0", "#4"], ["C"], 384)
-    for b in range(3):
-        mm(B[PL][:, 128 * b:128 * b + 128], T.C[:, 128 * b:128 * b + 128], T.ID[:, :], True, True, ["C", "ID"], ["#7"], 128)
-    op("v", lambda e: e.tensor_copy(T.U[:, :], B[PL][:, 0:384]), ["#7"], ["U"], 384)
-    for b in range(3):
-        mm(B[1][:, 128 * b:128 * b + 128], T.DUP[0:64, :], T.U[0:64, 128 * b:128 * b + 128], True, True, ["U", "DUP"], ["#1"], 128)
-    op("v", lambda e: e.tensor_copy(T.U2[:, :], B[1][:, 0:384]), ["#1"], ["U2"], 384)
-    ts(T.La[:, :], T.L[:, :], 3071.5, 3457.0, A.is_lt, A.mult, ["L0", "L1", "L2", "L3"], ["La"], 144)
-    tt(T.Lb[:, :], T.L[:, :], T.La[:, :], A.add, ["La"], ["Lb"], 288)
-    ts(T.LI[:, :], T.Lb[:, :], -3072.0, None, A.add, None, ["Lb"], ["LI"], 144)
-    banks = [2, 3, 5, 6, 4, 0, 1]
-    for j, q in enumerate([8, 0, 1, 2, 3, 4, 5, 6, 7]):
-        b = banks[j % 7]
-        if j < 3:
-            mm(B[b][:, 0:384], T.SWH[:, 128 * q:128 * q + 128], T.U[:, :], True, False, ["U", "SWH%d" % q], ["#%d" % b], 384)
-            mm(B[b][:, 0:384], T.SWL[:, 128 * q:128 * q + 128], T.U[:, :], False, True, ["U", "SWL%d" % q], ["#%d" % b], 384)
-        else:
-            mm(B[b][:, 0:384], T.SWH[:, 128 * q:128 * q + 128], T.U2[:, :], True, True, ["U2", "SWH%d" % q], ["#%d" % b], 384)
-        c0 = 385 + 384 * q if q < 8 else 0
-        if j in (0, 1, 3, 5, 7):
-            act(T.W0[:, c0:c0 + 384], B[b][:, 0:384], ["#%d" % b, "c10"], ["W0p%d" % q], 384, bias=col[10])
-        else:
-            ts(T.W0[:, c0:c0 + 384], B[b][:, 0:384], col[10], None, A.add, None, ["#%d" % b, "c10"], ["W0p%d" % q], 384)
-    first = ["W0p%d" % q for q in range(9)]
-    for h in range(2):
-        mm(B[YB[h]][:, 0:384], T.SY0[:, 128 * h:128 * h + 128], T.U[:, :], True, True, ["U", "SY0%d" % h], ["#%d" % YB[h]], 384)
-    dma("s", T.W1[:, 384:WW], T.W0[:, 384:WW], first[:8] + ["W0o"], ["W1o"], 8.0)
+    def alltoall(src, hand, hsem, land, sem):
+        tr = [RemoteDMATransfer(dst_ids=[dst(topo, hc, core)], dma_engine_mask=bits(inner[2 * j:2 * j + 2]), remote_sem=hsem,
+                                src=src[q], dst=hand[:, :]) for j, (hc, q) in enumerate(helpers)]
+        return tr + [RemoteDMATransfer(dst_ids=[dst(topo, cores[q], core)], dma_engine_mask=bits(dm[j]), remote_sem=sem,
+                                       src=src[q], dst=land[rank]) for j, q in enumerate(direct)]
+    tr0 = alltoall(T.stage, T.hand, T.sem.h0, T.land, T.sem.arr)
+    raw("g", lambda e: e.remote_dma_fused(tr0, local_sem=T.sem.sent), st, ["away"], 3.0)
+    dma("s", [(T.land[rank], T.stage[rank])], st, ["landown"])
+    iota(T.CY[0:32, :], [[3, 8], [0, 16]], 0, -1, ["CY"], 128)
+    iota(T.CV[:, :], [[4096, 384]], -1536 * 4096, 0, ["CV"], 384)
+    raw("g", lambda e: e.wait_ge(T.sem.sent, len(every)), ["away"], [], 0.5)
+    dma("g", [(T.own[:, :], T.pts[:, :])], [], ["own"], 4.0)
+    ms(T.nat[0:64, :], 0, ["nat0", "nat1"], 768)
+    ms(T.ZE[:, :], 0.0, ["ZE"], 132)
+    for p in range(8):
+        n = nsrc(p // 2, p % 2)
+        op("g", lambda e, p=p, n=n: e.affine_select(reset(p // 2, p % 2), T.ZE[:, 0:24 * n], [[0, 24], [1, n]], A.is_gt, BIG, 0, 0),
+           ["ZE"], ["RS%d" % p], cost=0.17 + 48 * n * cyc)
+    near, far = arrivals(T, topo, rank)
 
-    for t in range(4):
-        c = 16 + t if t < 3 else 15
-        act(T.SS[:, 8 * t:8 * t + 8], T.GM[:, :], ["GM", "c%d" % c], ["SS%d" % t], scale=col[c])
-    for t in range(1, 4):
-        act(T.TS[:, 8 * t - 8:8 * t], T.GM[:, :], ["GM", "M16"], ["TS%d" % t], scale=T.M16[:, 6 + 2 * t:7 + 2 * t])
-    ts(T.NS[:, :], T.SS[:, 0:8], 0.0, None, A.max, None, ["SS0"], ["NS"])
-    ts(T.SB[:, 0:128], T.CQ[:, :], kq, col[1], A.is_equal, A.mult, ["CQ", "KF", "c1"], ["SB0"], 128)
-    ts(T.SB[:, 128:192], T.CQ[:, 0:64], kq, col[2], A.is_equal, A.mult, ["CQ", "KF", "c2"], ["+SB1"])
-    ts(T.SB[:, 192:256], T.CQ[:, 0:64], kq, col[3], A.is_equal, A.mult, ["CQ", "KF", "c3"], ["+SB1"])
-    ts(T.SB[:, 256:384], T.CG[:, :], kq, col[3], A.is_equal, A.mult, ["CG", "KF", "c3"], ["SB2"], 128)
+    for j, (s, s2, o, o2) in enumerate([(15, None, A.bitwise_and, None), (4, None, A.arith_shift_right, None), (1, None, A.bitwise_and, None),
+                                        (14, None, A.bitwise_and, None), (1, 7, A.arith_shift_right, A.bitwise_and),
+                                        (1, 1, A.arith_shift_right, A.bitwise_and), (0, None, A.arith_shift_right, None)]):
+        ts(T.KJ[:, j:j + 1], T.KI[:, 0:1], s, s2, o, o2, ["KI"], ["KJ%d" % j])
+    op("v", lambda e: e.tensor_copy(T.KF[:, 0:7], T.KJ[:, 0:7]), ["KJ%d" % j for j in range(7)], ["KF"])
+    kr, kg, k1, k14, kj, k2, kp = [T.KF[:, j:j + 1] for j in range(7)]
+    col = [T.KC[:, j:j + 1] for j in range(40)]
+    ts(col[0], kg, 32.0, k14, A.mult, A.add, ["KF"], ["c0"])
+    ts(col[1], k1, 16.0, col[0], A.mult, A.add, ["KF", "c0"], ["c1"])
+    ts(col[2], col[1], 2.0, None, A.add, None, ["c1"], ["c2"])
+    ts(col[3], k14, 12.0, None, A.is_lt, None, ["KF"], ["c3"])
+    ts(T.Z1[:, :], T.CK[:, :], col[1], col[3], A.is_equal, A.mult, ["CK", "c1", "c3"], ["Z1"], 128)
+    ts(T.Z2[:, :], T.CK[:, :], col[2], col[3], A.is_equal, A.mult, ["CK", "c2", "c3"], ["Z2"], 128)
+    tt(T.ZF[:, :], T.Z1[:, :], T.Z2[:, :], A.subtract, ["Z1", "Z2"], ["ZF"], 256)
+    act(T.ZM[0:64, :], T.ZF[0:64, :], ["ZF"], ["ZMa"], 128, scale=-K)
+    ms(T.ZM[64:96, :], 0.0, ["ZM"])
+    ms(T.ZM[64:65, 1::2], -2048.0, ["ZM"])
+    ms(T.ZM[64:65, 0::16], 1537.0, ["ZM"])
+    ms(T.ZM[64:65, 1::16], -511.0, ["ZM"])
+    ms(T.natm[64:96, :], 1.0, ["ones"], 384)
+    ts(T.M16[:, :], T.C16[:, :], kr, None, A.is_equal, None, ["C16", "KF"], ["M16"])
+    ts(T.GM[:, :], T.C16[:, 0:8], kg, None, A.is_equal, None, ["C16", "KF"], ["GM"])
+    for r, c in [(12, 0.0), (14, 0.0), (13, 1.0), (15, 1.0)]:
+        ms(T.SL[:, r::16], c, ["SL"])
+    for r, c in [(7, -100.0), (14, 1.0), (15, 2.0)]:
+        ms(T.WN[:, r::16], c, ["WN"])
+    ts(T.B1[:, :], T.SL[:, :], kj, K, A.is_ge, A.mult, ["SL", "KF"], ["B1"], 128)
+    ts(T.B2[:, :], T.WN[:, :], kj, None, A.is_equal, None, ["WN", "KF"], ["B2"], 128)
+    tt(T.BP[:, :], T.B1[:, :], T.B2[:, :], A.add, ["B1", "B2"], ["BP"], 256)
+    for k in range(4):
+        act(T.SW[:, 128 * k:128 * k + 128], T.BP[:, :], ["BP", "GM"], ["SW%d" % k], 128, scale=T.GM[:, 2 * k:2 * k + 1])
+    ms(T.ST[:, :], 0.0, ["ST"], 128)
+    for w in range(2):
+        for k, q in enumerate(waves[w]):
+            act(T.ST[:, 128 * w + 16 * q:128 * w + 16 * q + 16], T.BP[:, 0:16], ["BP", "GM", "ST"], ["ST%d" % q],
+                scale=T.GM[:, 2 * k + 1:2 * k + 2])
+    act(col[4], T.M16[:, 7:8], ["M16"], ["c4"], bias=-1537.0 * K, scale=K)
+    for w in range(2):
+        ms(W[w][:, 0:OB], -1537.0 * K, ["W%de" % w])
+        ms(W[w][:, WW - 1:WW + 7], -1537.0 * K, ["W%df" % w])
+    ts(T.ID[:, :], T.J[:, 0:128], 0.0, None, A.is_equal, None, ["J"], ["ID"], 128)
+    ts(T.WH[:, :], T.J[:, :], 15.0, None, A.is_equal, None, ["J"], ["WH"], 160)
+    act(T.KID[:, :], T.ID[:, :], ["ID"], ["KID"], 128, scale=K)
+    act(T.NID[:, :], T.ID[:, :], ["ID"], ["NID"], 128, scale=-1.0)
+    act(T.MK[:, :], T.M16[:, :], ["M16"], ["MK"], scale=1.0 / K)
+    for j, r in enumerate(AROWS):
+        act(T.WD[:, 8 * j:8 * j + 8], T.GM[:, :], ["GM", "M16"], ["+WD"], scale=T.M16[:, r:r + 1])
+    for b in range(3):
+        ts(T.SY[0:32, 128 * b:128 * b + 128], T.CY[0:32, :], -float(b), K, A.is_equal, A.mult, ["CY"], ["+SY"], 128)
+    ms(T.TC[:, :], 0.0, ["TCz"], 756)
+    ts(col[5], kr, 12.0, None, A.is_ge, None, ["KF"], ["c5"])
+    tt(col[6], k2, k1, A.subtract, ["KF"], ["c6"])
+    ts(col[7], col[6], col[5], k1, A.mult, A.add, ["c5", "c6", "KF"], ["c7"])
+    act(col[8], col[7], ["c7"], ["c8"], bias=1.0, scale=-2.0)
     for t in range(3):
-        for r, c in zip([7 + 2 * t, 8 + 2 * t, TAIL[t]], [2, 3, 1]):
-            ts(T.SB[:, 384 + 128 * t + r:512 + 128 * t:16], T.C16[:, 0:8], kq, col[c], A.is_equal, A.mult, ["C16", "KF", "c%d" % c],
-               ["+SB%d" % (3 + t)])
-    for j in range(6):
-        for b in range(3):
-            act(T.SM[:, 384 * j + 128 * b:384 * j + 128 * b + 128], T.SB[:, 128 * j:128 * j + 128], ["SB%d" % j, "M3"],
-                ["SM%d%d" % (j, b)], 128, scale=T.M3[:, b:b + 1])
-    act(T.SH3[:, :], T.SWH[:, 1024:1152], ["SWH8"], ["SH3"], 128)
-    ms(T.SH3[:, 12::16], 0.0, ["+SH3"])
-    ms(T.SH3[:, 14::16], 0.0, ["+SH3"])
-    act(T.OK[:, :], T.CV[:, :], ["CV", "c11"], ["OK"], 384, bias=col[11], scale=K)
-    act(T.OC[:, :], T.CO[:, :], ["CO"], ["OC"], scale=K)
-    for j in range(2):
-        ts(T.TC[:, 288 * j:288 * j + 288], T.R0[:, 0:288], 0.0, None, A.mult, None, ["R0"], ["TCz%d" % j], 144)
-    op("v", lambda e: e.tensor_copy(T.ownf[:, :], T.own[:, :]), ["own"], ["ownf"], 768)
+        ts(col[9 + t], kr, 8.0 + 2 * t, col[5], A.is_lt, A.max, ["KF", "c5"], ["c%d" % (9 + t)])
+        ts(col[12 + t], col[9 + t], col[8], T.MK[:, 6 + 2 * t:7 + 2 * t], A.mult, A.add, ["c%d" % (9 + t), "c8", "MK"], ["c%d" % (12 + t)])
+    ts(col[16], T.M16[:, 13:14], -2.0, col[8], A.mult, A.add, ["M16", "c8"], ["c16"])
+    act(col[15], col[16], ["c16"], ["c15"], scale=1.0 / K)
+    for t in range(4):
+        act(T.SS[:, 8 * t:8 * t + 8], T.GM[:, :], ["GM", "c%d" % (12 + t)], ["SS%d" % t], scale=col[12 + t])
+    ts(T.NS[:, 0:8], T.SS[:, 0:8], 0.0, None, A.max, None, ["SS0"], ["NS0"])
+    for t in range(1, 4):
+        act(T.NS[:, 8 * t:8 * t + 8], T.GM[:, :], ["GM", "M16"], ["NS%d" % t], scale=T.M16[:, 6 + 2 * t:7 + 2 * t])
+    act(col[17], kg, ["KF"], ["c17"], scale=384.0 * K)
+    act(T.OK[:, :], T.CV[:, :], ["CV", "c17"], ["OK"], 384, bias=col[17])
+    ts(col[18], kp, 72.0, K + 1536.0, A.is_ge, A.mult, ["KF"], ["c18"])
+    ts(col[19], kp, 48.0, None, A.is_ge, None, ["KF"], ["c19"])
+    ts(col[20], kp, 72.0, col[19], A.is_lt, A.mult, ["KF", "c19"], ["c20"])
+    ts(col[21], col[18], -K, None, A.add, None, ["c18"], ["c21"])
+    ts(col[22], col[20], K, col[21], A.mult, A.add, ["c20", "c21"], ["c22"])
+    ts(col[23], col[20], 1921.0, col[21], A.mult, A.add, ["c20", "c21"], ["c23"])
+
+    def tc(s, kind=None):
+        o = 72 + 96 * s
+        return T.TC[:, o:o + 24] if kind is None else T.TC[:, o - 24 * kind:o - 24 * kind + 96]
+
+    def block(w, q, k, b, eng):
+        c0 = OB + V * q
+        mm(B[b][:, 0:V], T.SW[:, 128 * k:128 * k + 128], T.D[:, V * w:V * w + V], True, True, ["D%d" % w, "SW%d" % k], ["#%d" % b], V)
+        lin(eng, T.W0[:, c0:c0 + V], B[b][:, 0:V], ["#%d" % b, "c4"], ["W0p%d" % q], V, col[4])
+
+    def copy1(q, n):
+        c0 = OB + V * q
+        if n < PAR["gcopy"]:
+            gcopy(T.W1[:, c0:c0 + V], T.W0[:, c0:c0 + V], ["W0p%d" % q], ["W1p%d" % q], V)
+        else:
+            dma("s", [(T.W1[:, c0:c0 + V], T.W0[:, c0:c0 + V])], ["W0p%d" % q], ["W1p%d" % q], 3.0)
+
+    def tops(w):
+        for k, q in enumerate(waves[w]):
+            for b in range(3):
+                mm(B[PU][:, 3 * q + b:3 * q + b + 1], T.D[:, V * w + 128 * b:V * w + 128 * b + 128], T.SW[:, 128 * k + 6:128 * k + 7],
+                   True, True, ["D%d" % w, "SW%d" % k], ["#%d" % PU], 64)
+
+    def wave(w):
+        cs = slice(V * w, V * w + V)
+        dma("s", [(T.nat[16 * k:16 * k + 12, cs], T.land[q, 0:72, :]) for k, q in enumerate(waves[w])], ["landown"], ["nat%d" % w], 2.2)
+        act(T.natf[0:64, cs], T.nat[0:64, cs], ["nat%d" % w], ["natf%d" % w], V, bias=-1536.0)
+        ts(T.natm[0:64, cs], T.nat[0:64, cs], 3071.5, None, A.is_gt, None, ["nat%d" % w], ["natm%d" % w], V)
+        mm(B[PS][:, 0:V], T.ZF[0:64, :], T.natf[0:64, cs], True, False, ["natf%d" % w, "ZF"], ["#%d" % PS], V)
+        mm(B[PS][:, 0:V], T.ZM[0:96, :], T.natm[0:96, cs], False, True, ["natm%d" % w, "ZM", "ZMa", "ones"], ["#%d" % PS], V)
+        ts(T.D[:, cs], B[PS][:, 0:V], 0.0, 2048.0, A.max, A.min, ["#%d" % PS], ["D%d" % w], V)
+
+    raw("s", lambda e: e.wait_ge(T.sem.arr, near), ["away"], [], PAR["arr"])
+    wave(0)
+    for k, q in enumerate(waves[0]):
+        block(0, q, k, [2, 3, 6, 7][k], "av"[k % 2])
+        copy1(q, 0)
+    tops(0)
+    act(T.ownf[:, :], T.own[:, :], ["own"], ["ownf"], 768)
+    raw("s", lambda e: e.wait_ge(T.sem.arrf, far), ["away"], [], PAR["arrf"])
+    wave(1)
+    dma("s", [(T.LD[:, :], T.land[:, 72:84, :]), (T.L[:, :, 24:48], T.land[:, 84:96, :]), (T.L[:, 1, 0:24], T.land[:, 96:102, :]),
+              (T.L[:, 0, 0:24], T.land[:, 102:108, :])], ["landown"], ["L"], 2.4)
+    for k, q in enumerate(waves[1]):
+        block(1, q, k, [2, 3, 6, 7][k], "av"[k % 2])
+    for w in range(2):
+        mm(B[1][:, 0:V], T.ST[:, 128 * w:128 * w + 128], T.D[:, V * w:V * w + V], w == 0, w == 1,
+           ["D%d" % w] + ["ST%d" % q for q in waves[w]], ["#1"], V)
+    lin("a", T.W0[:, TM:TM + V], B[1][:, 0:V], ["#1", "c4"], ["W0p8"], V, col[4])
+    ts(T.LJ[:, :], T.LD[:, :], float(OB), None, A.add, None, ["L"], ["LJ"])
+    ts(T.LI[:, :, 0:48], T.L[:, :, :], float(OB), None, A.add, None, ["L"], ["LI"], 96)
+    tops(1)
+    for b in range(3):
+        for w in range(2):
+            mm(B[PU][:, 24 + b:48:3], T.D[:, V * w + 128 * b:V * w + 128 * b + 128], T.ST[:, 128 * w + 6:128 * w + 128:16], w == 0, w == 1,
+               ["D%d" % w] + ["ST%d" % q for q in waves[w]], ["#%d" % PU], 64)
+    for h in range(2):
+        ts(tc(h), B[PU][:, 24 * h:24 * h + 24], 1.0 / K, -1536.0, A.mult, A.add, ["#%d" % PU, "TCz"], ["TC%d" % h])
+    for n, q in enumerate(waves[1] + [8]):
+        copy1(q, n)
 
     def wkeys(t, full):
         w = "W%d" % (t % 2)
-        return (first if t == 0 else []) + [w + "o"] + ([w + "t"] if full else [])
+        return [w + "p%d" % q for q in range(9 if full else 8)] + [w + "e", w + "o"] + ([w + "f", w + "t"] if full else [])
 
     def window(t, full):
-        return W[t % 2][:, 0:WW] if full else W[t % 2][:, 384:WW]
+        return W[t % 2][:, 0:WW] if full else W[t % 2][:, 0:TM]
 
-    def ycopy(t, h):
-        if PAR["fused"][2 * t + h]:
-            act(T.YS[:, 384 * h:384 * h + 384], B[YB[h]][:, 0:384], ["#%d" % YB[h]], ["YS%d" % h], 384)
+    def thresholds(p):
+        h = p % 2
+        u = T.UT[0:24, 128 * p:128 * p + 128]
+        mm(B[PU][0:24, 0:128], tc(p), T.ID[:, :], True, True, ["TC%d" % p, "ID"], ["#%d" % PU], 128)
+        act(u, B[PU][0:24, 0:128], ["#%d" % PU], ["UT%d" % p], 128)
+        for b in range(3):
+            mm(B[YB[h]][:, 128 * b:128 * b + 128], T.SY[0:24, 128 * b:128 * b + 128], u, True, True, ["UT%d" % p, "SY"], ["#%d" % YB[h]], 128)
+        if "v" in PLAN[p]:
+            act(T.YS[:, V * h:V * h + V], B[YB[h]][:, 0:V], ["#%d" % YB[h]], ["YS%d" % h], V)
 
-    def edges(t, h):
+    def edges(t):
+        src, rd = window(t, True).indirect(T.LJ[:, :]), wkeys(t, True) + ["LJ", "MK"]
         if t == 0:
-            ts(T.EG[:, :], window(0, True).indirect(T.LI[:, 0:48]), 1.0 / K, None, A.mult, None, wkeys(0, True) + ["LI"],
-               ["EG0", "EG1"], 768 * gat)
+            act(T.EG[:, :], src, rd, ["EG"], 768 * gat, scale=1.0 / K)
             for j in range(2):
-                b = [PL, PU][j]
+                b = [PL, PX][j]
                 for x in range(16):
-                    mm(B[b][0:48, x:384:16], T.EG[:, x::16], T.WD[:, 24 * j:24 * j + 24], True, True, ["EG0", "EG1", "WD"], ["#%d" % b], 48)
-                act(T.TE[0:48, 384 * j:384 * j + 384], B[b][0:48, 0:384], ["#%d" % b], ["TE%d" % j], 384)
+                    mm(B[b][0:48, x:384:16], T.EG[:, x::16], T.WD[:, 24 * j:24 * j + 24], True, True, ["EG", "WD"], ["#%d" % b], 48)
+                lin("va"[j], T.TE[0:48, V * j:V * j + V], B[b][0:48, 0:V], ["#%d" % b], ["TE%d" % j], V, 0.0)
             for j in range(2):
-                b = [PS1, PL][j]
-                for i in range(3 * j, 3 * j + 3):
-                    mm(B[b][:, 48 * i:48 * i + 48], T.TE[0:48, 128 * i:128 * i + 128], T.WF[0:48, 15:63], True, True, ["TE%d" % j, "WF"],
-                       ["#%d" % b], 256)
-                ts(T.EL[:, 144 * j:144 * j + 144], B[b][:, 144 * j:144 * j + 144], 1537.0, None, A.add, None, ["#%d" % b],
-                   ["EL%d%d" % (i, hh) for i in range(3 * j, 3 * j + 3) for hh in range(2)], 144)
+                b = [PS, PL][j]
+                for i in range(3):
+                    for h in range(2):
+                        mm(B[b][:, 72 * h + 24 * i:72 * h + 24 * i + 24], T.TE[0:48, V * j + 128 * i:V * j + 128 * i + 128],
+                           T.ID[0:48, 24 * h:24 * h + 24], True, True, ["TE%d" % j, "ID"], ["#%d" % b], 64)
+                ts(T.LI[:, :, 48 + 72 * j:120 + 72 * j], B[b][:, 0:144], 1536.0 + OB, None, A.add, None, ["#%d" % b],
+                   ["EL%d" % i for i in range(3 * j, 3 * j + 3)], 144)
             return
-        src, rd = window(t, True).indirect(T.LI[:, 24 * h:24 * h + 24]), wkeys(t, True) + ["LI", "MK"]
-        ts(T.EG[:, 384 * h:384 * h + 384], src, T.MK[:, 6 + 2 * t:7 + 2 * t], None, A.mult, None, rd, ["EG%d" % h], 384 * gat)
+        act(T.EG[:, :], src, rd, ["EG"], 768 * gat, scale=T.MK[:, 6 + 2 * t:7 + 2 * t])
         for x in range(16):
             o = 15 + 6 + 2 * t - x
-            mm(B[PL][:, 0:24], T.WH[:, o:o + 128], T.EG[:, 384 * h + x:384 * h + 384:16], x == 0, x == 15, ["EG%d" % h, "WH"], ["#7"], 64)
-        c = 48 * (5 + t) + 24 * h
-        ts(T.EL[:, c:c + 24], B[PL][:, 0:24], 1537.0, None, A.add, None, ["#7"], ["EL%d%d" % (5 + t, h)])
+            mm(B[PL][:, 0:48], T.WH[:, o:o + 128], T.EG[:, x::16], x == 0, x == 15, ["EG", "WH"], ["#%d" % PL], 64)
+        c = 48 + 24 * (5 + t)
+        ts(T.LI[:, :, c:c + 24], B[PL][:, 0:48], 1536.0 + OB, None, A.add, None, ["#%d" % PL], ["EL%d" % (5 + t)])
+
+    def stores(t):
+        xb = T.XB[:, V * t:V * t + V]
+        tt(xb, window(t, True).indirect(T.LI[:, 1, 0:24]), T.OK[:, :], A.is_equal, wkeys(t, True) + ["LI", "OK"], ["XB%d" % t], V * gat)
+        for b in range(3):
+            for u in range(t + 1):
+                mm(B[PX][:, b:24:3], T.XB[:, V * u + 128 * b:V * u + 128 * b + 128], T.NS[:, 8 * u:8 * u + 8], u == 0, u == t,
+                   ["XB%d" % u, "NS%d" % u], ["#%d" % PX], 64)
+        o, E = 264 * 2 * t, nsrc(t, 0)
+        ts(T.RS[:, o + 1:o + 24 * E:E], B[PX][:, 0:24], 0.0, BIG, A.is_equal, A.mult, ["#%d" % PX, "RS%d" % (2 * t)], ["nm%d" % t])
 
     ring = [0]
 
-    def source(t, h, name, fused):
+    def call(t, h, eng, e0, n):
         E = nsrc(t, h)
-        if name == "ys":
-            e, off, full, k = 0, T.LI[:, 120:144], True, "LI"
-        elif name == "cp":
-            e, off, full, k = 1 - h, T.LI[:, 48 + 24 * h:72 + 24 * h], True, "LI"
+        full = e0 < 2 - h
+        if ring[0] % RING + n > RING:
+            ring[0] += RING - ring[0] % RING
+        s0 = ring[0] % RING
+        ring[0] += n
+        c = 24 * (e0 + h)
+        src = window(t, full).indirect(T.LI[:, h, c:c + 24 * n])
+        rd = wkeys(t, full) + ["LI"] + ["EL%d" % (e - 2 + h) for e in range(e0, e0 + n) if e >= 2 - h]
+        gk = ["G%d" % s for s in range(s0, s0 + n)]
+        if eng == "v":
+            tt(T.G[:, V * s0:V * s0 + V], src, T.YS[:, V * h:V * h + V], A.max, rd + ["YS%d" % h], gk, V * gat)
         else:
-            e, off, full, k = 2 - h + name, T.EL[:, 48 * name + 24 * h:48 * name + 24 * h + 24], False, "EL%d%d" % (name, h)
-        s = ring[0] % RING
-        ring[0] += 1
-        gs = T.G[:, 384 * s:384 * s + 384]
-        gk = "G%d" % s
-        src = window(t, full).indirect(off)
-        if fused:
-            tt(gs, src, T.YS[:, 384 * h:384 * h + 384], A.max, wkeys(t, full) + [k, "YS%d" % h], [gk], 384 * gat)
+            act(T.G[:, V * s0:V * (s0 + n)], src, rd, gk, V * n * gat)
+        for i in range(n):
+            s, e = s0 + i, e0 + i
+            gs = T.G[:, V * s:V * s + V]
+            if eng == "a":
+                tt(gs, gs, B[YB[h]][:, 0:V], A.max, [gk[i], "#%d" % YB[h]], [gk[i]], V)
+            for b in range(3):
+                o = b * E + e
+                lhs = T.G[:, V * s + b:V * s + V:3] if (t, h) == (3, 1) else T.G[:, V * s + 128 * b:V * s + 128 * b + 128]
+                mm(B[DB[h]][:, o:o + 21 * E + 1:3 * E], lhs, T.SS[:, 8 * t:8 * t + 8], True, True, [gk[i], "SS%d" % t], ["#%d" % DB[h]], 256)
+
+    def phase(t, h):
+        E = nsrc(t, h)
+        lo = 2 - h
+        seq = list(range(E)) if t == 0 or h else list(range(lo, E - 1)) + list(range(lo)) + [E - 1]
+        i = 0
+        for tok in PLAN[2 * t + h].split():
+            n = int(tok[1])
+            assert seq[i + n - 1] == seq[i] + n - 1, (t, h, tok)
+            call(t, h, tok[0], seq[i], n)
+            i += n
+        assert i == E, (t, h)
+
+    def put(p, w, kinds, extra=()):
+        t, h = p // 2, p % 2
+        s = slice(128 * p, 128 * p + 128)
+        r = 7 + 2 * t
+        if h == 0:
+            pairs = [(W[w][16 * q + r:16 * q + r + kinds, OB:TM], T.S[0:24 * kinds, s]) for q in range(8)]
+            dma("s", pairs, ["S%d" % p] + ["W%dp%d" % (w, q) for q in range(8)], ["+W%do" % w], PAR["put"])
         else:
-            act(gs, src, wkeys(t, full) + [k], [gk], 384 * gat)
-            tt(gs, gs, B[YB[h]][:, 0:384], A.max, [gk, "#%d" % YB[h]], [gk], 384)
-        for b in range(3):
-            o = 8 * b * E + e
-            mm(B[DB[h]][:, o:o + 7 * E + 1:E], T.G[:, 384 * s + 128 * b:384 * s + 128 * b + 128], T.SS[:, 8 * t:8 * t + 8],
-               True, True, [gk, "SS%d" % t], ["#%d" % DB[h]], 256)
-
-    def stores(t):
-        src = window(t, True).indirect(T.LI[:, 96:120])
-        if t == 0:
-            tt(T.XB[:, :], src, T.OK[:, :], A.is_equal, wkeys(t, True) + ["LI", "OK"], ["XB"], 384 * gat)
-            for b in range(3):
-                mm(B[PS2][:, 8 * b:8 * b + 8], T.XB[:, 128 * b:128 * b + 128], T.NS[:, :], True, True, ["XB", "NS"], ["#6"], 64)
-            ts(named(0), B[PS2][:, 0:24], 1.0, None, A.min, None, ["#6", "RS00"], ["nm0"])
-        else:
-            act(T.XG[:, :], src, wkeys(t, True) + ["LI"], ["XG"], 384 * gat)
-            for b in range(3):
-                mm(B[PS2][:, 8 * b:8 * b + 8], T.XG[:, 128 * b:128 * b + 128], T.TS[:, 8 * t - 8:8 * t], True, True,
-                   ["XG", "TS%d" % t], ["#6"], 256)
-            tt(T.NE[:, :], B[PS2][:, 0:24], T.OC[:, :], A.is_equal, ["#6", "OC"], ["NE"])
-            tt(named(t), T.NE[:, :], named(t - 1), A.max, ["NE", "nm%d" % (t - 1), "RS%d0" % t], ["nm%d" % t])
-
-    def tops0():
-        for h in range(2):
-            for b in range(3):
-                o = 128 * b + 64 * h + 7
-                ts(T.TN[:, 24 * h + 8 * b:24 * h + 8 * b + 8], T.C[:, o:o + 57:8], -1537.0, None, A.add, None, ["C"], ["TN0%d%d" % (h, b)])
-
-    def put(q, w, t, kinds, rd=()):
-        for kind in kinds:
-            r = [7 + 2 * t, 8 + 2 * t, TAIL[t]][kind]
-            if kind < 2:
-                in_, k = T.S1[64 * kind:64 * kind + 64, 384 * t:384 * t + 384], "S1%d" % t
-            else:
-                in_, k = T.S2[0:64, 384 * t:384 * t + 384], "S2%d" % t
-            dma(q, W[w][r::16, 385:WW], in_, [k] + list(rd), ["+W%do" % w])
-
-    def sel(j, b, m=128):
-        return T.SM[0:96, 384 * j + 128 * b:384 * j + 128 * b + m]
-
-    def ut(p):
-        return T.UT[0:96, 128 * p:128 * p + 128]
+            pairs = [(W[w][r + k::16, TM:TM + V], T.S[24 * k:24 * k + 24, s]) for k in range(kinds)]
+            dma("s", pairs, ["S%d" % p, "W%dp8" % w], ["+W%dt" % w])
 
     def gains(t, h):
         p = 2 * t + h
@@ -436,118 +424,77 @@ def rank_program(g, core, T, topo):
         n = 24 * E
         d, dk = B[DB[h]][:, 0:n], "#%d" % DB[h]
         if t == 3:
-            ma, mb, mc = [m[:, 264 * h:264 * h + n] for m in (T.MA, T.MB, T.MC)]
-            ts(ma, d, 1536.0, MAGIC, A.add, A.add, [dk], ["MA%d" % h], n)
-            if h == 0:
-                act(mb, ma, ["MA%d" % h], ["MB%d" % h], n, bias=-MAGIC)
-            else:
-                ts(mb, ma, -MAGIC, None, A.add, None, ["MA%d" % h], ["MB%d" % h], n)
-            tt(mc, d, mb, A.subtract, [dk, "MB%d" % h], ["MC%d" % h], n)
+            mq, mc = T.MQ[:, 264 * h:264 * h + n], T.MC[:, 264 * h:264 * h + n]
+            ts(mq, d, 0.375, None, A.add, None, [dk], ["MQ%d" % h], n)
+            tt(mc, d, mq, A.subtract, [dk, "MQ%d" % h], ["MC%d" % h], n)
             d, dk = mc, "MC%d" % h
         sc = T.SC[:, 264 * h:264 * h + n]
-        rk = ["RS%d%d" % (t, h)] + (["nm%d" % t] if h == 0 else [])
-        op("v", lambda e: e.tensor_tensor_scan(sc, reset(t, h), d, 0.0, A.mult, A.min), rk + [dk], ["SC%d" % h], n)
+        rk = ["RS%d" % p] + (["nm%d" % t] if h == 0 else [])
+        op("v", lambda e: e.tensor_tensor_scan(sc, reset(t, h), d, 0.0, A.add, A.min), rk + [dk], ["SC%d" % h], n)
         x = T.SC[:, 264 * h + E - 1:264 * h + n:E]
-        a, bs = T.SA[:, 24 * p:24 * p + 24], T.BS[:, 24 * p:24 * p + 24]
-        ts(a, x, 0.0, -4000.0 if t < 3 else 384.0, A.is_equal, A.mult, ["SC%d" % h], ["SA%d" % p])
-        tt(bs, x, a, A.add, ["SC%d" % h, "SA%d" % p], ["BS%d" % p])
-        if t == 3:
-            for b in range(3):
-                o = 18 + 3 * h + b
-                ts(T.SG[:, o:o + 169:24], T.BS[:, 24 * p + 8 * b:24 * p + 8 * b + 8], 1536.0, None, A.add, None, ["BS%d" % p],
-                   ["SG%d%d" % (h, b)])
+        s = T.S[:, 128 * p:128 * p + 128] if p < 7 else None
+        ps, pk = B[PS], "#%d" % PS
+        if p == 7:
+            ts(T.SG[:, :], x, K, 3456.0, A.mult, A.add, ["SC1"], ["SG"])
             return
-        old = ["TN0%d%d" % (h, b) for b in range(3)] if t == 0 else ["TN%d" % p]
-        new = T.TN[:, 24 * p + 48:24 * p + 72]
-        tt(new, T.TN[:, 24 * p:24 * p + 24], bs, A.max, old + ["BS%d" % p], ["TN%d" % (p + 2)])
-        for d2 in range(2):
-            ts(T.TC[:, 96 * p + d2:96 * p + 96:4], new, 1537.0, None, A.add, None, ["TN%d" % (p + 2), "TCz0", "TCz1"], ["TC%d%d" % (p, d2)])
-        mm(B[PU][0:96, 0:128], T.TC[:, 96 * p:96 * p + 96], T.ID[:, :], True, True, ["TC%d0" % p, "TC%d1" % p, "ID"], ["#4"], 128)
-        op("v", lambda e: e.tensor_copy(ut(p), B[PU][0:96, 0:128]), ["#4"], ["UT%d" % p], 128)
-        cs = [slice(128 * b, 128 * b + 128) for b in range(3)]
-        if h == 0:
-            for b in range(3):
-                if t == 0:
-                    mm(B[PS1][:, cs[b]], T.SO0[:, :], T.U[:, cs[b]], True, False, ["U", "SO0"], ["#5"], 128)
-                else:
-                    mm(B[PS1][:, cs[b]], sel(0, b), ut(p - 2), True, False, ["UT%d" % (p - 2), "SM0%d" % b], ["#5"], 128)
-                mm(B[PS1][:, cs[b]], sel(1, b), ut(p), False, True, ["UT%d" % p, "SM1%d" % b], ["#5"], 128)
-            for b in range(3):
-                mm(B[PS2][0:64, cs[b]], sel(0, b, 64), ut(p), True, True, ["UT%d" % p, "SM0%d" % b], ["#6"], 128)
-            act(T.S1[:, 384 * t:384 * t + 384], B[PS1][:, 0:384], ["#5"], ["S1%d" % t], 384, bias=-K)
-            ts(T.S2[0:64, 384 * t:384 * t + 384], B[PS2][0:64, 0:384], 1537.0 - K, None, A.add, None, ["#6"], ["S2%d" % t], 384)
-            put("s", (t + 1) % 2, t, [0, 1, 2])
-        else:
-            for b in range(3):
-                hi, hk = (T.SH3[:, :], "SH3") if t == 2 else (T.SWH[:, 1024:1152], "SWH8")
-                mm(B[PS1][:, cs[b]], hi, T.U[:, cs[b]], True, False, ["U", hk], ["#5"], 128)
-                mm(B[PS1][:, cs[b]], T.SWL[:, 1024:1152], T.U[:, cs[b]], False, False, ["U", "SWL8"], ["#5"], 128)
-                for u in range(t + 1):
-                    mm(B[PS1][:, cs[b]], sel(3 + u, b), ut(2 * u + 1), False, u == t, ["UT%d" % (2 * u + 1), "SM%d%d" % (3 + u, b)],
-                       ["#5"], 128)
-            act(W[(t + 1) % 2][:, 0:384], B[PS1][:, 0:384], ["#5", "c%d" % (25 + t)], ["W%dt" % ((t + 1) % 2)], 384, bias=col[25 + t])
-        for b in range(3):
-            mm(B[YB[h]][:, cs[b]], sel(2, b), ut(p), True, True, ["UT%d" % p, "SM2%d" % b], ["#%d" % YB[h]], 128)
-        ycopy(t + 1, h)
+        if p == 6:
+            ts(tc(14), x, K, 1920.0, A.mult, A.add, ["SC0", "TCz"], ["TG6"])
+            mm(ps[0:24, 0:128], tc(14), T.ID[:, :], True, True, ["TG6", "ID"], [pk], 128)
+            act(T.S[0:24, 768:896], ps[0:24, 0:128], [pk], ["S6"], 128, bias=1536.0)
+            dma("s", [(T.gst[:, 96:112, :], T.S[0:24, 768:896])], ["S6"], ["+gst"])
+            return
+        ts(T.EE[:, :], x, -2048.0, K + 1.0, A.is_lt, A.mult, ["SC%d" % h], ["EE"])
+        tt(tc(p + 2), x, T.EE[:, :], A.add, ["SC%d" % h, "EE", "TCz"], ["TC%d" % (p + 2)])
+        ts(tc(8 + p), x, K, 1920.0, A.add, A.min, ["SC%d" % h, "TCz"], ["TG%d" % p])
+        terms = [(p, 0, T.KID, "KID"), (p, 0, T.NID, "NID"), (p + 2, 0, T.ID, "ID"), (p + 2, 1, T.KID, "KID"), (p + 2, 2, T.KID, "KID")]
+        terms += [(p + 2, 2, T.NID, "NID")] if t == 2 else []
+        terms += [(8 + p, 3, T.ID, "ID")]
+        for i, (sl, kind, m, mk) in enumerate(terms):
+            mm(ps[0:96, 0:128], tc(sl, kind), m[:, :], i == 0, i == len(terms) - 1, ["TC%d" % sl if sl < 8 else "TG%d" % p, mk], [pk], 128)
+        c = 23 if t == 2 else 22
+        act(T.S[0:96, 128 * p:128 * p + 128], ps[0:96, 0:128], [pk, "c%d" % c], ["S%d" % p], 128, bias=T.KC[0:96, c:c + 1])
+        put(p, (t + 1) % 2, 3)
+        thresholds(p + 2)
+        rows = [32 * t + 16 * h] + ([112] if p == 0 else [])
+        dma("s", [(T.gst[:, r:r + 16, :], T.S[72:96, 128 * p:128 * p + 128]) for r in rows], ["S%d" % p], ["+gst"])
 
-    def early_gains():
-        ks = ["BS%d" % p for p in range(6)]
-        ts(T.GA[:, :], T.BS[:, 0:144], -3500.0, 4384.0, A.is_lt, A.mult, ks, ["GA"], 144)
-        tt(T.GB[:, :], T.BS[:, 0:144], T.GA[:, :], A.add, ks + ["GA"], ["GB"], 288)
-        for q in range(8):
-            ts(T.SG[:, 24 * q:24 * q + 18], T.GB[:, q::8], 1536.0, None, A.add, None, ["GB"], ["SGq%d" % q])
-
-    def phase(t, h, names):
-        nf, n = PAR["fused"][2 * t + h], len(names)
-        fz = set(((2 * j + 1) * n) // (2 * nf) for j in range(nf))
-        for i, name in enumerate(names):
-            if name == "ys" and t:
-                stores(t)
-            source(t, h, name, i in fz)
-
-    ycopy(0, 0)
-    edges(0, 0)
-    stores(0)
-    ycopy(0, 1)
+    thresholds(0)
+    edges(0)
+    thresholds(1)
     for t in range(RO):
         if t:
             gains(t - 1, 1)
-            edges(t, 0)
-        phase(t, 0, ["cp", "ys", 0, 1, 2, 3, 4, 5] if t == 0 else list(range(5 + t)) + ["cp", "ys", 5 + t])
-        if t == 0:
-            tops0()
-        gains(t, 0)
-        if t in (1, 2):
-            put("g", (t + 1) % 2, t - 1, [0, 1], ["EL%d0" % (5 + t)])
+            if t < 3:
+                put(2 * t - 2, (t + 1) % 2, 2)
+                put(2 * t - 1, (t + 1) % 2, 2)
+            edges(t)
         if t == 1:
-            dma("g", T.yp[:, :], T.ownf[:, :], ["ownf"], ["yp"])
-        if t:
-            edges(t, 1)
+            dma("g", [(T.yp[:, :], T.ownf[:, :])], ["ownf"], ["yp"], 4.0)
+        stores(t)
+        phase(t, 0)
+        gains(t, 0)
         if t == 3:
-            early_gains()
-        phase(t, 1, ["cp"] + list(range(6 + t)))
+            tr1 = alltoall(T.gst, T.hand2, T.sem.h1, T.land2, T.sem.arr2)
+            raw("g", lambda e: e.remote_dma_fused(tr1, local_sem=T.sem.sent), ["gst"], ["away1"], 1.0)
+            dma("s", [(T.land2[rank], T.gst[rank])], ["gst"], ["own2"])
+        phase(t, 1)
     gains(3, 1)
 
-    sg = ["SGq%d" % q for q in range(8)] + ["SG%d%d" % (h, b) for h in range(2) for b in range(3)]
-    tr1 = [RemoteDMATransfer(dst_ids=[dst(topo, hc, core)], dma_engine_mask=bits(inner[4 * j:4 * j + 4]), remote_sem=T.sem.h1,
-                             src=T.SG[:, 24 * span_start(qs):24 * span_start(qs) + 96], dst=T.handg[:, :])
-           for j, (hc, qs) in enumerate(helpers)]
-    tr2 = [RemoteDMATransfer(dst_ids=[dst(topo, cores[q], core)], dma_engine_mask=bits(dm[j]), remote_sem=T.sem.arrg,
-                             src=T.SG[:, 24 * q:24 * q + 24], dst=T.RG[:, 24 * rank:24 * rank + 24]) for j, q in enumerate(direct)]
-    sent[0] += 4 * len(helpers) + sum(len(m) for m in dm)
-    raw("g", lambda e: e.remote_dma_fused(tr1, local_sem=T.sem.sent), sg, ["away1"], 1.0)
-    raw("g", lambda e: e.remote_dma_fused(tr2, local_sem=T.sem.sent), sg, ["away2"], 1.0)
-    op("v", lambda e: e.tensor_copy(T.RG[:, 24 * rank:24 * rank + 24], T.SG[:, 24 * rank:24 * rank + 24]), sg, ["RG"])
-    raw("p", lambda e: e.wait_ge(T.sem.arrg, narr), ["away1", "away2"], ["home"], 6.0)
-    for j in range(2):
-        mm(B[j][0:96, 0:128], T.RG[:, 96 * j:96 * j + 96], T.ID[:, :], True, True, ["RG", "ID", "home"], ["#%d" % j], 128)
-    act(T.OG[0:96, 0:128], B[0][0:96, 0:128], ["#0"], ["OG0"], 128, bias=1536.0)
-    ts(T.OG[0:96, 128:256], B[1][0:96, 0:128], 1536.0, None, A.add, None, ["#1"], ["OG1"], 128)
-    for j in range(8):
-        q = (j % 2) * 4 + j // 2
-        dma("as"[j % 2], T.yp[16 * q + 6:16 * q + 10, :], T.OG[24 * (q % 4):24 * (q % 4) + 24, 128 * (q // 4):128 * (q // 4) + 128],
-            ["OG%d" % (q // 4)], ["+yp"])
-    raw("g", lambda e: e.wait_ge(T.sem.sent, sent[0]), [], [], 0.0)
+    tr2 = [RemoteDMATransfer(dst_ids=[dst(topo, hc, core)], dma_engine_mask=bits(every[4 * j:4 * j + 4]), remote_sem=T.sem.h2,
+                             src=T.SG[:, 3 * q:3 * q + 3], dst=T.hand3[:, :]) for j, (hc, q) in enumerate(helpers)]
+    tr3 = [RemoteDMATransfer(dst_ids=[dst(topo, cores[q], core)], dma_engine_mask=bits(dm[j]), remote_sem=T.sem.arr3,
+                             src=T.SG[:, 3 * q:3 * q + 3], dst=T.land3[rank]) for j, q in enumerate(direct)]
+    raw("g", lambda e: e.remote_dma_fused(tr2, local_sem=T.sem.sent), ["SG"], ["away2"], 1.0)
+    raw("g", lambda e: e.remote_dma_fused(tr3, local_sem=T.sem.sent), ["SG"], ["away3"], 1.0)
+    raw("s", lambda e: e.wait_ge(T.sem.arr2, near + far), ["away1"], [], 5.0)
+    dma("s", [(T.yp[6 + t::16, :], T.land2[:, 32 * t:32 * t + 32, :]) for t in range(3)] + [(T.yp[9::16, 0:V], T.land2[:, 96:112, :])],
+        ["own2"], ["+yp"])
+    dma("a", [(T.yp[16 * rank + 9:16 * rank + 10, V:2 * V], T.SG[:, 3 * rank:3 * rank + 3])], ["SG"], ["+yp"])
+    raw("s", lambda e: e.wait_ge(T.sem.arr3, near + far), ["away2", "away3"], [], 5.0)
+    last = [(T.yp[9:16 * rank:16, V:2 * V], T.land3[0:rank])] if rank else []
+    last += [(T.yp[16 * rank + 25::16, V:2 * V], T.land3[rank + 1:N])] if rank < N - 1 else []
+    dma("s", last, [], ["+yp"])
+    raw("g", lambda e: e.wait_ge(T.sem.sent, 3 * len(every) + sum(len(m) for m in dm)), [], [], 0.0)
     emit(g, T, ops)
 
 
@@ -615,7 +562,7 @@ def arrange(ops, deps):
         ready[q].remove(i)
         start = max(free[q], can[i])
         end = start + ops[i]["cost"]
-        free[q] = start + ((1.0 if q == "g" else 0.1) if ops[i]["kind"] == "dma" else ops[i]["cost"])
+        free[q] = start + ((1.0 if q == "g" else 0.1) * len(ops[i]["fn"]) if ops[i]["kind"] == "dma" else ops[i]["cost"])
         order.append(i)
         for j in after[i]:
             can[j] = max(can[j], end + 0.08 if i in deps[j][0] or ops[i]["kind"] == "raw" else start)
@@ -655,15 +602,17 @@ def emit(g, T, ops):
         e = eng[o["q"]]
         for j in waits[i]:
             e.wait_ge(mark[j][0], mark[j][1])
-        ins = o["fn"](e)
         if o["kind"] == "dma":
-            mark[i] = (T.sem["d%d" % nd], 16)
+            mark[i] = (T.sem["d%d" % nd], 16 * len(o["fn"]))
             nd += 1
-            ins.then_inc(mark[i][0], 16)
-        elif i in need:
+            for out, in_ in o["fn"]:
+                e.dma_start(out, in_).then_inc(mark[i][0], 16)
+            continue
+        ins = o["fn"](e)
+        if i in need:
             count[o["q"]] += 1
             mark[i] = (T.sem["c" + o["q"]], count[o["q"]])
             ins.then_inc(mark[i][0], 1)
     for i in order:
         if ops[i]["kind"] == "dma" and i not in need:
-            g.wait_ge(mark[i][0], 16)
+            g.wait_ge(mark[i][0], mark[i][1])

@@ -3,31 +3,34 @@ from concourse.mybir import AluOpType, ActivationFunctionType, AxisListType
 
 N, V, RO = 8, 384, 4
 K = 4096.0
-OB, TM, WW = 8, 3080, 3465
+E0, OB, TM, WW = 384, 392, 3464, 3849
 RING = 12
 BIG = 8192.0
 AROWS = [12, 13, 0, 2, 4, 6]
-PLAN = ["v1 v1 a2 v1 a2 a1", "a2 v1 a2 v1 a1", "a2 v1 a2 v1 a2 v1", "a2 v1 a2 v1 a1 v1", "a2 v1 a2 v1 a1 a2 v1", "a2 v1 a2 v1 a2 v1",
-        "a2 v1 a2 v1 a2 a2 v1", "a2 v1 a2 a2 a2 v1"]
-PAR = {"gat": 1.56, "cyc": 0.0009, "fix": 0.04, "pe": 0.00045, "dma": 2.4, "put": 3.6, "slack": 0.12, "arr": 3.5, "arrf": 4.0,
-       "gcopy": 3}
+PLAN = ['a2 v1 a2 v1 v1 v1', 'v1 a2 a2 a2', 'v1 a2 v1 v1 v1 a2 v1', 'v1 a2 a2 a2 a1', 'v1 a2 v1 a1 v1 v1 a2 v1', 'v1 a2 a2 a2 a2',
+        'v1 a2 v1 a1 v1 v1 v1 a2 v1', 'v1 a2 a2 a2 a2 a1']
+LOADS = ["va", "a", "a", "a"]
+PAR = {"wide": 0, "mq": "a", "rows": "vv", "late": 1, "gat": 1.4, "cyc": 0.001, "fix": 0.06, "pe": 0.00045, "dma": 1.5, "put": 2.6, "slack": 0.12,
+       "arr": 1.5, "arrf": 4.5, "gcopy": 3, "sem": 0.08, "turns": 2, "tops": 0}
 
 f32, f16, bf16, i32, u16 = "float32", "float16", "bfloat16", "int32", "uint16"
 SCRATCH = {"stage": ("dram", [8, 128, 64], i32), "land": ("dram", [8, 128, 64], i32), "hand": ("dram", [128, 64], i32),
            "gst": ("dram", [8, 128, 24], f32), "land2": ("dram", [8, 128, 24], f32), "hand2": ("dram", [128, 24], f32),
            "land3": ("dram", [8, 128, 3], f32), "hand3": ("dram", [128, 3], f32),
-           "LI": ("sbuf", [128, 2, 264], u16), "L": ("sbuf", [128, 2, 48], i32)}
+           "LI": ("sbuf", [128, 2, 264], u16)}
 for _d, _l in [
-    (f16, "natf 768 natm 768 D 768 EG 768 TE 768 TC 1512 UT 1024 ID 128 ZF 128 ZM 128 Z1 128 Z2 128"),
-    (f32, "ownf 768 W0 3472 W1 3472 KF 8 KC 40 J 160 CK 128 SL 128 WN 128 CY 128 C16 16 CV 384 M16 16 MK 16 GM 8 SS 32 OK 384 "
-          "SC 528 MC 528 EE 24 S 896 YS 768 G 4608 SG 24 B1 128 B2 128"),
-    (bf16, "BP 128 SW 512 ST 256 SY 384 KID 128 NID 128 WH 160 WD 48 NS 32 ZE 264 RS 2112 XB 1536"),
-    (i32, "own 768 nat 768 LD 48 KI 2 KJ 8 MQ 528"), (u16, "LJ 48")]:
+    (f16, "natf 768 natm 768 D 768 EG 768 TE 768 TC 1512 UT 1024 ID 128 ZF 128 ZM 128 Z1 128 Z2 128 XB 384"),
+    (f32, "ownf 768 W0 3856 W1 3856 LA 72 LB 72 KF 8 KC 40 J 160 CK 128 SL 128 WN 128 CY 128 C16 16 CV 384 M16 16 MK 16 GM 8 SS 32 OK 384 "
+          "SC 528 MC 528 SO 1152 S 896 YS 768 G 4608 SG 24 B1 128 B2 128 K6 16 OC 24 NE 24"),
+    (bf16, "BP 128 SW 512 ST 256 SY 384 KID 128 NID 128 WH 160 WD 48 NS 16 ZE 264 RS 2112 SZ 512"),
+    (i32, "own 768 nat 768 L 144 KI 2 KJ 8 MQ 528"), (u16, "LJ 48 LK 72")]:
     _w = _l.split()
     for _i in range(0, len(_w), 2):
         SCRATCH[_w[_i]] = ("sbuf", [128, int(_w[_i + 1])], _d)
-for _b in range(8):
-    SCRATCH["B%d" % _b + "p"] = ("psum", [128, 512], f32)
+for _b in range(2):
+    SCRATCH["Y%dp" % _b] = ("psum", [128, 2, 512], f32)
+for _b in range(2, 6):
+    SCRATCH["B%dp" % _b] = ("psum", [128, 512], f32)
 SEMAPHORES = ["cv", "ca", "cp", "cg", "sent", "arr", "arrf", "arr2", "arr3", "h0", "h1", "h2"] + ["d%d" % _i for _i in range(60)]
 
 A = AluOpType
@@ -39,7 +42,8 @@ def routes(T, topo, core):
     direct = [q for q in range(N) if cores[q] != core and topo.may_write(core, cores[q])]
     far = [q for q in range(N) if cores[q] != core and q not in direct]
     able = [c for c in topo.cores_of(core) if c not in cores and all(topo.may_write(c, cores[q]) for q in far)]
-    return direct, list(zip(able, far))
+    turn = len([q for q in direct if q < cores.index(core)])
+    return direct, [(able[(j + turn) % len(able)], q) for j, q in enumerate(far)]
 
 
 def bits(es):
@@ -137,9 +141,10 @@ def rank_program(g, core, T, topo):
     def gcopy(out, in_, rd, wr, n):
         op("g", lambda e: e.affine_select(out, in_, [[0, n]], A.is_ge, 0.0, 0, 0), rd, wr, cost=0.17 + 2 * n * cyc)
 
-    B = [T["B%dp" % b] for b in range(8)]
+    B = {b: T["B%dp" % b] for b in range(2, 6)}
+    YY = [T.Y0p, T.Y1p]
     W = [T.W0, T.W1]
-    YB, DB, PS, PU, PL, PX = [0, 1], [2, 3], 4, 5, 6, 7
+    DB, PS, PU, PL, PX = [2, 3], 4, 5, 5, 5
 
     def nsrc(t, h):
         return 8 + t - h
@@ -158,7 +163,6 @@ def rank_program(g, core, T, topo):
     iota(T.CK[:, :], [[2, 64], [0, 2]], 0, 0, ["CK"], 128)
     iota(T.SL[:, :], [[0, 8], [1, 8], [0, 2]], 2, 0, ["SL"], 128)
     iota(T.WN[:, :], [[0, 8], [1, 8], [100, 2]], -97, 0, ["WN"], 128)
-    iota(T.J[:, :], [[1, 160]], 0, -1, ["J"], 160)
     dm = direct_masks(topo, core, cores, direct)
     every = topo.engines(core, helpers[0][0])
     inner = [e for e in every if e not in topo.engines(core, cores[direct[0]])]
@@ -171,16 +175,19 @@ def rank_program(g, core, T, topo):
     tr0 = alltoall(T.stage, T.hand, T.sem.h0, T.land, T.sem.arr)
     raw("g", lambda e: e.remote_dma_fused(tr0, local_sem=T.sem.sent), st, ["away"], 3.0)
     dma("s", [(T.land[rank], T.stage[rank])], st, ["landown"])
+    iota(T.J[:, :], [[1, 160]], 0, -1, ["J"], 160)
     iota(T.CY[0:32, :], [[3, 8], [0, 16]], 0, -1, ["CY"], 128)
+    iota(T.OC[:, :], [[384, 8], [128, 3]], -1536, 1, ["OC"], 24)
     iota(T.CV[:, :], [[4096, 384]], -1536 * 4096, 0, ["CV"], 384)
-    raw("g", lambda e: e.wait_ge(T.sem.sent, len(every)), ["away"], [], 0.5)
-    dma("g", [(T.own[:, :], T.pts[:, :])], [], ["own"], 4.0)
-    ms(T.nat[0:64, :], 0, ["nat0", "nat1"], 768)
     ms(T.ZE[:, :], 0.0, ["ZE"], 132)
     for p in range(8):
         n = nsrc(p // 2, p % 2)
         op("g", lambda e, p=p, n=n: e.affine_select(reset(p // 2, p % 2), T.ZE[:, 0:24 * n], [[0, 24], [1, n]], A.is_gt, BIG, 0, 0),
            ["ZE"], ["RS%d" % p], cost=0.17 + 48 * n * cyc)
+        if p == 1:
+            for j in range(6):
+                op("g", lambda e, j=j: e.affine_select(T.TC[:, 252 * j:252 * j + 252], T.ZE[:, 0:252], [[0, 252]], A.is_ge, 0.0, 0, 0),
+                   ["ZE"], ["+TCz"], cost=0.17 + 504 * cyc)
     near, far = arrivals(T, topo, rank)
 
     for j, (s, s2, o, o2) in enumerate([(15, None, A.bitwise_and, None), (4, None, A.arith_shift_right, None), (1, None, A.bitwise_and, None),
@@ -219,9 +226,19 @@ def rank_program(g, core, T, topo):
         for k, q in enumerate(waves[w]):
             act(T.ST[:, 128 * w + 16 * q:128 * w + 16 * q + 16], T.BP[:, 0:16], ["BP", "GM", "ST"], ["ST%d" % q],
                 scale=T.GM[:, 2 * k + 1:2 * k + 2])
-    act(col[4], T.M16[:, 7:8], ["M16"], ["c4"], bias=-1537.0 * K, scale=K)
+    ms(T.ZM[64:65, 14:15], 1.0, ["ZM"])
+    ts(col[24], kj, 6.0, K, A.is_lt, A.mult, ["KF"], ["c24"])
+    ts(col[25], kp, 14.0, -1536.0 * K, A.is_equal, A.mult, ["KF"], ["c25"])
+    ts(T.K6[:, :], T.C16[:, :], -1.0, col[24], A.is_gt, A.mult, ["C16", "c24"], ["K6"])
+    ms(T.SZ[:, :], 0.0, ["SZ"], 256)
     for w in range(2):
-        ms(W[w][:, 0:OB], -1537.0 * K, ["W%de" % w])
+        for k, q in enumerate(waves[w]):
+            for h in range(2):
+                o = 256 * w + 128 * h + 16 * q
+                act(T.SZ[:, o:o + 16], T.K6[:, :], ["K6", "GM", "c25"], ["+SZ"], scale=T.GM[:, 2 * k + h:2 * k + h + 1], bias=col[25])
+    act(col[4], T.M16[:, 7:8], ["M16"], ["c4"], bias=-1537.0 * K, scale=K - 1.0)
+    for w in range(2):
+        ms(W[w][:, E0:OB], -1537.0 * K, ["W%de" % w])
         ms(W[w][:, WW - 1:WW + 7], -1537.0 * K, ["W%df" % w])
     ts(T.ID[:, :], T.J[:, 0:128], 0.0, None, A.is_equal, None, ["J"], ["ID"], 128)
     ts(T.WH[:, :], T.J[:, :], 15.0, None, A.is_equal, None, ["J"], ["WH"], 160)
@@ -232,7 +249,6 @@ def rank_program(g, core, T, topo):
         act(T.WD[:, 8 * j:8 * j + 8], T.GM[:, :], ["GM", "M16"], ["+WD"], scale=T.M16[:, r:r + 1])
     for b in range(3):
         ts(T.SY[0:32, 128 * b:128 * b + 128], T.CY[0:32, :], -float(b), K, A.is_equal, A.mult, ["CY"], ["+SY"], 128)
-    ms(T.TC[:, :], 0.0, ["TCz"], 756)
     ts(col[5], kr, 12.0, None, A.is_ge, None, ["KF"], ["c5"])
     tt(col[6], k2, k1, A.subtract, ["KF"], ["c6"])
     ts(col[7], col[6], col[5], k1, A.mult, A.add, ["c5", "c6", "KF"], ["c7"])
@@ -244,17 +260,22 @@ def rank_program(g, core, T, topo):
     act(col[15], col[16], ["c16"], ["c15"], scale=1.0 / K)
     for t in range(4):
         act(T.SS[:, 8 * t:8 * t + 8], T.GM[:, :], ["GM", "c%d" % (12 + t)], ["SS%d" % t], scale=col[12 + t])
-    ts(T.NS[:, 0:8], T.SS[:, 0:8], 0.0, None, A.max, None, ["SS0"], ["NS0"])
-    for t in range(1, 4):
-        act(T.NS[:, 8 * t:8 * t + 8], T.GM[:, :], ["GM", "M16"], ["NS%d" % t], scale=T.M16[:, 6 + 2 * t:7 + 2 * t])
+    ts(T.NS[:, 0:8], T.SS[:, 0:8], 0.0, None, A.max, None, ["SS0"], ["+NS"])
+    act(T.NS[:, 8:16], T.GM[:, :], ["GM"], ["+NS"])
     act(col[17], kg, ["KF"], ["c17"], scale=384.0 * K)
     act(T.OK[:, :], T.CV[:, :], ["CV", "c17"], ["OK"], 384, bias=col[17])
-    ts(col[18], kp, 72.0, K + 1536.0, A.is_ge, A.mult, ["KF"], ["c18"])
-    ts(col[19], kp, 48.0, None, A.is_ge, None, ["KF"], ["c19"])
-    ts(col[20], kp, 72.0, col[19], A.is_lt, A.mult, ["KF", "c19"], ["c20"])
-    ts(col[21], col[18], -K, None, A.add, None, ["c18"], ["c21"])
-    ts(col[22], col[20], K, col[21], A.mult, A.add, ["c20", "c21"], ["c22"])
-    ts(col[23], col[20], 1921.0, col[21], A.mult, A.add, ["c20", "c21"], ["c23"])
+    for h, u in enumerate([8.0, 24.0]):
+        c = 28 + 4 * h
+        if not (h or PAR["wide"]):
+            continue
+        ts(col[18], kp, 3 * u, 2 * K + 1535.0, A.is_ge, A.mult, ["KF"], ["c18"])
+        ts(col[27], kp, 3 * u, 2.0 ** 24, A.is_lt, A.mult, ["KF"], ["c27"])
+        act(col[c + 2], col[27], ["c27"], ["c%d" % (c + 2)], bias=3456.0)
+        ts(col[19], kp, 2 * u, None, A.is_ge, None, ["KF"], ["c19"])
+        ts(col[20], kp, 3 * u, col[19], A.is_lt, A.mult, ["KF", "c19"], ["c20"])
+        act(col[21], col[18], ["c18"], ["c21"], bias=-K)
+        act(col[c], col[20], ["c20", "c21"], ["c%d" % c], scale=K - 1.0, bias=col[21])
+        act(col[c + 1], col[20], ["c20", "c21"], ["c%d" % (c + 1)], scale=1921.0, bias=col[21])
 
     def tc(s, kind=None):
         o = 72 + 96 * s
@@ -262,8 +283,9 @@ def rank_program(g, core, T, topo):
 
     def block(w, q, k, b, eng):
         c0 = OB + V * q
-        mm(B[b][:, 0:V], T.SW[:, 128 * k:128 * k + 128], T.D[:, V * w:V * w + V], True, True, ["D%d" % w, "SW%d" % k], ["#%d" % b], V)
-        lin(eng, T.W0[:, c0:c0 + V], B[b][:, 0:V], ["#%d" % b, "c4"], ["W0p%d" % q], V, col[4])
+        bank = B[b][:, 0:V] if b in B else YY[b - 6][:, 1, 0:V]
+        mm(bank, T.SW[:, 128 * k:128 * k + 128], T.D[:, V * w:V * w + V], True, True, ["D%d" % w, "SW%d" % k], ["#%d" % b], V)
+        lin(eng, T.W0[:, c0:c0 + V], bank, ["#%d" % b, "c4"], ["W0p%d" % q, {2: "X0", 3: "X1", 6: "Z0", 7: "Z1"}[b]], V, col[4])
 
     def copy1(q, n):
         c0 = OB + V * q
@@ -272,15 +294,15 @@ def rank_program(g, core, T, topo):
         else:
             dma("s", [(T.W1[:, c0:c0 + V], T.W0[:, c0:c0 + V])], ["W0p%d" % q], ["W1p%d" % q], 3.0)
 
-    def tops(w):
-        for k, q in enumerate(waves[w]):
-            for b in range(3):
-                mm(B[PU][:, 3 * q + b:3 * q + b + 1], T.D[:, V * w + 128 * b:V * w + 128 * b + 128], T.SW[:, 128 * k + 6:128 * k + 7],
-                   True, True, ["D%d" % w, "SW%d" % k], ["#%d" % PU], 64)
+    def shared(w):
+        d = T.D[:, V * w:V * w + V]
+        mm(B[PU][:, 0:V], T.ST[:, 128 * w:128 * w + 128], d, w == 0, w == 1, ["D%d" % w] + ["ST%d" % q for q in waves[w]], ["#%d" % PU], V)
+        for h in range(2):
+            mm(YY[h][:, 0, 0:V], T.SZ[:, 256 * w + 128 * h:256 * w + 128 * h + 128], d, w == 0, w == 1, ["D%d" % w, "SZ"], ["Y%d" % h], V)
 
     def wave(w):
         cs = slice(V * w, V * w + V)
-        dma("s", [(T.nat[16 * k:16 * k + 12, cs], T.land[q, 0:72, :]) for k, q in enumerate(waves[w])], ["landown"], ["nat%d" % w], 2.2)
+        dma("s", [(T.nat[16 * k:16 * k + 16, cs], T.land[q, 0:96, :]) for k, q in enumerate(waves[w])], ["landown"], ["nat%d" % w], 2.2)
         act(T.natf[0:64, cs], T.nat[0:64, cs], ["nat%d" % w], ["natf%d" % w], V, bias=-1536.0)
         ts(T.natm[0:64, cs], T.nat[0:64, cs], 3071.5, None, A.is_gt, None, ["nat%d" % w], ["natm%d" % w], V)
         mm(B[PS][:, 0:V], T.ZF[0:64, :], T.natf[0:64, cs], True, False, ["natf%d" % w, "ZF"], ["#%d" % PS], V)
@@ -292,27 +314,19 @@ def rank_program(g, core, T, topo):
     for k, q in enumerate(waves[0]):
         block(0, q, k, [2, 3, 6, 7][k], "av"[k % 2])
         copy1(q, 0)
-    tops(0)
-    act(T.ownf[:, :], T.own[:, :], ["own"], ["ownf"], 768)
+    shared(0)
     raw("s", lambda e: e.wait_ge(T.sem.arrf, far), ["away"], [], PAR["arrf"])
     wave(1)
-    dma("s", [(T.LD[:, :], T.land[:, 72:84, :]), (T.L[:, :, 24:48], T.land[:, 84:96, :]), (T.L[:, 1, 0:24], T.land[:, 96:102, :]),
-              (T.L[:, 0, 0:24], T.land[:, 102:108, :])], ["landown"], ["L"], 2.4)
+    dma("s", [(T.L[:, 96:144], T.land[:, 72:84, :])], ["landown"], ["Ld"], 2.2)
+    dma("s", [(T.L[:, 24:72], T.land[:, 84:96, :]), (T.L[:, 0:24], T.land[:, 102:108, :]), (T.L[:, 72:96], T.land[:, 96:102, :])],
+        ["landown"], ["L"], 2.8)
     for k, q in enumerate(waves[1]):
         block(1, q, k, [2, 3, 6, 7][k], "av"[k % 2])
-    for w in range(2):
-        mm(B[1][:, 0:V], T.ST[:, 128 * w:128 * w + 128], T.D[:, V * w:V * w + V], w == 0, w == 1,
-           ["D%d" % w] + ["ST%d" % q for q in waves[w]], ["#1"], V)
-    lin("a", T.W0[:, TM:TM + V], B[1][:, 0:V], ["#1", "c4"], ["W0p8"], V, col[4])
-    ts(T.LJ[:, :], T.LD[:, :], float(OB), None, A.add, None, ["L"], ["LJ"])
-    ts(T.LI[:, :, 0:48], T.L[:, :, :], float(OB), None, A.add, None, ["L"], ["LI"], 96)
-    tops(1)
-    for b in range(3):
-        for w in range(2):
-            mm(B[PU][:, 24 + b:48:3], T.D[:, V * w + 128 * b:V * w + 128 * b + 128], T.ST[:, 128 * w + 6:128 * w + 128:16], w == 0, w == 1,
-               ["D%d" % w] + ["ST%d" % q for q in waves[w]], ["#%d" % PU], 64)
-    for h in range(2):
-        ts(tc(h), B[PU][:, 24 * h:24 * h + 24], 1.0 / K, -1536.0, A.mult, A.add, ["#%d" % PU, "TCz"], ["TC%d" % h])
+    shared(1)
+    lin("a", T.W0[:, TM:TM + V], B[PU][:, 0:V], ["#%d" % PU, "c4"], ["W0p8"], V, col[4])
+    ts(T.LJ[:, :], T.L[:, 96:144], float(OB - E0), None, A.add, None, ["Ld", "D1"], ["LJ"])
+    for out, a, b in [(T.LI[:, 0, 0:48], 0, 48), (T.LI[:, 1, 24:48], 48, 72), (T.LI[:, 1, 0:24], 72, 96)]:
+        ts(out, T.L[:, a:b], float(OB - E0), None, A.add, None, ["L", "D1"], ["+LI"])
     for n, q in enumerate(waves[1] + [8]):
         copy1(q, n)
 
@@ -321,26 +335,59 @@ def rank_program(g, core, T, topo):
         return [w + "p%d" % q for q in range(9 if full else 8)] + [w + "e", w + "o"] + ([w + "f", w + "t"] if full else [])
 
     def window(t, full):
-        return W[t % 2][:, 0:WW] if full else W[t % 2][:, 0:TM]
+        return W[t % 2][:, E0:WW] if full else W[t % 2][:, E0:TM]
+
+    def newest(t, a, b):
+        return W[t % 2][:, 0:TM].indirect(T.LK[:, a:b]), wkeys(t, False) + ["W%dy" % (t % 2), "LK", "MK"]
+
+    def tops():
+        for h in range(2):
+            for b in range(3):
+                for w in range(2):
+                    o = 256 * w + 128 * h
+                    mm(B[PU][:, 24 * h + b:24 * h + 24:3], T.D[:, V * w + 128 * b:V * w + 128 * b + 128], T.SZ[:, o:o + 128:16], w == 0, w == 1,
+                       ["D%d" % w, "SZ"], ["#%d" % PU], 64)
+        for h in range(2):
+            act(tc(h), B[PU][:, 24 * h:24 * h + 24], ["#%d" % PU, "TCz"], ["TC%d" % h], scale=1.0 / K)
 
     def thresholds(p):
         h = p % 2
         u = T.UT[0:24, 128 * p:128 * p + 128]
-        mm(B[PU][0:24, 0:128], tc(p), T.ID[:, :], True, True, ["TC%d" % p, "ID"], ["#%d" % PU], 128)
-        act(u, B[PU][0:24, 0:128], ["#%d" % PU], ["UT%d" % p], 128)
-        for b in range(3):
-            mm(B[YB[h]][:, 128 * b:128 * b + 128], T.SY[0:24, 128 * b:128 * b + 128], u, True, True, ["UT%d" % p, "SY"], ["#%d" % YB[h]], 128)
+        if p > 1:
+            mm(B[PU][0:24, 0:128], tc(p), T.ID[:, :], True, True, ["TC%d" % p, "ID"], ["#%d" % PU], 128)
+            act(u, B[PU][0:24, 0:128], ["#%d" % PU], ["UT%d" % p], 128)
+        for b in range(3 if p > 1 else 0):
+            mm(YY[h][:, 0, 128 * b:128 * b + 128], T.SY[0:24, 128 * b:128 * b + 128], u, True, True, ["UT%d" % p, "SY"], ["+Y%d" % h], 128)
+        for b in range(3 if p > 1 else 0):
+            mm(YY[h][:, 1, 128 * b:128 * b + 128], T.SY[0:24, 128 * b:128 * b + 128], u, True, True, ["UT%d" % p, "SY"], ["+Z%d" % h], 128)
+        for w in range(0 if p > 1 else 2):
+            mm(YY[h][:, 1, 0:V], T.SZ[:, 256 * w + 128 * h:256 * w + 128 * h + 128], T.D[:, V * w:V * w + V], w == 0, w == 1,
+               ["D%d" % w, "SZ"], ["Z%d" % h], V)
+        if h and p > 1 and PAR["tops"]:
+            act(W[p // 2 % 2][:, 0:V], YY[h][:, 0, 0:V], ["Y1"], ["W%dy" % (p // 2 % 2), "YS1"], V, bias=-K)
         if "v" in PLAN[p]:
-            act(T.YS[:, V * h:V * h + V], B[YB[h]][:, 0:V], ["#%d" % YB[h]], ["YS%d" % h], V)
+            act(T.YS[:, V * h:V * h + V], YY[h][:, 0, 0:V], ["Y%d" % h], ["YS%d" % h], V)
 
-    def edges(t):
-        src, rd = window(t, True).indirect(T.LJ[:, :]), wkeys(t, True) + ["LJ", "MK"]
+    def edges(t, h=0):
+        rd = wkeys(t, True) + ["LJ", "MK"]
+        scale = T.MK[:, 6 + 2 * t:7 + 2 * t] if t else 1.0 / K
+        m = 3 - len(LOADS[t])
+        if m == 2 and h:
+            return
+        for j in ([h] if t else [0, 1]):
+            src, out = window(t, True).indirect(T.LJ[:, 24 * j:24 * j + 24 * m]), T.EG[:, V * j:V * j + V * m]
+            if t and PAR["tops"]:
+                src, rd = newest(t, 24 + 24 * j, 24 + 24 * j + 24 * m)
+            ek = ["EG%d" % i for i in range(j, j + m)]
+            if LOADS[t][j] == "a":
+                act(out, src, rd, ek, V * m * gat, scale=scale)
+            else:
+                ts(out, src, scale, None, A.mult, None, rd, ek, V * m * gat)
         if t == 0:
-            act(T.EG[:, :], src, rd, ["EG"], 768 * gat, scale=1.0 / K)
             for j in range(2):
-                b = [PL, PX][j]
+                b = [PS, PU][j]
                 for x in range(16):
-                    mm(B[b][0:48, x:384:16], T.EG[:, x::16], T.WD[:, 24 * j:24 * j + 24], True, True, ["EG", "WD"], ["#%d" % b], 48)
+                    mm(B[b][0:48, x:384:16], T.EG[:, x::16], T.WD[:, 24 * j:24 * j + 24], True, True, ["EG0", "EG1", "WD"], ["#%d" % b], 48)
                 lin("va"[j], T.TE[0:48, V * j:V * j + V], B[b][0:48, 0:V], ["#%d" % b], ["TE%d" % j], V, 0.0)
             for j in range(2):
                 b = [PS, PL][j]
@@ -348,25 +395,35 @@ def rank_program(g, core, T, topo):
                     for h in range(2):
                         mm(B[b][:, 72 * h + 24 * i:72 * h + 24 * i + 24], T.TE[0:48, V * j + 128 * i:V * j + 128 * i + 128],
                            T.ID[0:48, 24 * h:24 * h + 24], True, True, ["TE%d" % j, "ID"], ["#%d" % b], 64)
-                ts(T.LI[:, :, 48 + 72 * j:120 + 72 * j], B[b][:, 0:144], 1536.0 + OB, None, A.add, None, ["#%d" % b],
-                   ["EL%d" % i for i in range(3 * j, 3 * j + 3)], 144)
+                ts(T.LI[:, :, 48 + 72 * j:120 + 72 * j], B[b][:, 0:144], 1536.0 + OB - E0, None, A.add, None, ["#%d" % b],
+                   ["EL%d%d" % (i, h) for i in range(3 * j, 3 * j + 3) for h in range(2)], 144)
             return
-        act(T.EG[:, :], src, rd, ["EG"], 768 * gat, scale=T.MK[:, 6 + 2 * t:7 + 2 * t])
         for x in range(16):
             o = 15 + 6 + 2 * t - x
-            mm(B[PL][:, 0:48], T.WH[:, o:o + 128], T.EG[:, x::16], x == 0, x == 15, ["EG", "WH"], ["#%d" % PL], 64)
+            mm(B[PL][:, 0:24 * m], T.WH[:, o:o + 128], T.EG[:, V * h + x:V * h + V * m:16], x == 0, x == 15, ek + ["WH"], ["#%d" % PL], 64)
         c = 48 + 24 * (5 + t)
-        ts(T.LI[:, :, c:c + 24], B[PL][:, 0:48], 1536.0 + OB, None, A.add, None, ["#%d" % PL], ["EL%d" % (5 + t)])
+        ts(T.LI[:, h:h + m, c:c + 24], B[PL][:, 0:24 * m], 1536.0 + OB - E0, None, A.add, None, ["#%d" % PL],
+           ["EL%d%d" % (5 + t, i) for i in range(h, h + m)])
+
+    def unnamed(t):
+        return T.RS[:, 528 * t + 1:528 * t + 24 * nsrc(t, 0):nsrc(t, 0)]
 
     def stores(t):
-        xb = T.XB[:, V * t:V * t + V]
-        tt(xb, window(t, True).indirect(T.LI[:, 1, 0:24]), T.OK[:, :], A.is_equal, wkeys(t, True) + ["LI", "OK"], ["XB%d" % t], V * gat)
+        src, rd = window(t, True).indirect(T.LI[:, 1, 0:24]), wkeys(t, True) + ["LI"]
+        if t == 0:
+            tt(T.XB[:, :], src, T.OK[:, :], A.is_equal, rd + ["OK"], ["XB"], V * gat)
+        else:
+            if PAR["tops"]:
+                src, rd = newest(t, 0, 24)
+            act(T.XB[:, :], src, rd + ["MK"], ["XB"], V * gat, scale=T.MK[:, 6 + 2 * t:7 + 2 * t])
         for b in range(3):
-            for u in range(t + 1):
-                mm(B[PX][:, b:24:3], T.XB[:, V * u + 128 * b:V * u + 128 * b + 128], T.NS[:, 8 * u:8 * u + 8], u == 0, u == t,
-                   ["XB%d" % u, "NS%d" % u], ["#%d" % PX], 64)
-        o, E = 264 * 2 * t, nsrc(t, 0)
-        ts(T.RS[:, o + 1:o + 24 * E:E], B[PX][:, 0:24], 0.0, BIG, A.is_equal, A.mult, ["#%d" % PX, "RS%d" % (2 * t)], ["nm%d" % t])
+            mm(B[PX][:, b:24:3], T.XB[:, 128 * b:128 * b + 128], T.NS[:, 8 * min(t, 1):8 * min(t, 1) + 8], True, True, ["XB", "NS"],
+               ["#%d" % PX], 64)
+        if t == 0:
+            ts(unnamed(0), B[PX][:, 0:24], 0.0, BIG, A.is_equal, A.mult, ["#%d" % PX, "RS0"], ["nm0"])
+        else:
+            tt(T.NE[:, :], B[PX][:, 0:24], T.OC[:, :], A.not_equal, ["#%d" % PX, "OC"], ["NE"])
+            tt(unnamed(t), T.NE[:, :], unnamed(t - 1), A.mult, ["NE", "nm%d" % (t - 1), "RS%d" % (2 * t)], ["nm%d" % t])
 
     ring = [0]
 
@@ -379,7 +436,7 @@ def rank_program(g, core, T, topo):
         ring[0] += n
         c = 24 * (e0 + h)
         src = window(t, full).indirect(T.LI[:, h, c:c + 24 * n])
-        rd = wkeys(t, full) + ["LI"] + ["EL%d" % (e - 2 + h) for e in range(e0, e0 + n) if e >= 2 - h]
+        rd = wkeys(t, full) + ["LI"] + ["EL%d%d" % (e - 2 + h, h) for e in range(e0, e0 + n) if e >= 2 - h]
         gk = ["G%d" % s for s in range(s0, s0 + n)]
         if eng == "v":
             tt(T.G[:, V * s0:V * s0 + V], src, T.YS[:, V * h:V * h + V], A.max, rd + ["YS%d" % h], gk, V * gat)
@@ -387,13 +444,14 @@ def rank_program(g, core, T, topo):
             act(T.G[:, V * s0:V * (s0 + n)], src, rd, gk, V * n * gat)
         for i in range(n):
             s, e = s0 + i, e0 + i
-            gs = T.G[:, V * s:V * s + V]
-            if eng == "a":
-                tt(gs, gs, B[YB[h]][:, 0:V], A.max, [gk[i], "#%d" % YB[h]], [gk[i]], V)
+            if eng == "a" and i % 2 == 0:
+                m = min(2, n - i)
+                gs = T.G[:, V * s:V * (s + m)]
+                tt(gs, gs, YY[h][:, 0:m, 0:V], A.max, gk[i:i + m] + ["Y%d" % h, "Z%d" % h, "YS%d" % h], gk[i:i + m], V * m)
             for b in range(3):
                 o = b * E + e
                 lhs = T.G[:, V * s + b:V * s + V:3] if (t, h) == (3, 1) else T.G[:, V * s + 128 * b:V * s + 128 * b + 128]
-                mm(B[DB[h]][:, o:o + 21 * E + 1:3 * E], lhs, T.SS[:, 8 * t:8 * t + 8], True, True, [gk[i], "SS%d" % t], ["#%d" % DB[h]], 256)
+                mm(B[DB[h]][:, o:o + 21 * E + 1:3 * E], lhs, T.SS[:, 8 * t:8 * t + 8], True, True, [gk[i], "SS%d" % t], ["+X%d" % h], 256)
 
     def phase(t, h):
         E = nsrc(t, h)
@@ -407,25 +465,29 @@ def rank_program(g, core, T, topo):
             i += n
         assert i == E, (t, h)
 
-    def put(p, w, kinds, extra=()):
+    def rows(p, a, b):
+        if p % 2 or not PAR["wide"]:
+            return T.S[24 * a:24 * b, 128 * p:128 * p + 128]
+        return T.SO[8 * a:8 * b, V * (p // 2):V * (p // 2) + V]
+
+    def put(p, w, kinds):
         t, h = p // 2, p % 2
-        s = slice(128 * p, 128 * p + 128)
         r = 7 + 2 * t
         if h == 0:
-            pairs = [(W[w][16 * q + r:16 * q + r + kinds, OB:TM], T.S[0:24 * kinds, s]) for q in range(8)]
+            pairs = [(W[w][16 * q + r:16 * q + r + kinds, OB:TM], rows(p, 0, kinds)) for q in range(8)]
             dma("s", pairs, ["S%d" % p] + ["W%dp%d" % (w, q) for q in range(8)], ["+W%do" % w], PAR["put"])
         else:
-            pairs = [(W[w][r + k::16, TM:TM + V], T.S[24 * k:24 * k + 24, s]) for k in range(kinds)]
+            pairs = [(W[w][r + k::16, TM:TM + V], rows(p, k, k + 1)) for k in range(kinds)]
             dma("s", pairs, ["S%d" % p, "W%dp8" % w], ["+W%dt" % w])
 
     def gains(t, h):
         p = 2 * t + h
         E = nsrc(t, h)
         n = 24 * E
-        d, dk = B[DB[h]][:, 0:n], "#%d" % DB[h]
+        d, dk = B[DB[h]][:, 0:n], "X%d" % h
         if t == 3:
             mq, mc = T.MQ[:, 264 * h:264 * h + n], T.MC[:, 264 * h:264 * h + n]
-            ts(mq, d, 0.375, None, A.add, None, [dk], ["MQ%d" % h], n)
+            lin(PAR["mq"], mq, d, [dk], ["MQ%d" % h], n, 0.375)
             tt(mc, d, mq, A.subtract, [dk, "MQ%d" % h], ["MC%d" % h], n)
             d, dk = mc, "MC%d" % h
         sc = T.SC[:, 264 * h:264 * h + n]
@@ -443,24 +505,39 @@ def rank_program(g, core, T, topo):
             act(T.S[0:24, 768:896], ps[0:24, 0:128], [pk], ["S6"], 128, bias=1536.0)
             dma("s", [(T.gst[:, 96:112, :], T.S[0:24, 768:896])], ["S6"], ["+gst"])
             return
-        ts(T.EE[:, :], x, -2048.0, K + 1.0, A.is_lt, A.mult, ["SC%d" % h], ["EE"])
-        tt(tc(p + 2), x, T.EE[:, :], A.add, ["SC%d" % h, "EE", "TCz"], ["TC%d" % (p + 2)])
-        ts(tc(8 + p), x, K, 1920.0, A.add, A.min, ["SC%d" % h, "TCz"], ["TG%d" % p])
-        terms = [(p, 0, T.KID, "KID"), (p, 0, T.NID, "NID"), (p + 2, 0, T.ID, "ID"), (p + 2, 1, T.KID, "KID"), (p + 2, 2, T.KID, "KID")]
+        ts(tc(8 + p), x, -2048.0, K, A.is_lt, A.mult, ["SC%d" % h, "TCz"], ["TG%d" % p])
+        tt(tc(p + 2), x, tc(8 + p), A.add, ["SC%d" % h, "TG%d" % p, "TCz"], ["TC%d" % (p + 2)])
+        terms = [(p, 0, T.KID, "KID"), (p, 0, T.NID, "NID"), (8 + p, 3, T.NID, "NID"), (p + 2, 0, T.ID, "ID"), (p + 2, 1, T.KID, "KID"),
+                 (p + 2, 2, T.KID, "KID"), (p + 2, 3, T.ID, "ID")]
         terms += [(p + 2, 2, T.NID, "NID")] if t == 2 else []
-        terms += [(8 + p, 3, T.ID, "ID")]
+        nb = 1 if h or not PAR["wide"] else 3
+        u = 24 // nb
+        if nb == 3:
+            mm(ps[0:32, 0:V], T.TC[:, 0:32], T.D[:, 0:V], True, False, ["TCz", "D0"], [pk], V)
         for i, (sl, kind, m, mk) in enumerate(terms):
-            mm(ps[0:96, 0:128], tc(sl, kind), m[:, :], i == 0, i == len(terms) - 1, ["TC%d" % sl if sl < 8 else "TG%d" % p, mk], [pk], 128)
-        c = 23 if t == 2 else 22
-        act(T.S[0:96, 128 * p:128 * p + 128], ps[0:96, 0:128], [pk, "c%d" % c], ["S%d" % p], 128, bias=T.KC[0:96, c:c + 1])
+            o = 72 + 96 * sl - 24 * kind
+            for b in range(nb):
+                mm(ps[0:4 * u, 128 * b:128 * b + 128], T.TC[:, o + b:o + 96:nb], m[:, :], i == 0 and nb == 1,
+                   i == len(terms) - 1 and b == nb - 1, ["TC%d" % sl if sl < 8 else "TG%d" % p, mk], [pk], 128)
+        c0 = 32 if nb == 1 else 28
+        c = c0 + (t == 2)
+        ts(rows(p, 0, 4), ps[0:4 * u, 0:128 * nb], T.KC[0:4 * u, c:c + 1], T.KC[0:4 * u, c0 + 2:c0 + 3], A.add, A.min,
+           [pk, "c%d" % c, "c%d" % (c0 + 2)], ["S%d" % p], 128 * nb)
         put(p, (t + 1) % 2, 3)
-        thresholds(p + 2)
-        rows = [32 * t + 16 * h] + ([112] if p == 0 else [])
-        dma("s", [(T.gst[:, r:r + 16, :], T.S[72:96, 128 * p:128 * p + 128]) for r in rows], ["S%d" % p], ["+gst"])
+        if h or not PAR["late"]:
+            thresholds(p + 2)
+        to = [32 * t + 16 * h] + ([112] if p == 0 else [])
+        dma("s", [(T.gst[:, r:r + 16, :], rows(p, 3, 4)) for r in to], ["S%d" % p], ["+gst"])
 
     thresholds(0)
     edges(0)
     thresholds(1)
+    tops()
+    dma("g", [(T.own[:, :], T.pts[:, :])], ["TE0"], ["own"], 4.0)
+    gcopy(T.ownf[:, :], T.own[:, :], ["own"], ["ownf"], 768)
+    ts(T.LA[:, :], T.L[:, 72:144], 3071.5, float(TM), A.is_lt, A.mult, ["L", "Ld", "EG0"], ["LA"])
+    tt(T.LB[:, :], T.L[:, 72:144], T.LA[:, :], A.add, ["LA"], ["LB"], 144)
+    ts(T.LK[:, :], T.LB[:, :], -3072.0, None, A.add, None, ["LB"], ["LK"])
     for t in range(RO):
         if t:
             gains(t - 1, 1)
@@ -469,7 +546,7 @@ def rank_program(g, core, T, topo):
                 put(2 * t - 1, (t + 1) % 2, 2)
             edges(t)
         if t == 1:
-            dma("g", [(T.yp[:, :], T.ownf[:, :])], ["ownf"], ["yp"], 4.0)
+            dma("g", [(T.yp[:, :], T.ownf[:, :])], ["ownf", "EL60"], ["yp"], 4.0)
         stores(t)
         phase(t, 0)
         gains(t, 0)
@@ -477,7 +554,11 @@ def rank_program(g, core, T, topo):
             tr1 = alltoall(T.gst, T.hand2, T.sem.h1, T.land2, T.sem.arr2)
             raw("g", lambda e: e.remote_dma_fused(tr1, local_sem=T.sem.sent), ["gst"], ["away1"], 1.0)
             dma("s", [(T.land2[rank], T.gst[rank])], ["gst"], ["own2"])
+        if t:
+            edges(t, 1)
         phase(t, 1)
+        if t < 3 and PAR["late"]:
+            thresholds(2 * t + 2)
     gains(3, 1)
 
     tr2 = [RemoteDMATransfer(dst_ids=[dst(topo, hc, core)], dma_engine_mask=bits(every[4 * j:4 * j + 4]), remote_sem=T.sem.h2,
@@ -544,32 +625,50 @@ def depends(ops):
 
 def arrange(ops, deps):
     n = len(ops)
+    wait = [o["cost"] if o["kind"] == "raw" and o["q"] == "s" else 0.0 for o in ops]
+    hold = [(1.0 if o["q"] == "g" else 0.1) * len(o["fn"]) if o["kind"] == "dma" else o["cost"] - wait[i] for i, o in enumerate(ops)]
+    before = [[(j, ops[j]["cost"] + PAR["sem"] + wait[i]) for j in hard] + [(j, hold[j]) for j in soft] for i, (hard, soft) in enumerate(deps)]
     after = [[] for i in range(n)]
-    for i, (hard, soft) in enumerate(deps):
-        for j in hard | soft:
-            after[j].append(i)
-    left = [len(h | s) for h, s in deps]
-    ready = {q: [] for q in "gvaps"}
-    can = [0.0] * n
-    free = {q: 0.0 for q in "gvaps"}
     for i in range(n):
-        if not left[i]:
-            ready[ops[i]["q"]].append(i)
-    order = []
-    while len(order) < n:
+        for j, lag in before[i]:
+            after[j].append((i, lag))
+
+    def lay(order, back):
+        start, taken = [0.0] * n, {q: [] for q in "gvaps"}
+        for i in order:
+            if back:
+                t = max([ops[i]["cost"] - wait[i]] + [start[j] + lag for j, lag in after[i]]) - hold[i]
+            else:
+                t = max([0.0] + [start[j] + lag for j, lag in before[i]])
+            row = taken[ops[i]["q"]]
+            k = len(row)
+            while k and row[k - 1][1] > t:
+                k -= 1
+            while k < len(row) and row[k][0] < t + hold[i] - 1e-9:
+                t = max(t, row[k][1])
+                k += 1
+            row.insert(k, (t, t + hold[i]))
+            start[i] = t + hold[i] if back else t
+        return start
+
+    left = [len(b) for b in before]
+    ready = {q: [i for i in range(n) if ops[i]["q"] == q and not left[i]] for q in "gvaps"}
+    can, start, free = [0.0] * n, [0.0] * n, {q: 0.0 for q in "gvaps"}
+    for step in range(n):
         t0, q = min((max(free[q], min(can[i] for i in ready[q])), q) for q in ready if ready[q])
         i = min(i for i in ready[q] if can[i] <= t0 + PAR["slack"])
         ready[q].remove(i)
-        start = max(free[q], can[i])
-        end = start + ops[i]["cost"]
-        free[q] = start + ((1.0 if q == "g" else 0.1) * len(ops[i]["fn"]) if ops[i]["kind"] == "dma" else ops[i]["cost"])
-        order.append(i)
-        for j in after[i]:
-            can[j] = max(can[j], end + 0.08 if i in deps[j][0] or ops[i]["kind"] == "raw" else start)
+        start[i] = max(free[q], can[i])
+        free[q] = start[i] + hold[i]
+        for j, lag in after[i]:
+            can[j] = max(can[j], start[i] + lag)
             left[j] -= 1
             if not left[j]:
                 ready[ops[j]["q"]].append(j)
-    return order
+    for turn in range(PAR["turns"]):
+        late = lay(sorted(range(n), key=lambda i: (-start[i], -i)), True)
+        start = lay(sorted(range(n), key=lambda i: (-late[i], i)), False)
+    return sorted(range(n), key=lambda i: (start[i], i))
 
 
 def emit(g, T, ops):

@@ -4,26 +4,27 @@ from concourse.mybir import AluOpType, ActivationFunctionType, AxisListType
 N, V, RO = 8, 384, 4
 K = 4096.0
 E0, OB, TM, WW = 384, 392, 3464, 3849
-RING = 12
+RING = 14
 BIG = 8192.0
-AROWS = [12, 13, 0, 2, 4, 6]
-PLAN = ['a2 v1 a2 v1 v1 v1', 'v1 a2 a2 a2', 'v1 a2 v1 v1 v1 a2 v1', 'v1 a2 a2 a2 a1', 'v1 a2 v1 a1 v1 v1 a2 v1', 'v1 a2 a2 a2 a2',
-        'v1 a2 v1 a1 v1 v1 v1 a2 v1', 'v1 a2 a2 a2 a2 a1']
-LOADS = ["va", "a", "a", "a"]
-PAR = {"wide": 0, "mq": "a", "rows": "vv", "late": 1, "gat": 1.4, "cyc": 0.001, "fix": 0.06, "pe": 0.00045, "dma": 1.5, "put": 2.6, "slack": 0.12,
-       "arr": 1.5, "arrf": 4.5, "gcopy": 3, "sem": 0.08, "turns": 2, "tops": 0}
+PLAN = ['a1 v1 a1 b2 v1 a1 v1', 'a1 b2 b2 a1 v1', 'v1 v1 b3 v1 v1 v1 v1', 'a1 a1 b2 b2 a1 a1', 'v1 v1 v1 b3 a1 v1 a1 v1',
+        'a1 b2 a2 v1 a1 v1 a1', 'v1 v1 v1 a2 a2 v1 v1 v1 v1', 'a2 a2 a2 a1 a1 a1 a1']
+LOADS = ["va", "a", "va", "aa"]
+PAR = {"mq": "a", "el": "vaaaa", "late": 0, "gat": 1.5, "cyc": 0.00092, "fix": 0.07, "pe": 0.00045, "dma": 1.7, "put": 3.0, "slack": 0.12,
+       "arr": 0.8, "arrf": 3.6, "copies": "ggggggggs", "sem": 0.13, "turns": 3}
 
 f32, f16, bf16, i32, u16 = "float32", "float16", "bfloat16", "int32", "uint16"
-SCRATCH = {"stage": ("dram", [8, 128, 64], i32), "land": ("dram", [8, 128, 64], i32), "hand": ("dram", [128, 64], i32),
+SCRATCH = {"stage": ("dram", [8, 128, 36], i32), "land": ("dram", [8, 128, 36], i32), "hand": ("dram", [128, 36], i32),
+           "stagl": ("dram", [8, 128, 24], i32), "landl": ("dram", [8, 128, 24], i32), "handl": ("dram", [128, 24], i32),
            "gst": ("dram", [8, 128, 24], f32), "land2": ("dram", [8, 128, 24], f32), "hand2": ("dram", [128, 24], f32),
            "land3": ("dram", [8, 128, 3], f32), "hand3": ("dram", [128, 3], f32),
-           "LI": ("sbuf", [128, 2, 264], u16)}
+           "LI": ("sbuf", [128, 2, 264], u16), "SL": ("sbuf", [128, 8, 16], f32), "WN": ("sbuf", [128, 8, 16], f32),
+           "RW": ("sbuf", [128, 4, 16], f32), "TE": ("sbuf", [128, 48, 16], f16)}
 for _d, _l in [
-    (f16, "natf 768 natm 768 D 768 EG 768 TE 768 TC 1512 UT 1024 ID 128 ZF 128 ZM 128 Z1 128 Z2 128 XB 384"),
-    (f32, "ownf 768 W0 3856 W1 3856 LA 72 LB 72 KF 8 KC 40 J 160 CK 128 SL 128 WN 128 CY 128 C16 16 CV 384 M16 16 MK 16 GM 8 SS 32 OK 384 "
-          "SC 528 MC 528 SO 1152 S 896 YS 768 G 4608 SG 24 B1 128 B2 128 K6 16 OC 24 NE 24"),
-    (bf16, "BP 128 SW 512 ST 256 SY 384 KID 128 NID 128 WH 160 WD 48 NS 16 ZE 264 RS 2112 SZ 512"),
-    (i32, "own 768 nat 768 L 144 KI 2 KJ 8 MQ 528"), (u16, "LJ 48 LK 72")]:
+    (f16, "natf 768 natm 768 D 768 EG 768 TC 1512 UT 1024 ID 128 ZF 128 ZM 128 Z1 128 Z2 128 XB 384 OH 24"),
+    (f32, "ownf 768 W0 3856 W1 3856 KF 8 KC 40 CK 128 GI 128 GM 8 C16 64 CV 384 M16 64 MK 16 SS 32 OK 384 "
+          "SC 528 MC 528 S 896 YS 768 G %d SG 24 B1 128 B2 128 OC 24 NE 24" % (V * RING)),
+    (bf16, "BP 128 SW 128 ST 256 SY 384 KID 128 NID 128 WH 160 WD 48 NS 16 ZE 512 RS 2112 SZ 512"),
+    (i32, "own 768 nat 768 L 144 KI 2 KJ 8 MQ 528"), (u16, "LJ 48")]:
     _w = _l.split()
     for _i in range(0, len(_w), 2):
         SCRATCH[_w[_i]] = ("sbuf", [128, int(_w[_i + 1])], _d)
@@ -31,7 +32,7 @@ for _b in range(2):
     SCRATCH["Y%dp" % _b] = ("psum", [128, 2, 512], f32)
 for _b in range(2, 6):
     SCRATCH["B%dp" % _b] = ("psum", [128, 512], f32)
-SEMAPHORES = ["cv", "ca", "cp", "cg", "sent", "arr", "arrf", "arr2", "arr3", "h0", "h1", "h2"] + ["d%d" % _i for _i in range(60)]
+SEMAPHORES = ["cv", "ca", "cp", "cg", "sent", "arr", "arrf", "arr2", "arr3", "arrl", "h0", "h1", "h2", "hl"] + ["d%d" % _i for _i in range(60)]
 
 A = AluOpType
 IDENT = ActivationFunctionType.Identity
@@ -59,11 +60,11 @@ def helper_program(g, core, T, topo, rank, q):
     to = T.cores[q]
     es = topo.engines(core, to)
     rid, pid = topo.addr(to, core)
-    for sem, n, out, in_, arr in [(T.sem.h0, 2, T.land, T.hand, T.sem.arrf), (T.sem.h1, 2, T.land2, T.hand2, T.sem.arr2),
-                                  (T.sem.h2, 4, T.land3, T.hand3, T.sem.arr3)]:
+    for sem, n, out, in_, arr in [(T.sem.h0, 2, T.land, T.hand, T.sem.arrf), (T.sem.hl, 2, T.landl, T.handl, T.sem.arrl),
+                                  (T.sem.h1, 2, T.land2, T.hand2, T.sem.arr2), (T.sem.h2, 4, T.land3, T.hand3, T.sem.arr3)]:
         g.wait_ge(sem, n)
         g.remote_dma(out[rank], in_[:, :], arr, T.sem.sent, pid, rid, bits(es))
-    g.wait_ge(T.sem.sent, 3 * len(es))
+    g.wait_ge(T.sem.sent, 4 * len(es))
 
 
 def direct_masks(topo, core, cores, direct):
@@ -138,8 +139,17 @@ def rank_program(g, core, T, topo):
         else:
             op("g", lambda e: e.iota(out, pat, base, cm), [], wr, cost=0.13 + 2 * n * cyc)
 
+    def sel(out, in_, pat, cmp, c, base, cm, rd, wr, n):
+        op("g", lambda e: e.affine_select(out, in_, pat, cmp, c, base, cm), rd, wr, cost=0.17 + 2 * n * cyc)
+
+    def mark(out, pat, c, base, wr, n, parts=128):
+        sel(out, T.ZE[0:parts, 0:n], pat, A.not_equal, c, base, -1, ["ZE"], wr, n)
+
+    def fill(out, zeros, c, wr, n):
+        sel(out, zeros, [[0, n]], A.is_gt, c, 0, 0, ["ZE"], wr, n)
+
     def gcopy(out, in_, rd, wr, n):
-        op("g", lambda e: e.affine_select(out, in_, [[0, n]], A.is_ge, 0.0, 0, 0), rd, wr, cost=0.17 + 2 * n * cyc)
+        sel(out, in_, [[0, n]], A.is_ge, 0.0, 0, 0, rd, wr, n)
 
     B = {b: T["B%dp" % b] for b in range(2, 6)}
     YY = [T.Y0p, T.Y1p]
@@ -153,182 +163,181 @@ def rank_program(g, core, T, topo):
         o = 264 * (2 * t + h)
         return T.RS[:, o:o + 24 * nsrc(t, h)]
 
-    dma("s", [(T.stage[:, 12 * i:12 * i + 12, :], T.pts[i::16, :]) for i in (0, 2, 4)] +
-        [(T.stage[:, 72:84, :], T.ld[:, :]), (T.stage[:, 96:102, :], T.xs[:, :]), (T.stage[:, 108:120, :], T.pts[6::16, :])], [], ["st0"])
-    dma("a", [(T.stage[:, 12 * i:12 * i + 12, :], T.pts[i::16, :]) for i in (1, 3, 5)] +
-        [(T.stage[:, 84:96, :], T.cp[:, :]), (T.stage[:, 102:108, :], T.ys[:, :]), (T.stage[:, 120:128, :], T.pts[7::16, 0:512])], [], ["st1"])
+    other = [q for q in range(N) if q != rank]
+    dma("s", [(T.stage[q], T.pts[16 * q:16 * q + 6, :]) for q in other[0:4]], [], ["st0"])
+    dma("a", [(T.stage[q], T.pts[16 * q:16 * q + 6, :]) for q in other[4:7]], [], ["st1"])
+    dma("s", [(T.stagl[:, 0:32, :], T.ld[:, :]), (T.stagl[:, 64:80, :], T.xs[:, :]), (T.stagl[:, 96:128, :], T.pts[6::16, :])], [], ["sl0"])
+    dma("a", [(T.stagl[:, 32:64, :], T.cp[:, :]), (T.stagl[:, 80:96, :], T.ys[:, :])], [], ["sl1"])
+    dma("a", [(T.land[rank], T.pts[16 * rank:16 * rank + 6, :])], [], ["landown"])
     st = ["st0", "st1"]
+    ms(T.ZE[:, :], 0.0, ["ZE"], 256)
+    ms(T.nat[0:64, :], 1536, ["nat0", "nat1"], 768)
     iota(T.KI[:, 0:1], [[1, 1]], 0, 1, ["KI"], 1, False)
-    iota(T.C16[:, :], [[1, 16]], 0, 0, ["C16"], 16)
-    iota(T.CK[:, :], [[2, 64], [0, 2]], 0, 0, ["CK"], 128)
-    iota(T.SL[:, :], [[0, 8], [1, 8], [0, 2]], 2, 0, ["SL"], 128)
-    iota(T.WN[:, :], [[0, 8], [1, 8], [100, 2]], -97, 0, ["WN"], 128)
+    iota(T.CK[0:64, :], [[1, 64], [0, 2]], 0, -1, ["CK"], 128)
+    iota(T.SL[:, :, 0:12], [[0, 8], [1, 6], [0, 2]], 2, 0, ["+SL"], 96)
+    iota(T.SL[:, :, 12:16], [[0, 8], [0, 2], [1, 2]], 0, 0, ["+SL"], 32)
+    iota(T.WN[:, :, 0:12], [[0, 8], [1, 6], [100, 2]], -97, 0, ["+WN"], 96)
+    iota(T.WN[:, :, 12:16], [[0, 8], [100, 2], [1, 2]], -99, 0, ["+WN"], 32)
     dm = direct_masks(topo, core, cores, direct)
     every = topo.engines(core, helpers[0][0])
     inner = [e for e in every if e not in topo.engines(core, cores[direct[0]])]
 
     def alltoall(src, hand, hsem, land, sem):
-        tr = [RemoteDMATransfer(dst_ids=[dst(topo, hc, core)], dma_engine_mask=bits(inner[2 * j:2 * j + 2]), remote_sem=hsem,
-                                src=src[q], dst=hand[:, :]) for j, (hc, q) in enumerate(helpers)]
+        tr = [RemoteDMATransfer(dst_ids=[dst(topo, hc, core)], dma_engine_mask=bits(inner[4 * (j % 2) + j // 2:4 * (j % 2) + 4:2]), remote_sem=hsem,
+                                src=src[q], dst=hand[:, :]) for j, (hc, q) in enumerate(sorted(helpers, key=lambda x: topo.die(x[0])))]
         return tr + [RemoteDMATransfer(dst_ids=[dst(topo, cores[q], core)], dma_engine_mask=bits(dm[j]), remote_sem=sem,
                                        src=src[q], dst=land[rank]) for j, q in enumerate(direct)]
     tr0 = alltoall(T.stage, T.hand, T.sem.h0, T.land, T.sem.arr)
     raw("g", lambda e: e.remote_dma_fused(tr0, local_sem=T.sem.sent), st, ["away"], 3.0)
-    dma("s", [(T.land[rank], T.stage[rank])], st, ["landown"])
-    iota(T.J[:, :], [[1, 160]], 0, -1, ["J"], 160)
-    iota(T.CY[0:32, :], [[3, 8], [0, 16]], 0, -1, ["CY"], 128)
-    iota(T.OC[:, :], [[384, 8], [128, 3]], -1536, 1, ["OC"], 24)
-    iota(T.CV[:, :], [[4096, 384]], -1536 * 4096, 0, ["CV"], 384)
-    ms(T.ZE[:, :], 0.0, ["ZE"], 132)
-    for p in range(8):
-        n = nsrc(p // 2, p % 2)
-        op("g", lambda e, p=p, n=n: e.affine_select(reset(p // 2, p % 2), T.ZE[:, 0:24 * n], [[0, 24], [1, n]], A.is_gt, BIG, 0, 0),
-           ["ZE"], ["RS%d" % p], cost=0.17 + 48 * n * cyc)
-        if p == 1:
-            for j in range(6):
-                op("g", lambda e, j=j: e.affine_select(T.TC[:, 252 * j:252 * j + 252], T.ZE[:, 0:252], [[0, 252]], A.is_ge, 0.0, 0, 0),
-                   ["ZE"], ["+TCz"], cost=0.17 + 504 * cyc)
+    iota(T.GI[:, :], [[1, 8], [0, 16]], 0, 0, ["GI"], 128)
+    iota(T.C16[:, :], [[0, 4], [1, 16]], 0, 0, ["C16"], 64)
+    trl = alltoall(T.stagl, T.handl, T.sem.hl, T.landl, T.sem.arrl)
+    raw("g", lambda e: e.remote_dma_fused(trl, local_sem=T.sem.sent), ["sl0", "sl1"], ["awayl"], 1.0)
+    dma("s", [(T.landl[rank], T.stagl[rank])], ["sl0", "sl1"], ["listown"])
     near, far = arrivals(T, topo, rank)
 
-    for j, (s, s2, o, o2) in enumerate([(15, None, A.bitwise_and, None), (4, None, A.arith_shift_right, None), (1, None, A.bitwise_and, None),
-                                        (14, None, A.bitwise_and, None), (1, 7, A.arith_shift_right, A.bitwise_and),
-                                        (1, 1, A.arith_shift_right, A.bitwise_and), (0, None, A.arith_shift_right, None)]):
-        ts(T.KJ[:, j:j + 1], T.KI[:, 0:1], s, s2, o, o2, ["KI"], ["KJ%d" % j])
-    op("v", lambda e: e.tensor_copy(T.KF[:, 0:7], T.KJ[:, 0:7]), ["KJ%d" % j for j in range(7)], ["KF"])
-    kr, kg, k1, k14, kj, k2, kp = [T.KF[:, j:j + 1] for j in range(7)]
     col = [T.KC[:, j:j + 1] for j in range(40)]
-    ts(col[0], kg, 32.0, k14, A.mult, A.add, ["KF"], ["c0"])
-    ts(col[1], k1, 16.0, col[0], A.mult, A.add, ["KF", "c0"], ["c1"])
-    ts(col[2], col[1], 2.0, None, A.add, None, ["c1"], ["c2"])
-    ts(col[3], k14, 12.0, None, A.is_lt, None, ["KF"], ["c3"])
-    ts(T.Z1[:, :], T.CK[:, :], col[1], col[3], A.is_equal, A.mult, ["CK", "c1", "c3"], ["Z1"], 128)
-    ts(T.Z2[:, :], T.CK[:, :], col[2], col[3], A.is_equal, A.mult, ["CK", "c2", "c3"], ["Z2"], 128)
-    tt(T.ZF[:, :], T.Z1[:, :], T.Z2[:, :], A.subtract, ["Z1", "Z2"], ["ZF"], 256)
+    for w in range(2):
+        for k, q in enumerate(waves[w]):
+            act(T.KC[32 * k:32 * k + 32, w:w + 1], T.ZE[32 * k:32 * k + 32, 0:1], ["ZE"], ["+q%d" % w], bias=float(q))
+    for j, (s, s2, o, o2) in enumerate([(15, None, A.bitwise_and, None), (4, None, A.arith_shift_right, None), (31, None, A.bitwise_and, None),
+                                        (2, 7, A.arith_shift_right, A.bitwise_and), (1, 1, A.arith_shift_right, A.bitwise_and)]):
+        ts(T.KJ[:, j:j + 1], T.KI[:, 0:1], s, s2, o, o2, ["KI"], ["KJ%d" % j])
+    op("v", lambda e: e.tensor_copy(T.KF[:, 0:5], T.KJ[:, 0:5]), ["KJ%d" % j for j in range(5)], ["KF"])
+    kr, kg, k31, kj, kh = [T.KF[:, j:j + 1] for j in range(5)]
+    ts(T.Z1[0:64, :], T.CK[0:64, :], 0.0, None, A.is_equal, None, ["CK"], ["Z1"], 128)
+    ts(T.Z2[0:64, :], T.CK[0:64, :], 2.0, None, A.is_equal, None, ["CK"], ["Z2"], 128)
+    tt(T.ZF[0:64, :], T.Z1[0:64, :], T.Z2[0:64, :], A.subtract, ["Z1", "Z2"], ["ZF"], 256)
     act(T.ZM[0:64, :], T.ZF[0:64, :], ["ZF"], ["ZMa"], 128, scale=-K)
-    ms(T.ZM[64:96, :], 0.0, ["ZM"])
-    ms(T.ZM[64:65, 1::2], -2048.0, ["ZM"])
-    ms(T.ZM[64:65, 0::16], 1537.0, ["ZM"])
-    ms(T.ZM[64:65, 1::16], -511.0, ["ZM"])
-    ms(T.natm[64:96, :], 1.0, ["ones"], 384)
-    ts(T.M16[:, :], T.C16[:, :], kr, None, A.is_equal, None, ["C16", "KF"], ["M16"])
-    ts(T.GM[:, :], T.C16[:, 0:8], kg, None, A.is_equal, None, ["C16", "KF"], ["GM"])
-    for r, c in [(12, 0.0), (14, 0.0), (13, 1.0), (15, 1.0)]:
-        ms(T.SL[:, r::16], c, ["SL"])
-    for r, c in [(7, -100.0), (14, 1.0), (15, 2.0)]:
-        ms(T.WN[:, r::16], c, ["WN"])
-    ts(T.B1[:, :], T.SL[:, :], kj, K, A.is_ge, A.mult, ["SL", "KF"], ["B1"], 128)
-    ts(T.B2[:, :], T.WN[:, :], kj, None, A.is_equal, None, ["WN", "KF"], ["B2"], 128)
+    for h in range(2):
+        act(T.natm[64:65, V * h:V * h + V], T.ZE[64:65, 0:V], ["ZE"], ["+ones"], V, bias=1.0)
+    for a, step, c, rd, wr in [(0, 2, 0.0, "ZE", "+ZN"), (1, 2, -2048.0, "ZE", "+ZN"), (0, 32, 1537.0, "ZN", "+ZM"), (2, 32, 1537.0, "ZN", "+ZM"),
+                               (1, 32, -511.0, "ZN", "+ZM"), (3, 32, -511.0, "ZN", "+ZM"), (28, 32, 1.0, "ZN", "+ZM")]:
+        act(T.ZM[64:65, a::step], T.ZE[64:65, 0:128 // step], [rd], [wr], bias=c)
+    ms(T.WN[:, :, 7], -100.0, ["WN"])
+    ts(T.B1[:, :], T.SL[:, :, :], kj, K, A.is_ge, A.mult, ["SL", "KF"], ["B1"], 128)
+    ts(T.B2[:, :], T.WN[:, :, :], kj, None, A.is_equal, None, ["WN", "KF"], ["B2"], 128)
     tt(T.BP[:, :], T.B1[:, :], T.B2[:, :], A.add, ["B1", "B2"], ["BP"], 256)
-    for k in range(4):
-        act(T.SW[:, 128 * k:128 * k + 128], T.BP[:, :], ["BP", "GM"], ["SW%d" % k], 128, scale=T.GM[:, 2 * k:2 * k + 1])
-    ms(T.ST[:, :], 0.0, ["ST"], 128)
-    for w in range(2):
-        for k, q in enumerate(waves[w]):
-            act(T.ST[:, 128 * w + 16 * q:128 * w + 16 * q + 16], T.BP[:, 0:16], ["BP", "GM", "ST"], ["ST%d" % q],
-                scale=T.GM[:, 2 * k + 1:2 * k + 2])
-    ms(T.ZM[64:65, 14:15], 1.0, ["ZM"])
-    ts(col[24], kj, 6.0, K, A.is_lt, A.mult, ["KF"], ["c24"])
-    ts(col[25], kp, 14.0, -1536.0 * K, A.is_equal, A.mult, ["KF"], ["c25"])
-    ts(T.K6[:, :], T.C16[:, :], -1.0, col[24], A.is_gt, A.mult, ["C16", "c24"], ["K6"])
-    ms(T.SZ[:, :], 0.0, ["SZ"], 256)
-    for w in range(2):
-        for k, q in enumerate(waves[w]):
-            for h in range(2):
-                o = 256 * w + 128 * h + 16 * q
-                act(T.SZ[:, o:o + 16], T.K6[:, :], ["K6", "GM", "c25"], ["+SZ"], scale=T.GM[:, 2 * k + h:2 * k + h + 1], bias=col[25])
+    act(col[2], kh, ["KF"], ["c2"], bias=1.0, scale=-1.0)
+    act(T.SW[:, :], T.BP[:, :], ["BP", "c2"], ["SW"], 128, scale=col[2])
+    ts(T.M16[:, :], T.C16[:, :], kr, None, A.is_equal, None, ["C16", "KF"], ["M16"])
     act(col[4], T.M16[:, 7:8], ["M16"], ["c4"], bias=-1537.0 * K, scale=K - 1.0)
+    ts(col[5], kj, 6.0, K, A.is_lt, A.mult, ["KF"], ["c5"])
+    ts(col[6], k31, 28.0, -1536.0 * K, A.is_equal, A.mult, ["KF"], ["c6"])
+    act(col[7], col[5], ["c2", "c5", "c6"], ["c7"], scale=col[2], bias=col[6])
+    act(col[8], col[5], ["KF", "c5", "c6"], ["c8"], scale=kh, bias=col[6])
     for w in range(2):
-        ms(W[w][:, E0:OB], -1537.0 * K, ["W%de" % w])
-        ms(W[w][:, WW - 1:WW + 7], -1537.0 * K, ["W%df" % w])
-    ts(T.ID[:, :], T.J[:, 0:128], 0.0, None, A.is_equal, None, ["J"], ["ID"], 128)
-    ts(T.WH[:, :], T.J[:, :], 15.0, None, A.is_equal, None, ["J"], ["WH"], 160)
-    act(T.KID[:, :], T.ID[:, :], ["ID"], ["KID"], 128, scale=K)
-    act(T.NID[:, :], T.ID[:, :], ["ID"], ["NID"], 128, scale=-1.0)
-    act(T.MK[:, :], T.M16[:, :], ["M16"], ["MK"], scale=1.0 / K)
-    for j, r in enumerate(AROWS):
-        act(T.WD[:, 8 * j:8 * j + 8], T.GM[:, :], ["GM", "M16"], ["+WD"], scale=T.M16[:, r:r + 1])
-    for b in range(3):
-        ts(T.SY[0:32, 128 * b:128 * b + 128], T.CY[0:32, :], -float(b), K, A.is_equal, A.mult, ["CY"], ["+SY"], 128)
-    ts(col[5], kr, 12.0, None, A.is_ge, None, ["KF"], ["c5"])
-    tt(col[6], k2, k1, A.subtract, ["KF"], ["c6"])
-    ts(col[7], col[6], col[5], k1, A.mult, A.add, ["c5", "c6", "KF"], ["c7"])
-    act(col[8], col[7], ["c7"], ["c8"], bias=1.0, scale=-2.0)
-    for t in range(3):
-        ts(col[9 + t], kr, 8.0 + 2 * t, col[5], A.is_lt, A.max, ["KF", "c5"], ["c%d" % (9 + t)])
-        ts(col[12 + t], col[9 + t], col[8], T.MK[:, 6 + 2 * t:7 + 2 * t], A.mult, A.add, ["c%d" % (9 + t), "c8", "MK"], ["c%d" % (12 + t)])
-    ts(col[16], T.M16[:, 13:14], -2.0, col[8], A.mult, A.add, ["M16", "c8"], ["c16"])
-    act(col[15], col[16], ["c16"], ["c15"], scale=1.0 / K)
+        ts(T.B1[:, :], T.GI[:, :], col[w], kh, A.is_equal, A.mult, ["GI", "q%d" % w, "KF"], ["B1"], 128)
+        tt(T.ST[:, 128 * w:128 * w + 128], T.B1[:, :], T.BP[:, :], A.mult, ["B1", "BP"], ["ST%d" % w], 256)
+        for h in range(2):
+            o = 256 * w + 128 * h
+            ts(T.SZ[:, o:o + 128], T.GI[:, :], col[w], col[7 + h], A.is_equal, A.mult, ["GI", "q%d" % w, "c%d" % (7 + h)], ["+SZ"], 128)
+    act(T.MK[:, :], T.M16[:, 0:16], ["M16"], ["MK"], scale=1.0 / K)
+    for w in range(2):
+        act(W[w][:, E0:OB], T.ZE[:, 0:8], ["ZE"], ["W%de" % w], bias=-1537.0 * K)
+        act(W[w][:, WW - 1:WW + 7], T.ZE[:, 0:8], ["ZE"], ["W%df" % w], bias=-1537.0 * K)
+    for j in range(3):
+        act(T.TC[:, 504 * j:504 * j + 504], T.ZE[:, 0:504], ["ZE"], ["+TCz"], 504)
+
+    def resets(p):
+        n = nsrc(p // 2, p % 2)
+        sel(reset(p // 2, p % 2), T.ZE[:, 0:24 * n], [[0, 24], [1, n]], A.is_gt, BIG, 0, 0, ["ZE"], ["RS%d" % p], 24 * n)
+
+    mark(T.WD[:, 0:16], [[1, 2], [16, 8]], 1.0, 12, ["+WD"], 16)
+    mark(T.WD[:, 16:48], [[2, 4], [16, 8]], 1.0, 0, ["+WD"], 32)
+    mark(T.ID[:, :], [[1, 128]], 1.0, 0, ["ID"], 128)
+    iota(T.RW[:, :, 0:12], [[0, 4], [0, 6], [-2, 2]], 1, 0, ["+RW"], 48)
+    iota(T.RW[:, :, 12:16], [[0, 4], [-2, 2], [0, 2]], 1, 0, ["+RW"], 16)
+    iota(T.CV[:, :], [[4096, 384]], -1536 * 4096, 0, ["CV"], 384)
+    for t, a, b, c in [(0, 8, 12, 0.0), (1, 10, 12, 0.0), (0, 6, 7, 1 + 1 / K), (1, 8, 9, 1 + 1 / K), (2, 10, 11, 1 + 1 / K), (3, 13, 14, -1.0)]:
+        act(T.RW[:, t, a:b], T.ZE[:, 0:b - a], ["RW"], ["+RX"], bias=c)
+    tt(T.B2[:, 0:64], T.M16[:, :], T.RW[:, :, :], A.mult, ["M16", "RW", "RX"], ["B2"], 128)
+    ts(T.GM[:, :], T.C16[:, 0:8], kg, None, A.is_equal, None, ["C16", "KF"], ["GM"])
     for t in range(4):
-        act(T.SS[:, 8 * t:8 * t + 8], T.GM[:, :], ["GM", "c%d" % (12 + t)], ["SS%d" % t], scale=col[12 + t])
-    ts(T.NS[:, 0:8], T.SS[:, 0:8], 0.0, None, A.max, None, ["SS0"], ["+NS"])
-    act(T.NS[:, 8:16], T.GM[:, :], ["GM"], ["+NS"])
+        op("v", lambda e, t=t: e.tensor_reduce(col[12 + t], T.B2[:, 16 * t:16 * t + 16], AxisListType.X, A.add), ["B2"], ["c%d" % (12 + t)])
+    act(col[16], col[15], ["c15"], ["c16"], scale=1.0 / K)
+    for t, c in enumerate([12, 13, 14, 16]):
+        act(T.SS[:, 8 * t:8 * t + 8], T.GM[:, :], ["GM", "c%d" % c], ["SS%d" % t], scale=col[c])
+    ts(T.NS[:, 0:8], T.SS[:, 0:8], 0.0, None, A.max, None, ["SS0"], ["NS"])
+    act(T.NS[:, 8:16], T.GM[:, :], ["GM"], ["NS1"])
     act(col[17], kg, ["KF"], ["c17"], scale=384.0 * K)
     act(T.OK[:, :], T.CV[:, :], ["CV", "c17"], ["OK"], 384, bias=col[17])
-    for h, u in enumerate([8.0, 24.0]):
-        c = 28 + 4 * h
-        if not (h or PAR["wide"]):
-            continue
-        ts(col[18], kp, 3 * u, 2 * K + 1535.0, A.is_ge, A.mult, ["KF"], ["c18"])
-        ts(col[27], kp, 3 * u, 2.0 ** 24, A.is_lt, A.mult, ["KF"], ["c27"])
-        act(col[c + 2], col[27], ["c27"], ["c%d" % (c + 2)], bias=3456.0)
-        ts(col[19], kp, 2 * u, None, A.is_ge, None, ["KF"], ["c19"])
-        ts(col[20], kp, 3 * u, col[19], A.is_lt, A.mult, ["KF", "c19"], ["c20"])
-        act(col[21], col[18], ["c18"], ["c21"], bias=-K)
-        act(col[c], col[20], ["c20", "c21"], ["c%d" % c], scale=K - 1.0, bias=col[21])
-        act(col[c + 1], col[20], ["c20", "c21"], ["c%d" % (c + 1)], scale=1921.0, bias=col[21])
+    act(T.KID[:, :], T.ID[:, :], ["ID"], ["KID"], 128, scale=K)
+    act(T.NID[:, :], T.ID[:, :], ["ID"], ["NID"], 128, scale=-1.0)
 
-    def tc(s, kind=None):
+    def later():
+        fill(T.KC[:, 32:34], T.ZE[:, 0:2], -K, ["c32", "c33"], 2)
+        for j, c in [(32, -1.0), (33, 1921.0 - K)]:
+            sel(col[j], col[j], [[0, 1]], A.is_ge, c, 47, -1, ["c%d" % j], ["c%d" % j], 1)
+        sel(T.KC[:, 32:34], T.KC[:, 32:34], [[0, 2]], A.is_ge, K + 1535.0, 71, -1, ["c32", "c33"], ["c32", "c33"], 2)
+        fill(col[34], T.ZE[:, 0:1], 2.0 ** 24, ["c34"], 1)
+        sel(col[34], col[34], [[0, 1]], A.is_ge, 3456.0, 71, -1, ["c34"], ["c34"], 1)
+        mark(T.SY[0:32, :], [[1, 3], [3, 8], [0, 16]], K, 0, ["SY"], 384, 32)
+
+    def latest():
+        mark(T.WH[:, :], [[1, 160]], 1.0, -15, ["WH"], 160)
+        iota(T.OC[:, :], [[384, 8], [128, 3]], -1536, 1, ["OC"], 24)
+        gcopy(T.OH[:, :], T.OC[:, :], ["OC"], ["OH"], 24)
+        for p in range(2, 8):
+            resets(p)
+
+    def tc(s):
         o = 72 + 96 * s
-        return T.TC[:, o:o + 24] if kind is None else T.TC[:, o - 24 * kind:o - 24 * kind + 96]
+        return T.TC[:, o:o + 24]
 
     def block(w, q, k, b, eng):
         c0 = OB + V * q
         bank = B[b][:, 0:V] if b in B else YY[b - 6][:, 1, 0:V]
-        mm(bank, T.SW[:, 128 * k:128 * k + 128], T.D[:, V * w:V * w + V], True, True, ["D%d" % w, "SW%d" % k], ["#%d" % b], V)
+        mm(bank, T.SW[32 * k:32 * k + 32, :], T.D[32 * k:32 * k + 32, V * w:V * w + V], True, True, ["D%d" % w, "SW"], ["#%d" % b], V)
         lin(eng, T.W0[:, c0:c0 + V], bank, ["#%d" % b, "c4"], ["W0p%d" % q, {2: "X0", 3: "X1", 6: "Z0", 7: "Z1"}[b]], V, col[4])
 
-    def copy1(q, n):
+    def copy1(q, by):
         c0 = OB + V * q
-        if n < PAR["gcopy"]:
+        if by == "g":
             gcopy(T.W1[:, c0:c0 + V], T.W0[:, c0:c0 + V], ["W0p%d" % q], ["W1p%d" % q], V)
         else:
             dma("s", [(T.W1[:, c0:c0 + V], T.W0[:, c0:c0 + V])], ["W0p%d" % q], ["W1p%d" % q], 3.0)
 
     def shared(w):
         d = T.D[:, V * w:V * w + V]
-        mm(B[PU][:, 0:V], T.ST[:, 128 * w:128 * w + 128], d, w == 0, w == 1, ["D%d" % w] + ["ST%d" % q for q in waves[w]], ["#%d" % PU], V)
+        mm(B[PU][:, 0:V], T.ST[:, 128 * w:128 * w + 128], d, w == 0, w == 1, ["D%d" % w, "ST%d" % w], ["#%d" % PU], V)
         for h in range(2):
             mm(YY[h][:, 0, 0:V], T.SZ[:, 256 * w + 128 * h:256 * w + 128 * h + 128], d, w == 0, w == 1, ["D%d" % w, "SZ"], ["Y%d" % h], V)
 
     def wave(w):
         cs = slice(V * w, V * w + V)
-        dma("s", [(T.nat[16 * k:16 * k + 16, cs], T.land[q, 0:96, :]) for k, q in enumerate(waves[w])], ["landown"], ["nat%d" % w], 2.2)
+        dma("s", [(T.nat[16 * k:16 * k + 12, cs], T.land[q]) for k, q in enumerate(waves[w])], ["landown"], ["nat%d" % w], 2.2)
         act(T.natf[0:64, cs], T.nat[0:64, cs], ["nat%d" % w], ["natf%d" % w], V, bias=-1536.0)
         ts(T.natm[0:64, cs], T.nat[0:64, cs], 3071.5, None, A.is_gt, None, ["nat%d" % w], ["natm%d" % w], V)
         mm(B[PS][:, 0:V], T.ZF[0:64, :], T.natf[0:64, cs], True, False, ["natf%d" % w, "ZF"], ["#%d" % PS], V)
-        mm(B[PS][:, 0:V], T.ZM[0:96, :], T.natm[0:96, cs], False, True, ["natm%d" % w, "ZM", "ZMa", "ones"], ["#%d" % PS], V)
+        mm(B[PS][:, 0:V], T.ZM[0:65, :], T.natm[0:65, cs], False, True, ["natm%d" % w, "ZM", "ZMa", "ones"], ["#%d" % PS], V)
         ts(T.D[:, cs], B[PS][:, 0:V], 0.0, 2048.0, A.max, A.min, ["#%d" % PS], ["D%d" % w], V)
 
     raw("s", lambda e: e.wait_ge(T.sem.arr, near), ["away"], [], PAR["arr"])
     wave(0)
     for k, q in enumerate(waves[0]):
         block(0, q, k, [2, 3, 6, 7][k], "av"[k % 2])
-        copy1(q, 0)
     shared(0)
-    raw("s", lambda e: e.wait_ge(T.sem.arrf, far), ["away"], [], PAR["arrf"])
+    resets(0)
+    resets(1)
+    later()
+    for by, q in zip(PAR["copies"], waves[0]):
+        copy1(q, by)
+    raw("s", lambda e: e.wait_ge(T.sem.arrf, far), ["away"], ["far"], PAR["arrf"])
     wave(1)
-    dma("s", [(T.L[:, 96:144], T.land[:, 72:84, :])], ["landown"], ["Ld"], 2.2)
-    dma("s", [(T.L[:, 24:72], T.land[:, 84:96, :]), (T.L[:, 0:24], T.land[:, 102:108, :]), (T.L[:, 72:96], T.land[:, 96:102, :])],
-        ["landown"], ["L"], 2.8)
+    raw("s", lambda e: e.wait_ge(T.sem.arrl, near + far), ["awayl"], [], PAR["arrf"])
+    dma("s", [(T.L[:, 96:144], T.landl[:, 0:32, :])], ["listown"], ["Ld"], 2.2)
+    dma("s", [(T.L[:, 0:24], T.landl[:, 80:96, :]), (T.L[:, 24:48], T.landl[:, 32:64:2, :]), (T.L[:, 48:72], T.landl[:, 64:80, :]),
+              (T.L[:, 72:96], T.landl[:, 33:64:2, :])], ["listown"], ["L"], 2.8)
     for k, q in enumerate(waves[1]):
         block(1, q, k, [2, 3, 6, 7][k], "av"[k % 2])
     shared(1)
     lin("a", T.W0[:, TM:TM + V], B[PU][:, 0:V], ["#%d" % PU, "c4"], ["W0p8"], V, col[4])
     ts(T.LJ[:, :], T.L[:, 96:144], float(OB - E0), None, A.add, None, ["Ld", "D1"], ["LJ"])
-    for out, a, b in [(T.LI[:, 0, 0:48], 0, 48), (T.LI[:, 1, 24:48], 48, 72), (T.LI[:, 1, 0:24], 72, 96)]:
-        ts(out, T.L[:, a:b], float(OB - E0), None, A.add, None, ["L", "D1"], ["+LI"])
-    for n, q in enumerate(waves[1] + [8]):
-        copy1(q, n)
+    ts(T.LI[:, :, 0:48], T.L[:, 0:96], float(OB - E0), None, A.add, None, ["L", "D1"], ["LI"], 96)
+    for by, q in zip(PAR["copies"][4:], waves[1] + [8]):
+        copy1(q, by)
+    latest()
 
     def wkeys(t, full):
         w = "W%d" % (t % 2)
@@ -336,9 +345,6 @@ def rank_program(g, core, T, topo):
 
     def window(t, full):
         return W[t % 2][:, E0:WW] if full else W[t % 2][:, E0:TM]
-
-    def newest(t, a, b):
-        return W[t % 2][:, 0:TM].indirect(T.LK[:, a:b]), wkeys(t, False) + ["W%dy" % (t % 2), "LK", "MK"]
 
     def tops():
         for h in range(2):
@@ -353,18 +359,17 @@ def rank_program(g, core, T, topo):
     def thresholds(p):
         h = p % 2
         u = T.UT[0:24, 128 * p:128 * p + 128]
+        twice = "a2" in PLAN[p]
         if p > 1:
             mm(B[PU][0:24, 0:128], tc(p), T.ID[:, :], True, True, ["TC%d" % p, "ID"], ["#%d" % PU], 128)
             act(u, B[PU][0:24, 0:128], ["#%d" % PU], ["UT%d" % p], 128)
         for b in range(3 if p > 1 else 0):
             mm(YY[h][:, 0, 128 * b:128 * b + 128], T.SY[0:24, 128 * b:128 * b + 128], u, True, True, ["UT%d" % p, "SY"], ["+Y%d" % h], 128)
-        for b in range(3 if p > 1 else 0):
+        for b in range(3 if p > 1 and twice else 0):
             mm(YY[h][:, 1, 128 * b:128 * b + 128], T.SY[0:24, 128 * b:128 * b + 128], u, True, True, ["UT%d" % p, "SY"], ["+Z%d" % h], 128)
-        for w in range(0 if p > 1 else 2):
+        for w in range(2 if p < 2 and twice else 0):
             mm(YY[h][:, 1, 0:V], T.SZ[:, 256 * w + 128 * h:256 * w + 128 * h + 128], T.D[:, V * w:V * w + V], w == 0, w == 1,
                ["D%d" % w, "SZ"], ["Z%d" % h], V)
-        if h and p > 1 and PAR["tops"]:
-            act(W[p // 2 % 2][:, 0:V], YY[h][:, 0, 0:V], ["Y1"], ["W%dy" % (p // 2 % 2), "YS1"], V, bias=-K)
         if "v" in PLAN[p]:
             act(T.YS[:, V * h:V * h + V], YY[h][:, 0, 0:V], ["Y%d" % h], ["YS%d" % h], V)
 
@@ -376,8 +381,6 @@ def rank_program(g, core, T, topo):
             return
         for j in ([h] if t else [0, 1]):
             src, out = window(t, True).indirect(T.LJ[:, 24 * j:24 * j + 24 * m]), T.EG[:, V * j:V * j + V * m]
-            if t and PAR["tops"]:
-                src, rd = newest(t, 24 + 24 * j, 24 + 24 * j + 24 * m)
             ek = ["EG%d" % i for i in range(j, j + m)]
             if LOADS[t][j] == "a":
                 act(out, src, rd, ek, V * m * gat, scale=scale)
@@ -386,24 +389,24 @@ def rank_program(g, core, T, topo):
         if t == 0:
             for j in range(2):
                 b = [PS, PU][j]
-                for x in range(16):
-                    mm(B[b][0:48, x:384:16], T.EG[:, x::16], T.WD[:, 24 * j:24 * j + 24], True, True, ["EG0", "EG1", "WD"], ["#%d" % b], 48)
-                lin("va"[j], T.TE[0:48, V * j:V * j + V], B[b][0:48, 0:V], ["#%d" % b], ["TE%d" % j], V, 0.0)
+                for x in range(8):
+                    mm(B[b][0:48, x:384:8], T.EG[:, 8 * j + x::16], T.WD[:, :], True, True, ["EG0", "EG1", "WD"], ["#%d" % b], 48)
+                lin("va"[j], T.TE[0:48, :, 8 * j:8 * j + 8], B[b][0:48, 0:V], ["#%d" % b], ["TE%d" % j], V, 0.0)
             for j in range(2):
                 b = [PS, PL][j]
                 for i in range(3):
                     for h in range(2):
-                        mm(B[b][:, 72 * h + 24 * i:72 * h + 24 * i + 24], T.TE[0:48, V * j + 128 * i:V * j + 128 * i + 128],
-                           T.ID[0:48, 24 * h:24 * h + 24], True, True, ["TE%d" % j, "ID"], ["#%d" % b], 64)
-                ts(T.LI[:, :, 48 + 72 * j:120 + 72 * j], B[b][:, 0:144], 1536.0 + OB - E0, None, A.add, None, ["#%d" % b],
-                   ["EL%d%d" % (i, h) for i in range(3 * j, 3 * j + 3) for h in range(2)], 144)
+                        mm(B[b][:, 72 * h + 24 * i:72 * h + 24 * i + 24], T.TE[0:48, 24 * j + 8 * i:24 * j + 8 * i + 8, :],
+                           T.ID[0:48, 24 * h:24 * h + 24], True, True, ["TE0", "TE1", "ID"], ["#%d" % b], 64)
+                lin(PAR["el"][j], T.LI[:, :, 48 + 72 * j:120 + 72 * j], B[b][:, 0:144], ["#%d" % b],
+                    ["EL%d%d" % (i, h) for i in range(3 * j, 3 * j + 3) for h in range(2)], 144, 1536.0 + OB - E0)
             return
         for x in range(16):
             o = 15 + 6 + 2 * t - x
             mm(B[PL][:, 0:24 * m], T.WH[:, o:o + 128], T.EG[:, V * h + x:V * h + V * m:16], x == 0, x == 15, ek + ["WH"], ["#%d" % PL], 64)
         c = 48 + 24 * (5 + t)
-        ts(T.LI[:, h:h + m, c:c + 24], B[PL][:, 0:24 * m], 1536.0 + OB - E0, None, A.add, None, ["#%d" % PL],
-           ["EL%d%d" % (5 + t, i) for i in range(h, h + m)])
+        lin(PAR["el"][1 + t], T.LI[:, h:h + m, c:c + 24], B[PL][:, 0:24 * m], ["#%d" % PL], ["EL%d%d" % (5 + t, i) for i in range(h, h + m)],
+            64, 1536.0 + OB - E0)
 
     def unnamed(t):
         return T.RS[:, 528 * t + 1:528 * t + 24 * nsrc(t, 0):nsrc(t, 0)]
@@ -413,17 +416,17 @@ def rank_program(g, core, T, topo):
         if t == 0:
             tt(T.XB[:, :], src, T.OK[:, :], A.is_equal, rd + ["OK"], ["XB"], V * gat)
         else:
-            if PAR["tops"]:
-                src, rd = newest(t, 0, 24)
             act(T.XB[:, :], src, rd + ["MK"], ["XB"], V * gat, scale=T.MK[:, 6 + 2 * t:7 + 2 * t])
+        if t:
+            mm(B[PX][:, 0:24], T.NID[:, :], T.OH[:, :], True, False, ["XB", "NID", "OH"], ["#%d" % PX], 64)
         for b in range(3):
-            mm(B[PX][:, b:24:3], T.XB[:, 128 * b:128 * b + 128], T.NS[:, 8 * min(t, 1):8 * min(t, 1) + 8], True, True, ["XB", "NS"],
-               ["#%d" % PX], 64)
+            mm(B[PX][:, b:24:3], T.XB[:, 128 * b:128 * b + 128], T.NS[:, 8 * min(t, 1):8 * min(t, 1) + 8], t == 0, t == 0 or b == 2,
+               ["XB", "NS1" if t else "NS"], ["#%d" % PX], 64)
         if t == 0:
             ts(unnamed(0), B[PX][:, 0:24], 0.0, BIG, A.is_equal, A.mult, ["#%d" % PX, "RS0"], ["nm0"])
         else:
-            tt(T.NE[:, :], B[PX][:, 0:24], T.OC[:, :], A.not_equal, ["#%d" % PX, "OC"], ["NE"])
-            tt(unnamed(t), T.NE[:, :], unnamed(t - 1), A.mult, ["NE", "nm%d" % (t - 1), "RS%d" % (2 * t)], ["nm%d" % t])
+            op("a", lambda e: e.activation(T.NE[:, :], B[PX][:, 0:24], ActivationFunctionType.Abs, scale=BIG), ["#%d" % PX], ["NE"])
+            tt(unnamed(t), T.NE[:, :], unnamed(t - 1), A.min, ["NE", "nm%d" % (t - 1), "RS%d" % (2 * t)], ["nm%d" % t])
 
     ring = [0]
 
@@ -444,8 +447,8 @@ def rank_program(g, core, T, topo):
             act(T.G[:, V * s0:V * (s0 + n)], src, rd, gk, V * n * gat)
         for i in range(n):
             s, e = s0 + i, e0 + i
-            if eng == "a" and i % 2 == 0:
-                m = min(2, n - i)
+            if eng == "b" or (eng == "a" and i % 2 == 0):
+                m = min(2, n - i) if eng == "a" else 1
                 gs = T.G[:, V * s:V * (s + m)]
                 tt(gs, gs, YY[h][:, 0:m, 0:V], A.max, gk[i:i + m] + ["Y%d" % h, "Z%d" % h, "YS%d" % h], gk[i:i + m], V * m)
             for b in range(3):
@@ -466,9 +469,7 @@ def rank_program(g, core, T, topo):
         assert i == E, (t, h)
 
     def rows(p, a, b):
-        if p % 2 or not PAR["wide"]:
-            return T.S[24 * a:24 * b, 128 * p:128 * p + 128]
-        return T.SO[8 * a:8 * b, V * (p // 2):V * (p // 2) + V]
+        return T.S[24 * a:24 * b, 128 * p:128 * p + 128]
 
     def put(p, w, kinds):
         t, h = p // 2, p % 2
@@ -494,7 +495,6 @@ def rank_program(g, core, T, topo):
         rk = ["RS%d" % p] + (["nm%d" % t] if h == 0 else [])
         op("v", lambda e: e.tensor_tensor_scan(sc, reset(t, h), d, 0.0, A.add, A.min), rk + [dk], ["SC%d" % h], n)
         x = T.SC[:, 264 * h + E - 1:264 * h + n:E]
-        s = T.S[:, 128 * p:128 * p + 128] if p < 7 else None
         ps, pk = B[PS], "#%d" % PS
         if p == 7:
             ts(T.SG[:, :], x, K, 3456.0, A.mult, A.add, ["SC1"], ["SG"])
@@ -510,19 +510,11 @@ def rank_program(g, core, T, topo):
         terms = [(p, 0, T.KID, "KID"), (p, 0, T.NID, "NID"), (8 + p, 3, T.NID, "NID"), (p + 2, 0, T.ID, "ID"), (p + 2, 1, T.KID, "KID"),
                  (p + 2, 2, T.KID, "KID"), (p + 2, 3, T.ID, "ID")]
         terms += [(p + 2, 2, T.NID, "NID")] if t == 2 else []
-        nb = 1 if h or not PAR["wide"] else 3
-        u = 24 // nb
-        if nb == 3:
-            mm(ps[0:32, 0:V], T.TC[:, 0:32], T.D[:, 0:V], True, False, ["TCz", "D0"], [pk], V)
         for i, (sl, kind, m, mk) in enumerate(terms):
             o = 72 + 96 * sl - 24 * kind
-            for b in range(nb):
-                mm(ps[0:4 * u, 128 * b:128 * b + 128], T.TC[:, o + b:o + 96:nb], m[:, :], i == 0 and nb == 1,
-                   i == len(terms) - 1 and b == nb - 1, ["TC%d" % sl if sl < 8 else "TG%d" % p, mk], [pk], 128)
-        c0 = 32 if nb == 1 else 28
-        c = c0 + (t == 2)
-        ts(rows(p, 0, 4), ps[0:4 * u, 0:128 * nb], T.KC[0:4 * u, c:c + 1], T.KC[0:4 * u, c0 + 2:c0 + 3], A.add, A.min,
-           [pk, "c%d" % c, "c%d" % (c0 + 2)], ["S%d" % p], 128 * nb)
+            mm(ps[0:96, 0:128], T.TC[:, o:o + 96], m[:, :], i == 0, i == len(terms) - 1, ["TC%d" % sl if sl < 8 else "TG%d" % p, mk], [pk], 128)
+        c = 32 + (t == 2)
+        ts(rows(p, 0, 4), ps[0:96, 0:128], T.KC[0:96, c:c + 1], T.KC[0:96, 34:35], A.add, A.min, [pk, "c%d" % c, "c34"], ["S%d" % p], 128)
         put(p, (t + 1) % 2, 3)
         if h or not PAR["late"]:
             thresholds(p + 2)
@@ -535,9 +527,6 @@ def rank_program(g, core, T, topo):
     tops()
     dma("g", [(T.own[:, :], T.pts[:, :])], ["TE0"], ["own"], 4.0)
     gcopy(T.ownf[:, :], T.own[:, :], ["own"], ["ownf"], 768)
-    ts(T.LA[:, :], T.L[:, 72:144], 3071.5, float(TM), A.is_lt, A.mult, ["L", "Ld", "EG0"], ["LA"])
-    tt(T.LB[:, :], T.L[:, 72:144], T.LA[:, :], A.add, ["LA"], ["LB"], 144)
-    ts(T.LK[:, :], T.LB[:, :], -3072.0, None, A.add, None, ["LB"], ["LK"])
     for t in range(RO):
         if t:
             gains(t - 1, 1)
@@ -575,7 +564,7 @@ def rank_program(g, core, T, topo):
     last = [(T.yp[9:16 * rank:16, V:2 * V], T.land3[0:rank])] if rank else []
     last += [(T.yp[16 * rank + 25::16, V:2 * V], T.land3[rank + 1:N])] if rank < N - 1 else []
     dma("s", last, [], ["+yp"])
-    raw("g", lambda e: e.wait_ge(T.sem.sent, 3 * len(every) + sum(len(m) for m in dm)), [], [], 0.0)
+    raw("g", lambda e: e.wait_ge(T.sem.sent, 4 * len(every) + sum(len(m) for m in dm)), [], [], 0.0)
     emit(g, T, ops)
 
 
@@ -584,7 +573,7 @@ def depends(ops):
     deps = []
     for i, o in enumerate(ops):
         d = set()
-        if o["q"] in "gs" or (o["q"] == "a" and o["kind"] == "dma"):
+        if o["q"] in "gs" or (o["q"] == "a" and o["kind"] != "c"):
             d.update(tail.get(o["q"], []))
             tail[o["q"]] = [i]
         for k in o["rd"] + o["wr"]:

from concourse.bass import DstId, RemoteDMATransfer
from concourse.mybir import AluOpType, ActivationFunctionType, AxisListType

N, V, RO = 8, 384, 4
K = 4096.0
E0, OB, TM, WW = 384, 392, 3464, 3849
RING = 14
BIG = 8192.0
PLAN = ['a1 v1 a1 b2 v1 a1 v1', 'a1 b2 b2 a1 v1', 'v1 v1 b3 v1 v1 v1 v1', 'a1 a1 b2 b2 a1 a1', 'v1 v1 v1 b3 a1 v1 a1 v1',
        'a1 b2 a2 v1 a1 v1 a1', 'v1 v1 v1 a2 a2 v1 v1 v1 v1', 'a2 a2 a2 a1 a1 a1 a1']
LOADS = ["va", "a", "va", "aa"]
PAR = {"mq": "a", "el": "vaaaa", "late": 0, "gat": 1.5, "cyc": 0.00092, "fix": 0.07, "pe": 0.00045, "dma": 1.7, "put": 3.0, "slack": 0.12,
       "arr": 0.8, "arrf": 3.6, "copies": "ggggggggs", "sem": 0.13, "turns": 3}

f32, f16, bf16, i32, u16 = "float32", "float16", "bfloat16", "int32", "uint16"
SCRATCH = {"stage": ("dram", [8, 128, 36], i32), "land": ("dram", [8, 128, 36], i32), "hand": ("dram", [128, 36], i32),
           "stagl": ("dram", [8, 128, 24], i32), "landl": ("dram", [8, 128, 24], i32), "handl": ("dram", [128, 24], i32),
           "gst": ("dram", [8, 128, 24], f32), "land2": ("dram", [8, 128, 24], f32), "hand2": ("dram", [128, 24], f32),
           "land3": ("dram", [8, 128, 3], f32), "hand3": ("dram", [128, 3], f32),
           "LI": ("sbuf", [128, 2, 264], u16), "SL": ("sbuf", [128, 8, 16], f32), "WN": ("sbuf", [128, 8, 16], f32),
           "RW": ("sbuf", [128, 4, 16], f32), "TE": ("sbuf", [128, 48, 16], f16)}
for _d, _l in [
    (f16, "natf 768 natm 768 D 768 EG 768 TC 1512 UT 1024 ID 128 ZF 128 ZM 128 Z1 128 Z2 128 XB 384 OH 24"),
    (f32, "ownf 768 W0 3856 W1 3856 KF 8 KC 40 CK 128 GI 128 GM 8 C16 64 CV 384 M16 64 MK 16 SS 32 OK 384 "
          "SC 528 MC 528 S 896 YS 768 G %d SG 24 B1 128 B2 128 OC 24 NE 24" % (V * RING)),
    (bf16, "BP 128 SW 128 ST 256 SY 384 KID 128 NID 128 WH 160 WD 48 NS 16 ZE 512 RS 2112 SZ 512"),
    (i32, "own 768 nat 768 L 144 KI 2 KJ 8 MQ 528"), (u16, "LJ 48")]:
    _w = _l.split()
    for _i in range(0, len(_w), 2):
        SCRATCH[_w[_i]] = ("sbuf", [128, int(_w[_i + 1])], _d)
for _b in range(2):
    SCRATCH["Y%dp" % _b] = ("psum", [128, 2, 512], f32)
for _b in range(2, 6):
    SCRATCH["B%dp" % _b] = ("psum", [128, 512], f32)
SEMAPHORES = ["cv", "ca", "cp", "cg", "sent", "arr", "arrf", "arr2", "arr3", "arrl", "h0", "h1", "h2", "hl"] + ["d%d" % _i for _i in range(60)]

A = AluOpType
IDENT = ActivationFunctionType.Identity


def routes(T, topo, core):
    cores = list(T.cores)
    direct = [q for q in range(N) if cores[q] != core and topo.may_write(core, cores[q])]
    far = [q for q in range(N) if cores[q] != core and q not in direct]
    able = [c for c in topo.cores_of(core) if c not in cores and all(topo.may_write(c, cores[q]) for q in far)]
    turn = len([q for q in direct if q < cores.index(core)])
    return direct, [(able[(j + turn) % len(able)], q) for j, q in enumerate(far)]


def bits(es):
    return sum(1 << e for e in es)


def dst(topo, d, s):
    rid, pid = topo.addr(d, s)
    return DstId(rid=rid, pnc=pid)


def helper_program(g, core, T, topo, rank, q):
    to = T.cores[q]
    es = topo.engines(core, to)
    rid, pid = topo.addr(to, core)
    for sem, n, out, in_, arr in [(T.sem.h0, 2, T.land, T.hand, T.sem.arrf), (T.sem.hl, 2, T.landl, T.handl, T.sem.arrl),
                                  (T.sem.h1, 2, T.land2, T.hand2, T.sem.arr2), (T.sem.h2, 4, T.land3, T.hand3, T.sem.arr3)]:
        g.wait_ge(sem, n)
        g.remote_dma(out[rank], in_[:, :], arr, T.sem.sent, pid, rid, bits(es))
    g.wait_ge(T.sem.sent, 4 * len(es))


def direct_masks(topo, core, cores, direct):
    es = topo.engines(core, cores[direct[0]])
    return [es[0:4], es[4:6], es[6:8]]


def arrivals(T, topo, rank):
    cores = list(T.cores)
    near = far = 0
    for s in range(N):
        if s != rank:
            direct, helpers = routes(T, topo, cores[s])
            if rank in direct:
                near += len(direct_masks(topo, cores[s], cores, direct)[direct.index(rank)])
            else:
                far += len(topo.engines([c for c, q in helpers if q == rank][0], cores[rank]))
    return near, far


def rank_program(g, core, T, topo):
    rank = T.rank_of(core)
    if rank is None:
        for r, c in enumerate(T.cores):
            if c in topo.cores_of(core):
                for hc, q in routes(T, topo, c)[1]:
                    if hc == core:
                        helper_program(g, core, T, topo, r, q)
        return
    cores = list(T.cores)
    direct, helpers = routes(T, topo, core)
    waves = [sorted(direct + [rank]), [q for hc, q in helpers]]
    ops = []
    cyc, gat = PAR["cyc"], PAR["gat"]

    def op(q, fn, rd, wr, n=64, kind="c", cost=None):
        ops.append({"q": q, "fn": fn, "rd": rd, "wr": wr, "kind": kind, "cost": PAR["fix"] + max(n, 64) * cyc if cost is None else cost})

    def raw(q, fn, rd, wr, cost):
        op(q, fn, rd, wr, kind="raw", cost=cost)

    def dma(q, pairs, rd, wr, cost=None):
        op(q, pairs, rd, wr, kind="dma", cost=PAR["dma"] if cost is None else cost)

    def ts(out, in0, s1, s2, o0, o1, rd, wr, n=64):
        if o1 is None:
            op("v", lambda e: e.tensor_scalar(out, in0, s1, None, o0), rd, wr, n)
        else:
            op("v", lambda e: e.tensor_scalar(out, in0, s1, s2, o0, o1), rd, wr, n)

    def tt(out, a, b, o, rd, wr, n=64):
        op("v", lambda e: e.tensor_tensor(out, a, b, o), rd, wr, n)

    def ms(ap, c, wr, n=64):
        op("v", lambda e: e.memset(ap, c), [], wr, n)

    def mm(out, lhsT, rhs, start, stop, rd, wr, n):
        op("p", lambda e: e.matmul(out, lhsT, rhs, start, stop), rd, wr, cost=0.01 + n * PAR["pe"])

    def act(out, in_, rd, wr, n=64, bias=0.0, scale=1.0):
        op("a", lambda e: e.activation(out, in_, IDENT, bias=bias, scale=scale), rd, wr, n)

    def lin(q, out, in_, rd, wr, n, bias):
        if q == "a":
            act(out, in_, rd, wr, n, bias=bias)
        else:
            ts(out, in_, bias, None, A.add, None, rd, wr, n)

    def iota(out, pat, base, cm, wr, n, flt=True):
        if flt:
            op("g", lambda e: e.iota(out, pat, base, cm, allow_small_or_imprecise_dtypes=True), [], wr, cost=0.13 + 2 * n * cyc)
        else:
            op("g", lambda e: e.iota(out, pat, base, cm), [], wr, cost=0.13 + 2 * n * cyc)

    def sel(out, in_, pat, cmp, c, base, cm, rd, wr, n):
        op("g", lambda e: e.affine_select(out, in_, pat, cmp, c, base, cm), rd, wr, cost=0.17 + 2 * n * cyc)

    def mark(out, pat, c, base, wr, n, parts=128):
        sel(out, T.ZE[0:parts, 0:n], pat, A.not_equal, c, base, -1, ["ZE"], wr, n)

    def fill(out, zeros, c, wr, n):
        sel(out, zeros, [[0, n]], A.is_gt, c, 0, 0, ["ZE"], wr, n)

    def gcopy(out, in_, rd, wr, n):
        sel(out, in_, [[0, n]], A.is_ge, 0.0, 0, 0, rd, wr, n)

    B = {b: T["B%dp" % b] for b in range(2, 6)}
    YY = [T.Y0p, T.Y1p]
    W = [T.W0, T.W1]
    DB, PS, PU, PL, PX = [2, 3], 4, 5, 5, 5

    def nsrc(t, h):
        return 8 + t - h

    def reset(t, h):
        o = 264 * (2 * t + h)
        return T.RS[:, o:o + 24 * nsrc(t, h)]

    other = [q for q in range(N) if q != rank]
    dma("s", [(T.stage[q], T.pts[16 * q:16 * q + 6, :]) for q in other[0:4]], [], ["st0"])
    dma("a", [(T.stage[q], T.pts[16 * q:16 * q + 6, :]) for q in other[4:7]], [], ["st1"])
    dma("s", [(T.stagl[:, 0:32, :], T.ld[:, :]), (T.stagl[:, 64:80, :], T.xs[:, :]), (T.stagl[:, 96:128, :], T.pts[6::16, :])], [], ["sl0"])
    dma("a", [(T.stagl[:, 32:64, :], T.cp[:, :]), (T.stagl[:, 80:96, :], T.ys[:, :])], [], ["sl1"])
    dma("a", [(T.land[rank], T.pts[16 * rank:16 * rank + 6, :])], [], ["landown"])
    st = ["st0", "st1"]
    ms(T.ZE[:, :], 0.0, ["ZE"], 256)
    ms(T.nat[0:64, :], 1536, ["nat0", "nat1"], 768)
    iota(T.KI[:, 0:1], [[1, 1]], 0, 1, ["KI"], 1, False)
    iota(T.CK[0:64, :], [[1, 64], [0, 2]], 0, -1, ["CK"], 128)
    iota(T.SL[:, :, 0:12], [[0, 8], [1, 6], [0, 2]], 2, 0, ["+SL"], 96)
    iota(T.SL[:, :, 12:16], [[0, 8], [0, 2], [1, 2]], 0, 0, ["+SL"], 32)
    iota(T.WN[:, :, 0:12], [[0, 8], [1, 6], [100, 2]], -97, 0, ["+WN"], 96)
    iota(T.WN[:, :, 12:16], [[0, 8], [100, 2], [1, 2]], -99, 0, ["+WN"], 32)
    dm = direct_masks(topo, core, cores, direct)
    every = topo.engines(core, helpers[0][0])
    inner = [e for e in every if e not in topo.engines(core, cores[direct[0]])]

    def alltoall(src, hand, hsem, land, sem):
        tr = [RemoteDMATransfer(dst_ids=[dst(topo, hc, core)], dma_engine_mask=bits(inner[4 * (j % 2) + j // 2:4 * (j % 2) + 4:2]), remote_sem=hsem,
                                src=src[q], dst=hand[:, :]) for j, (hc, q) in enumerate(sorted(helpers, key=lambda x: topo.die(x[0])))]
        return tr + [RemoteDMATransfer(dst_ids=[dst(topo, cores[q], core)], dma_engine_mask=bits(dm[j]), remote_sem=sem,
                                       src=src[q], dst=land[rank]) for j, q in enumerate(direct)]
    tr0 = alltoall(T.stage, T.hand, T.sem.h0, T.land, T.sem.arr)
    raw("g", lambda e: e.remote_dma_fused(tr0, local_sem=T.sem.sent), st, ["away"], 3.0)
    iota(T.GI[:, :], [[1, 8], [0, 16]], 0, 0, ["GI"], 128)
    iota(T.C16[:, :], [[0, 4], [1, 16]], 0, 0, ["C16"], 64)
    trl = alltoall(T.stagl, T.handl, T.sem.hl, T.landl, T.sem.arrl)
    raw("g", lambda e: e.remote_dma_fused(trl, local_sem=T.sem.sent), ["sl0", "sl1"], ["awayl"], 1.0)
    dma("s", [(T.landl[rank], T.stagl[rank])], ["sl0", "sl1"], ["listown"])
    near, far = arrivals(T, topo, rank)

    col = [T.KC[:, j:j + 1] for j in range(40)]
    for w in range(2):
        for k, q in enumerate(waves[w]):
            act(T.KC[32 * k:32 * k + 32, w:w + 1], T.ZE[32 * k:32 * k + 32, 0:1], ["ZE"], ["+q%d" % w], bias=float(q))
    for j, (s, s2, o, o2) in enumerate([(15, None, A.bitwise_and, None), (4, None, A.arith_shift_right, None), (31, None, A.bitwise_and, None),
                                        (2, 7, A.arith_shift_right, A.bitwise_and), (1, 1, A.arith_shift_right, A.bitwise_and)]):
        ts(T.KJ[:, j:j + 1], T.KI[:, 0:1], s, s2, o, o2, ["KI"], ["KJ%d" % j])
    op("v", lambda e: e.tensor_copy(T.KF[:, 0:5], T.KJ[:, 0:5]), ["KJ%d" % j for j in range(5)], ["KF"])
    kr, kg, k31, kj, kh = [T.KF[:, j:j + 1] for j in range(5)]
    ts(T.Z1[0:64, :], T.CK[0:64, :], 0.0, None, A.is_equal, None, ["CK"], ["Z1"], 128)
    ts(T.Z2[0:64, :], T.CK[0:64, :], 2.0, None, A.is_equal, None, ["CK"], ["Z2"], 128)
    tt(T.ZF[0:64, :], T.Z1[0:64, :], T.Z2[0:64, :], A.subtract, ["Z1", "Z2"], ["ZF"], 256)
    act(T.ZM[0:64, :], T.ZF[0:64, :], ["ZF"], ["ZMa"], 128, scale=-K)
    for h in range(2):
        act(T.natm[64:65, V * h:V * h + V], T.ZE[64:65, 0:V], ["ZE"], ["+ones"], V, bias=1.0)
    for a, step, c, rd, wr in [(0, 2, 0.0, "ZE", "+ZN"), (1, 2, -2048.0, "ZE", "+ZN"), (0, 32, 1537.0, "ZN", "+ZM"), (2, 32, 1537.0, "ZN", "+ZM"),
                               (1, 32, -511.0, "ZN", "+ZM"), (3, 32, -511.0, "ZN", "+ZM"), (28, 32, 1.0, "ZN", "+ZM")]:
        act(T.ZM[64:65, a::step], T.ZE[64:65, 0:128 // step], [rd], [wr], bias=c)
    ms(T.WN[:, :, 7], -100.0, ["WN"])
    ts(T.B1[:, :], T.SL[:, :, :], kj, K, A.is_ge, A.mult, ["SL", "KF"], ["B1"], 128)
    ts(T.B2[:, :], T.WN[:, :, :], kj, None, A.is_equal, None, ["WN", "KF"], ["B2"], 128)
    tt(T.BP[:, :], T.B1[:, :], T.B2[:, :], A.add, ["B1", "B2"], ["BP"], 256)
    act(col[2], kh, ["KF"], ["c2"], bias=1.0, scale=-1.0)
    act(T.SW[:, :], T.BP[:, :], ["BP", "c2"], ["SW"], 128, scale=col[2])
    ts(T.M16[:, :], T.C16[:, :], kr, None, A.is_equal, None, ["C16", "KF"], ["M16"])
    act(col[4], T.M16[:, 7:8], ["M16"], ["c4"], bias=-1537.0 * K, scale=K - 1.0)
    ts(col[5], kj, 6.0, K, A.is_lt, A.mult, ["KF"], ["c5"])
    ts(col[6], k31, 28.0, -1536.0 * K, A.is_equal, A.mult, ["KF"], ["c6"])
    act(col[7], col[5], ["c2", "c5", "c6"], ["c7"], scale=col[2], bias=col[6])
    act(col[8], col[5], ["KF", "c5", "c6"], ["c8"], scale=kh, bias=col[6])
    for w in range(2):
        ts(T.B1[:, :], T.GI[:, :], col[w], kh, A.is_equal, A.mult, ["GI", "q%d" % w, "KF"], ["B1"], 128)
        tt(T.ST[:, 128 * w:128 * w + 128], T.B1[:, :], T.BP[:, :], A.mult, ["B1", "BP"], ["ST%d" % w], 256)
        for h in range(2):
            o = 256 * w + 128 * h
            ts(T.SZ[:, o:o + 128], T.GI[:, :], col[w], col[7 + h], A.is_equal, A.mult, ["GI", "q%d" % w, "c%d" % (7 + h)], ["+SZ"], 128)
    act(T.MK[:, :], T.M16[:, 0:16], ["M16"], ["MK"], scale=1.0 / K)
    for w in range(2):
        act(W[w][:, E0:OB], T.ZE[:, 0:8], ["ZE"], ["W%de" % w], bias=-1537.0 * K)
        act(W[w][:, WW - 1:WW + 7], T.ZE[:, 0:8], ["ZE"], ["W%df" % w], bias=-1537.0 * K)
    for j in range(3):
        act(T.TC[:, 504 * j:504 * j + 504], T.ZE[:, 0:504], ["ZE"], ["+TCz"], 504)

    def resets(p):
        n = nsrc(p // 2, p % 2)
        sel(reset(p // 2, p % 2), T.ZE[:, 0:24 * n], [[0, 24], [1, n]], A.is_gt, BIG, 0, 0, ["ZE"], ["RS%d" % p], 24 * n)

    mark(T.WD[:, 0:16], [[1, 2], [16, 8]], 1.0, 12, ["+WD"], 16)
    mark(T.WD[:, 16:48], [[2, 4], [16, 8]], 1.0, 0, ["+WD"], 32)
    mark(T.ID[:, :], [[1, 128]], 1.0, 0, ["ID"], 128)
    iota(T.RW[:, :, 0:12], [[0, 4], [0, 6], [-2, 2]], 1, 0, ["+RW"], 48)
    iota(T.RW[:, :, 12:16], [[0, 4], [-2, 2], [0, 2]], 1, 0, ["+RW"], 16)
    iota(T.CV[:, :], [[4096, 384]], -1536 * 4096, 0, ["CV"], 384)
    for t, a, b, c in [(0, 8, 12, 0.0), (1, 10, 12, 0.0), (0, 6, 7, 1 + 1 / K), (1, 8, 9, 1 + 1 / K), (2, 10, 11, 1 + 1 / K), (3, 13, 14, -1.0)]:
        act(T.RW[:, t, a:b], T.ZE[:, 0:b - a], ["RW"], ["+RX"], bias=c)
    tt(T.B2[:, 0:64], T.M16[:, :], T.RW[:, :, :], A.mult, ["M16", "RW", "RX"], ["B2"], 128)
    ts(T.GM[:, :], T.C16[:, 0:8], kg, None, A.is_equal, None, ["C16", "KF"], ["GM"])
    for t in range(4):
        op("v", lambda e, t=t: e.tensor_reduce(col[12 + t], T.B2[:, 16 * t:16 * t + 16], AxisListType.X, A.add), ["B2"], ["c%d" % (12 + t)])
    act(col[16], col[15], ["c15"], ["c16"], scale=1.0 / K)
    for t, c in enumerate([12, 13, 14, 16]):
        act(T.SS[:, 8 * t:8 * t + 8], T.GM[:, :], ["GM", "c%d" % c], ["SS%d" % t], scale=col[c])
    ts(T.NS[:, 0:8], T.SS[:, 0:8], 0.0, None, A.max, None, ["SS0"], ["NS"])
    act(T.NS[:, 8:16], T.GM[:, :], ["GM"], ["NS1"])
    act(col[17], kg, ["KF"], ["c17"], scale=384.0 * K)
    act(T.OK[:, :], T.CV[:, :], ["CV", "c17"], ["OK"], 384, bias=col[17])
    act(T.KID[:, :], T.ID[:, :], ["ID"], ["KID"], 128, scale=K)
    act(T.NID[:, :], T.ID[:, :], ["ID"], ["NID"], 128, scale=-1.0)

    def later():
        fill(T.KC[:, 32:34], T.ZE[:, 0:2], -K, ["c32", "c33"], 2)
        for j, c in [(32, -1.0), (33, 1921.0 - K)]:
            sel(col[j], col[j], [[0, 1]], A.is_ge, c, 47, -1, ["c%d" % j], ["c%d" % j], 1)
        sel(T.KC[:, 32:34], T.KC[:, 32:34], [[0, 2]], A.is_ge, K + 1535.0, 71, -1, ["c32", "c33"], ["c32", "c33"], 2)
        fill(col[34], T.ZE[:, 0:1], 2.0 ** 24, ["c34"], 1)
        sel(col[34], col[34], [[0, 1]], A.is_ge, 3456.0, 71, -1, ["c34"], ["c34"], 1)
        mark(T.SY[0:32, :], [[1, 3], [3, 8], [0, 16]], K, 0, ["SY"], 384, 32)

    def latest():
        mark(T.WH[:, :], [[1, 160]], 1.0, -15, ["WH"], 160)
        iota(T.OC[:, :], [[384, 8], [128, 3]], -1536, 1, ["OC"], 24)
        gcopy(T.OH[:, :], T.OC[:, :], ["OC"], ["OH"], 24)
        for p in range(2, 8):
            resets(p)

    def tc(s):
        o = 72 + 96 * s
        return T.TC[:, o:o + 24]

    def block(w, q, k, b, eng):
        c0 = OB + V * q
        bank = B[b][:, 0:V] if b in B else YY[b - 6][:, 1, 0:V]
        mm(bank, T.SW[32 * k:32 * k + 32, :], T.D[32 * k:32 * k + 32, V * w:V * w + V], True, True, ["D%d" % w, "SW"], ["#%d" % b], V)
        lin(eng, T.W0[:, c0:c0 + V], bank, ["#%d" % b, "c4"], ["W0p%d" % q, {2: "X0", 3: "X1", 6: "Z0", 7: "Z1"}[b]], V, col[4])

    def copy1(q, by):
        c0 = OB + V * q
        if by == "g":
            gcopy(T.W1[:, c0:c0 + V], T.W0[:, c0:c0 + V], ["W0p%d" % q], ["W1p%d" % q], V)
        else:
            dma("s", [(T.W1[:, c0:c0 + V], T.W0[:, c0:c0 + V])], ["W0p%d" % q], ["W1p%d" % q], 3.0)

    def shared(w):
        d = T.D[:, V * w:V * w + V]
        mm(B[PU][:, 0:V], T.ST[:, 128 * w:128 * w + 128], d, w == 0, w == 1, ["D%d" % w, "ST%d" % w], ["#%d" % PU], V)
        for h in range(2):
            mm(YY[h][:, 0, 0:V], T.SZ[:, 256 * w + 128 * h:256 * w + 128 * h + 128], d, w == 0, w == 1, ["D%d" % w, "SZ"], ["Y%d" % h], V)

    def wave(w):
        cs = slice(V * w, V * w + V)
        dma("s", [(T.nat[16 * k:16 * k + 12, cs], T.land[q]) for k, q in enumerate(waves[w])], ["landown"], ["nat%d" % w], 2.2)
        act(T.natf[0:64, cs], T.nat[0:64, cs], ["nat%d" % w], ["natf%d" % w], V, bias=-1536.0)
        ts(T.natm[0:64, cs], T.nat[0:64, cs], 3071.5, None, A.is_gt, None, ["nat%d" % w], ["natm%d" % w], V)
        mm(B[PS][:, 0:V], T.ZF[0:64, :], T.natf[0:64, cs], True, False, ["natf%d" % w, "ZF"], ["#%d" % PS], V)
        mm(B[PS][:, 0:V], T.ZM[0:65, :], T.natm[0:65, cs], False, True, ["natm%d" % w, "ZM", "ZMa", "ones"], ["#%d" % PS], V)
        ts(T.D[:, cs], B[PS][:, 0:V], 0.0, 2048.0, A.max, A.min, ["#%d" % PS], ["D%d" % w], V)

    raw("s", lambda e: e.wait_ge(T.sem.arr, near), ["away"], [], PAR["arr"])
    wave(0)
    for k, q in enumerate(waves[0]):
        block(0, q, k, [2, 3, 6, 7][k], "av"[k % 2])
    shared(0)
    resets(0)
    resets(1)
    later()
    for by, q in zip(PAR["copies"], waves[0]):
        copy1(q, by)
    raw("s", lambda e: e.wait_ge(T.sem.arrf, far), ["away"], ["far"], PAR["arrf"])
    wave(1)
    raw("s", lambda e: e.wait_ge(T.sem.arrl, near + far), ["awayl"], [], PAR["arrf"])
    dma("s", [(T.L[:, 96:144], T.landl[:, 0:32, :])], ["listown"], ["Ld"], 2.2)
    dma("s", [(T.L[:, 0:24], T.landl[:, 80:96, :]), (T.L[:, 24:48], T.landl[:, 32:64:2, :]), (T.L[:, 48:72], T.landl[:, 64:80, :]),
              (T.L[:, 72:96], T.landl[:, 33:64:2, :])], ["listown"], ["L"], 2.8)
    for k, q in enumerate(waves[1]):
        block(1, q, k, [2, 3, 6, 7][k], "av"[k % 2])
    shared(1)
    lin("a", T.W0[:, TM:TM + V], B[PU][:, 0:V], ["#%d" % PU, "c4"], ["W0p8"], V, col[4])
    ts(T.LJ[:, :], T.L[:, 96:144], float(OB - E0), None, A.add, None, ["Ld", "D1"], ["LJ"])
    ts(T.LI[:, :, 0:48], T.L[:, 0:96], float(OB - E0), None, A.add, None, ["L", "D1"], ["LI"], 96)
    for by, q in zip(PAR["copies"][4:], waves[1] + [8]):
        copy1(q, by)
    latest()

    def wkeys(t, full):
        w = "W%d" % (t % 2)
        return [w + "p%d" % q for q in range(9 if full else 8)] + [w + "e", w + "o"] + ([w + "f", w + "t"] if full else [])

    def window(t, full):
        return W[t % 2][:, E0:WW] if full else W[t % 2][:, E0:TM]

    def tops():
        for h in range(2):
            for b in range(3):
                for w in range(2):
                    o = 256 * w + 128 * h
                    mm(B[PU][:, 24 * h + b:24 * h + 24:3], T.D[:, V * w + 128 * b:V * w + 128 * b + 128], T.SZ[:, o:o + 128:16], w == 0, w == 1,
                       ["D%d" % w, "SZ"], ["#%d" % PU], 64)
        for h in range(2):
            act(tc(h), B[PU][:, 24 * h:24 * h + 24], ["#%d" % PU, "TCz"], ["TC%d" % h], scale=1.0 / K)

    def thresholds(p):
        h = p % 2
        u = T.UT[0:24, 128 * p:128 * p + 128]
        twice = "a2" in PLAN[p]
        if p > 1:
            mm(B[PU][0:24, 0:128], tc(p), T.ID[:, :], True, True, ["TC%d" % p, "ID"], ["#%d" % PU], 128)
            act(u, B[PU][0:24, 0:128], ["#%d" % PU], ["UT%d" % p], 128)
        for b in range(3 if p > 1 else 0):
            mm(YY[h][:, 0, 128 * b:128 * b + 128], T.SY[0:24, 128 * b:128 * b + 128], u, True, True, ["UT%d" % p, "SY"], ["+Y%d" % h], 128)
        for b in range(3 if p > 1 and twice else 0):
            mm(YY[h][:, 1, 128 * b:128 * b + 128], T.SY[0:24, 128 * b:128 * b + 128], u, True, True, ["UT%d" % p, "SY"], ["+Z%d" % h], 128)
        for w in range(2 if p < 2 and twice else 0):
            mm(YY[h][:, 1, 0:V], T.SZ[:, 256 * w + 128 * h:256 * w + 128 * h + 128], T.D[:, V * w:V * w + V], w == 0, w == 1,
               ["D%d" % w, "SZ"], ["Z%d" % h], V)
        if "v" in PLAN[p]:
            act(T.YS[:, V * h:V * h + V], YY[h][:, 0, 0:V], ["Y%d" % h], ["YS%d" % h], V)

    def edges(t, h=0):
        rd = wkeys(t, True) + ["LJ", "MK"]
        scale = T.MK[:, 6 + 2 * t:7 + 2 * t] if t else 1.0 / K
        m = 3 - len(LOADS[t])
        if m == 2 and h:
            return
        for j in ([h] if t else [0, 1]):
            src, out = window(t, True).indirect(T.LJ[:, 24 * j:24 * j + 24 * m]), T.EG[:, V * j:V * j + V * m]
            ek = ["EG%d" % i for i in range(j, j + m)]
            if LOADS[t][j] == "a":
                act(out, src, rd, ek, V * m * gat, scale=scale)
            else:
                ts(out, src, scale, None, A.mult, None, rd, ek, V * m * gat)
        if t == 0:
            for j in range(2):
                b = [PS, PU][j]
                for x in range(8):
                    mm(B[b][0:48, x:384:8], T.EG[:, 8 * j + x::16], T.WD[:, :], True, True, ["EG0", "EG1", "WD"], ["#%d" % b], 48)
                lin("va"[j], T.TE[0:48, :, 8 * j:8 * j + 8], B[b][0:48, 0:V], ["#%d" % b], ["TE%d" % j], V, 0.0)
            for j in range(2):
                b = [PS, PL][j]
                for i in range(3):
                    for h in range(2):
                        mm(B[b][:, 72 * h + 24 * i:72 * h + 24 * i + 24], T.TE[0:48, 24 * j + 8 * i:24 * j + 8 * i + 8, :],
                           T.ID[0:48, 24 * h:24 * h + 24], True, True, ["TE0", "TE1", "ID"], ["#%d" % b], 64)
                lin(PAR["el"][j], T.LI[:, :, 48 + 72 * j:120 + 72 * j], B[b][:, 0:144], ["#%d" % b],
                    ["EL%d%d" % (i, h) for i in range(3 * j, 3 * j + 3) for h in range(2)], 144, 1536.0 + OB - E0)
            return
        for x in range(16):
            o = 15 + 6 + 2 * t - x
            mm(B[PL][:, 0:24 * m], T.WH[:, o:o + 128], T.EG[:, V * h + x:V * h + V * m:16], x == 0, x == 15, ek + ["WH"], ["#%d" % PL], 64)
        c = 48 + 24 * (5 + t)
        lin(PAR["el"][1 + t], T.LI[:, h:h + m, c:c + 24], B[PL][:, 0:24 * m], ["#%d" % PL], ["EL%d%d" % (5 + t, i) for i in range(h, h + m)],
            64, 1536.0 + OB - E0)

    def unnamed(t):
        return T.RS[:, 528 * t + 1:528 * t + 24 * nsrc(t, 0):nsrc(t, 0)]

    def stores(t):
        src, rd = window(t, True).indirect(T.LI[:, 1, 0:24]), wkeys(t, True) + ["LI"]
        if t == 0:
            tt(T.XB[:, :], src, T.OK[:, :], A.is_equal, rd + ["OK"], ["XB"], V * gat)
        else:
            act(T.XB[:, :], src, rd + ["MK"], ["XB"], V * gat, scale=T.MK[:, 6 + 2 * t:7 + 2 * t])
        if t:
            mm(B[PX][:, 0:24], T.NID[:, :], T.OH[:, :], True, False, ["XB", "NID", "OH"], ["#%d" % PX], 64)
        for b in range(3):
            mm(B[PX][:, b:24:3], T.XB[:, 128 * b:128 * b + 128], T.NS[:, 8 * min(t, 1):8 * min(t, 1) + 8], t == 0, t == 0 or b == 2,
               ["XB", "NS1" if t else "NS"], ["#%d" % PX], 64)
        if t == 0:
            ts(unnamed(0), B[PX][:, 0:24], 0.0, BIG, A.is_equal, A.mult, ["#%d" % PX, "RS0"], ["nm0"])
        else:
            op("a", lambda e: e.activation(T.NE[:, :], B[PX][:, 0:24], ActivationFunctionType.Abs, scale=BIG), ["#%d" % PX], ["NE"])
            tt(unnamed(t), T.NE[:, :], unnamed(t - 1), A.min, ["NE", "nm%d" % (t - 1), "RS%d" % (2 * t)], ["nm%d" % t])

    ring = [0]

    def call(t, h, eng, e0, n):
        E = nsrc(t, h)
        full = e0 < 2 - h
        if ring[0] % RING + n > RING:
            ring[0] += RING - ring[0] % RING
        s0 = ring[0] % RING
        ring[0] += n
        c = 24 * (e0 + h)
        src = window(t, full).indirect(T.LI[:, h, c:c + 24 * n])
        rd = wkeys(t, full) + ["LI"] + ["EL%d%d" % (e - 2 + h, h) for e in range(e0, e0 + n) if e >= 2 - h]
        gk = ["G%d" % s for s in range(s0, s0 + n)]
        if eng == "v":
            tt(T.G[:, V * s0:V * s0 + V], src, T.YS[:, V * h:V * h + V], A.max, rd + ["YS%d" % h], gk, V * gat)
        else:
            act(T.G[:, V * s0:V * (s0 + n)], src, rd, gk, V * n * gat)
        for i in range(n):
            s, e = s0 + i, e0 + i
            if eng == "b" or (eng == "a" and i % 2 == 0):
                m = min(2, n - i) if eng == "a" else 1
                gs = T.G[:, V * s:V * (s + m)]
                tt(gs, gs, YY[h][:, 0:m, 0:V], A.max, gk[i:i + m] + ["Y%d" % h, "Z%d" % h, "YS%d" % h], gk[i:i + m], V * m)
            for b in range(3):
                o = b * E + e
                lhs = T.G[:, V * s + b:V * s + V:3] if (t, h) == (3, 1) else T.G[:, V * s + 128 * b:V * s + 128 * b + 128]
                mm(B[DB[h]][:, o:o + 21 * E + 1:3 * E], lhs, T.SS[:, 8 * t:8 * t + 8], True, True, [gk[i], "SS%d" % t], ["+X%d" % h], 256)

    def phase(t, h):
        E = nsrc(t, h)
        lo = 2 - h
        seq = list(range(E)) if t == 0 or h else list(range(lo, E - 1)) + list(range(lo)) + [E - 1]
        i = 0
        for tok in PLAN[2 * t + h].split():
            n = int(tok[1])
            assert seq[i + n - 1] == seq[i] + n - 1, (t, h, tok)
            call(t, h, tok[0], seq[i], n)
            i += n
        assert i == E, (t, h)

    def rows(p, a, b):
        return T.S[24 * a:24 * b, 128 * p:128 * p + 128]

    def put(p, w, kinds):
        t, h = p // 2, p % 2
        r = 7 + 2 * t
        if h == 0:
            pairs = [(W[w][16 * q + r:16 * q + r + kinds, OB:TM], rows(p, 0, kinds)) for q in range(8)]
            dma("s", pairs, ["S%d" % p] + ["W%dp%d" % (w, q) for q in range(8)], ["+W%do" % w], PAR["put"])
        else:
            pairs = [(W[w][r + k::16, TM:TM + V], rows(p, k, k + 1)) for k in range(kinds)]
            dma("s", pairs, ["S%d" % p, "W%dp8" % w], ["+W%dt" % w])

    def gains(t, h):
        p = 2 * t + h
        E = nsrc(t, h)
        n = 24 * E
        d, dk = B[DB[h]][:, 0:n], "X%d" % h
        if t == 3:
            mq, mc = T.MQ[:, 264 * h:264 * h + n], T.MC[:, 264 * h:264 * h + n]
            lin(PAR["mq"], mq, d, [dk], ["MQ%d" % h], n, 0.375)
            tt(mc, d, mq, A.subtract, [dk, "MQ%d" % h], ["MC%d" % h], n)
            d, dk = mc, "MC%d" % h
        sc = T.SC[:, 264 * h:264 * h + n]
        rk = ["RS%d" % p] + (["nm%d" % t] if h == 0 else [])
        op("v", lambda e: e.tensor_tensor_scan(sc, reset(t, h), d, 0.0, A.add, A.min), rk + [dk], ["SC%d" % h], n)
        x = T.SC[:, 264 * h + E - 1:264 * h + n:E]
        ps, pk = B[PS], "#%d" % PS
        if p == 7:
            ts(T.SG[:, :], x, K, 3456.0, A.mult, A.add, ["SC1"], ["SG"])
            return
        if p == 6:
            ts(tc(14), x, K, 1920.0, A.mult, A.add, ["SC0", "TCz"], ["TG6"])
            mm(ps[0:24, 0:128], tc(14), T.ID[:, :], True, True, ["TG6", "ID"], [pk], 128)
            act(T.S[0:24, 768:896], ps[0:24, 0:128], [pk], ["S6"], 128, bias=1536.0)
            dma("s", [(T.gst[:, 96:112, :], T.S[0:24, 768:896])], ["S6"], ["+gst"])
            return
        ts(tc(8 + p), x, -2048.0, K, A.is_lt, A.mult, ["SC%d" % h, "TCz"], ["TG%d" % p])
        tt(tc(p + 2), x, tc(8 + p), A.add, ["SC%d" % h, "TG%d" % p, "TCz"], ["TC%d" % (p + 2)])
        terms = [(p, 0, T.KID, "KID"), (p, 0, T.NID, "NID"), (8 + p, 3, T.NID, "NID"), (p + 2, 0, T.ID, "ID"), (p + 2, 1, T.KID, "KID"),
                 (p + 2, 2, T.KID, "KID"), (p + 2, 3, T.ID, "ID")]
        terms += [(p + 2, 2, T.NID, "NID")] if t == 2 else []
        for i, (sl, kind, m, mk) in enumerate(terms):
            o = 72 + 96 * sl - 24 * kind
            mm(ps[0:96, 0:128], T.TC[:, o:o + 96], m[:, :], i == 0, i == len(terms) - 1, ["TC%d" % sl if sl < 8 else "TG%d" % p, mk], [pk], 128)
        c = 32 + (t == 2)
        ts(rows(p, 0, 4), ps[0:96, 0:128], T.KC[0:96, c:c + 1], T.KC[0:96, 34:35], A.add, A.min, [pk, "c%d" % c, "c34"], ["S%d" % p], 128)
        put(p, (t + 1) % 2, 3)
        if h or not PAR["late"]:
            thresholds(p + 2)
        to = [32 * t + 16 * h] + ([112] if p == 0 else [])
        dma("s", [(T.gst[:, r:r + 16, :], rows(p, 3, 4)) for r in to], ["S%d" % p], ["+gst"])

    thresholds(0)
    edges(0)
    thresholds(1)
    tops()
    dma("g", [(T.own[:, :], T.pts[:, :])], ["TE0"], ["own"], 4.0)
    gcopy(T.ownf[:, :], T.own[:, :], ["own"], ["ownf"], 768)
    for t in range(RO):
        if t:
            gains(t - 1, 1)
            if t < 3:
                put(2 * t - 2, (t + 1) % 2, 2)
                put(2 * t - 1, (t + 1) % 2, 2)
            edges(t)
        if t == 1:
            dma("g", [(T.yp[:, :], T.ownf[:, :])], ["ownf", "EL60"], ["yp"], 4.0)
        stores(t)
        phase(t, 0)
        gains(t, 0)
        if t == 3:
            tr1 = alltoall(T.gst, T.hand2, T.sem.h1, T.land2, T.sem.arr2)
            raw("g", lambda e: e.remote_dma_fused(tr1, local_sem=T.sem.sent), ["gst"], ["away1"], 1.0)
            dma("s", [(T.land2[rank], T.gst[rank])], ["gst"], ["own2"])
        if t:
            edges(t, 1)
        phase(t, 1)
        if t < 3 and PAR["late"]:
            thresholds(2 * t + 2)
    gains(3, 1)

    tr2 = [RemoteDMATransfer(dst_ids=[dst(topo, hc, core)], dma_engine_mask=bits(every[4 * j:4 * j + 4]), remote_sem=T.sem.h2,
                             src=T.SG[:, 3 * q:3 * q + 3], dst=T.hand3[:, :]) for j, (hc, q) in enumerate(helpers)]
    tr3 = [RemoteDMATransfer(dst_ids=[dst(topo, cores[q], core)], dma_engine_mask=bits(dm[j]), remote_sem=T.sem.arr3,
                             src=T.SG[:, 3 * q:3 * q + 3], dst=T.land3[rank]) for j, q in enumerate(direct)]
    raw("g", lambda e: e.remote_dma_fused(tr2, local_sem=T.sem.sent), ["SG"], ["away2"], 1.0)
    raw("g", lambda e: e.remote_dma_fused(tr3, local_sem=T.sem.sent), ["SG"], ["away3"], 1.0)
    raw("s", lambda e: e.wait_ge(T.sem.arr2, near + far), ["away1"], [], 5.0)
    dma("s", [(T.yp[6 + t::16, :], T.land2[:, 32 * t:32 * t + 32, :]) for t in range(3)] + [(T.yp[9::16, 0:V], T.land2[:, 96:112, :])],
        ["own2"], ["+yp"])
    dma("a", [(T.yp[16 * rank + 9:16 * rank + 10, V:2 * V], T.SG[:, 3 * rank:3 * rank + 3])], ["SG"], ["+yp"])
    raw("s", lambda e: e.wait_ge(T.sem.arr3, near + far), ["away2", "away3"], [], 5.0)
    last = [(T.yp[9:16 * rank:16, V:2 * V], T.land3[0:rank])] if rank else []
    last += [(T.yp[16 * rank + 25::16, V:2 * V], T.land3[rank + 1:N])] if rank < N - 1 else []
    dma("s", last, [], ["+yp"])
    raw("g", lambda e: e.wait_ge(T.sem.sent, 4 * len(every) + sum(len(m) for m in dm)), [], [], 0.0)
    emit(g, T, ops)


def depends(ops):
    writers, readers, base, bank, tail = {}, {}, {}, {}, {}
    deps = []
    for i, o in enumerate(ops):
        d = set()
        if o["q"] in "gs" or (o["q"] == "a" and o["kind"] != "c"):
            d.update(tail.get(o["q"], []))
            tail[o["q"]] = [i]
        for k in o["rd"] + o["wr"]:
            if k[0] == "#":
                last = bank.setdefault(k, {})
                d.update(last.values())
                last[o["q"]] = i
        soft = set(j for j in d if ops[j]["q"] == o["q"])
        hard = d - soft
        for k in o["rd"]:
            if k[0] != "#":
                hard.update(writers.get(k, []))
        for k in o["wr"]:
            if k[0] == "#":
                continue
            if k[0] == "+":
                k = k[1:]
                if readers.get(k) or k not in base:
                    base[k] = list(writers.get(k, [])) + list(readers.get(k, []))
                    writers[k] = list(writers.get(k, []))
                    readers[k] = []
                hard.update(base[k])
                writers[k].append(i)
            else:
                hard.update(writers.get(k, []))
                hard.update(readers.get(k, []))
                writers[k] = [i]
                readers[k] = []
                base.pop(k, None)
        for k in o["rd"]:
            if k[0] != "#":
                readers.setdefault(k, []).append(i)
        hard.discard(i)
        soft.discard(i)
        deps.append((hard, soft - hard))
    return deps


def arrange(ops, deps):
    n = len(ops)
    wait = [o["cost"] if o["kind"] == "raw" and o["q"] == "s" else 0.0 for o in ops]
    hold = [(1.0 if o["q"] == "g" else 0.1) * len(o["fn"]) if o["kind"] == "dma" else o["cost"] - wait[i] for i, o in enumerate(ops)]
    before = [[(j, ops[j]["cost"] + PAR["sem"] + wait[i]) for j in hard] + [(j, hold[j]) for j in soft] for i, (hard, soft) in enumerate(deps)]
    after = [[] for i in range(n)]
    for i in range(n):
        for j, lag in before[i]:
            after[j].append((i, lag))

    def lay(order, back):
        start, taken = [0.0] * n, {q: [] for q in "gvaps"}
        for i in order:
            if back:
                t = max([ops[i]["cost"] - wait[i]] + [start[j] + lag for j, lag in after[i]]) - hold[i]
            else:
                t = max([0.0] + [start[j] + lag for j, lag in before[i]])
            row = taken[ops[i]["q"]]
            k = len(row)
            while k and row[k - 1][1] > t:
                k -= 1
            while k < len(row) and row[k][0] < t + hold[i] - 1e-9:
                t = max(t, row[k][1])
                k += 1
            row.insert(k, (t, t + hold[i]))
            start[i] = t + hold[i] if back else t
        return start

    left = [len(b) for b in before]
    ready = {q: [i for i in range(n) if ops[i]["q"] == q and not left[i]] for q in "gvaps"}
    can, start, free = [0.0] * n, [0.0] * n, {q: 0.0 for q in "gvaps"}
    for step in range(n):
        t0, q = min((max(free[q], min(can[i] for i in ready[q])), q) for q in ready if ready[q])
        i = min(i for i in ready[q] if can[i] <= t0 + PAR["slack"])
        ready[q].remove(i)
        start[i] = max(free[q], can[i])
        free[q] = start[i] + hold[i]
        for j, lag in after[i]:
            can[j] = max(can[j], start[i] + lag)
            left[j] -= 1
            if not left[j]:
                ready[ops[j]["q"]].append(j)
    for turn in range(PAR["turns"]):
        late = lay(sorted(range(n), key=lambda i: (-start[i], -i)), True)
        start = lay(sorted(range(n), key=lambda i: (-late[i], i)), False)
    return sorted(range(n), key=lambda i: (start[i], i))


def emit(g, T, ops):
    eng = {"g": g, "v": g.vector, "a": g.scalar, "p": g.tensor, "s": g.sync}
    deps = depends(ops)
    order = arrange(ops, deps)
    place = {i: n for n, i in enumerate(order)}
    seen = {q: {} for q in eng}
    need, waits = set(), {}
    for i in order:
        late = {}
        for j in deps[i][0]:
            if ops[j]["kind"] == "dma":
                late[("d", j)] = j
            elif ops[j]["kind"] == "c":
                k = ops[j]["q"]
                if k not in late or place[late[k]] < place[j]:
                    late[k] = j
        waits[i] = []
        for k, j in late.items():
            if seen[ops[i]["q"]].get(k, -1) < place[j]:
                seen[ops[i]["q"]][k] = place[j]
                waits[i].append(j)
                need.add(j)
    count = {q: 0 for q in eng}
    mark = {}
    nd = 0
    for i in order:
        o = ops[i]
        e = eng[o["q"]]
        for j in waits[i]:
            e.wait_ge(mark[j][0], mark[j][1])
        if o["kind"] == "dma":
            mark[i] = (T.sem["d%d" % nd], 16 * len(o["fn"]))
            nd += 1
            for out, in_ in o["fn"]:
                e.dma_start(out, in_).then_inc(mark[i][0], 16)
            continue
        ins = o["fn"](e)
        if i in need:
            count[o["q"]] += 1
            mark[i] = (T.sem["c" + o["q"]], count[o["q"]])
            ins.then_inc(mark[i][0], 1)
    for i in order:
        if ops[i]["kind"] == "dma" and i not in need:
            g.wait_ge(mark[i][0], mark[i][1])
